import numpy as np
import ml_dtypes


def mxq(x, axis, fmt="e4m3"):
    dtype, down = {"e4m3": (ml_dtypes.float8_e4m3fn, 7), "e5m2": (ml_dtypes.float8_e5m2, 14)}[fmt]
    v = np.moveaxis(np.asarray(x, np.float32).astype(ml_dtypes.bfloat16).astype(np.float64), axis, -1)
    blocks = v.reshape(v.shape[:-1] + (-1, 32))
    amax = np.abs(blocks).max(-1, keepdims=True)
    byte = np.maximum(np.where(amax > 0, np.frexp(amax)[1] - 1 + 127, 0) - down, 1)
    scale = np.exp2(byte - 127.0)
    codes = (blocks / scale).astype(np.float32).astype(dtype).astype(np.float64)
    return np.moveaxis((codes * scale).reshape(v.shape), -1, axis)


WIDE = False


def mx_kscale(k):
    if not WIDE:
        return np.ones(k)
    levels = np.array([10, -10, 5, -5, 0])
    if k % 512:
        return np.exp2(np.random.permutation(np.resize(levels, k // 32))).repeat(32)
    a = np.empty((k // 512, 16))
    for p in range(k // 512):
        a[p, :8] = np.random.permutation(np.resize(levels, 8))
        for g in range(8):
            far = levels[np.abs(levels - a[p, g]) >= 10]
            a[p, g + 8] = far[np.random.randint(len(far))]
    return np.exp2(a.ravel()).repeat(32)


def f64(x):
    return np.asarray(x).astype(np.float64)


def striped(idx):
    return np.tile(idx.reshape(-1, 16).T, (8, 1)).astype(np.uint16)


def unstriped(offs):
    return offs[:16].T.reshape(-1).astype(np.int64)


E2M1 = np.array([0.0, 0.5, 1.0, 1.5, 2.0, 3.0, 4.0, 6.0, -0.0, -0.5, -1.0, -1.5, -2.0, -3.0, -4.0, -6.0])


def pack_weight(w, fmt):
    k, n = w.shape
    w = f64(np.asarray(w, np.float32).astype(ml_dtypes.bfloat16)).reshape(k // 32, 32, n)
    amax = np.abs(w).max(1)
    if fmt == "e4m3":
        byte = np.frexp(amax)[1] - 1 + 127 - 7
    else:
        mant, ex = np.frexp(amax / 6.0)
        byte = np.where(mant > 0.5, ex, ex - 1) + 127
    byte = np.clip(np.where(amax > 0, byte, 1), 1, 254)
    scaled = (w * np.exp2(127.0 - byte)[:, None, :]).reshape(k, n).astype(np.float32)
    by_word = np.ascontiguousarray(scaled.reshape(k // 512, 128, 4, n).transpose(0, 1, 3, 2))
    if fmt == "e4m3":
        words = by_word.astype(ml_dtypes.float8_e4m3fn).view(np.uint8)
    else:
        c = by_word.astype(ml_dtypes.float4_e2m1fn).view(np.uint8) & 0xF
        words = (c[..., 0::2] | (c[..., 1::2] << 4)).reshape(k // 512, 128, 2 * n)
    return np.ascontiguousarray(words), np.ascontiguousarray(byte.astype(np.uint8).reshape(k // 512, 16, n))


def unpack_weight(words, scales, fmt):
    g, _, n = scales.shape
    words = np.ascontiguousarray(words).reshape(g, 128, n, -1)
    if fmt == "e4m3":
        vals = words.view(ml_dtypes.float8_e4m3fn).astype(np.float64)
    else:
        nib = np.empty((g, 128, n, 4), np.uint8)
        nib[..., 0::2] = words & 0xF
        nib[..., 1::2] = words >> 4
        vals = E2M1[nib]
    vals = vals * np.repeat(np.exp2(scales.astype(np.float64) - 127.0), 8, axis=1)[..., None]
    return vals.transpose(0, 1, 3, 2).reshape(g * 512, n)


def sigmoid(v):
    return 1.0 / (1.0 + np.exp(-np.maximum(v, -700.0)))


def d_sigmoid(v):
    s = 1.0 / (1.0 + np.exp(-np.maximum(v, -700.0)))
    return s * (1.0 - s)


K, T, E, C, H, N = 256, 768, 4, 128, 1024, 512


def by_expert(wq, xq):
    return np.concatenate([wq[e].T @ xq[:, e * C:(e + 1) * C] for e in range(E)], axis=1)


def setup_inputs():
    n = np.random.standard_normal
    s = mx_kscale(N)[:, None]
    u = mx_kscale(H)
    w2 = [pack_weight(m, "e2m1") for m in n((E, N, H)) / np.sqrt(N) / s[None] * u[None, None, :]]
    w1 = [pack_weight(m, "e2m1") for m in n((E, H, K)) / np.sqrt(H) / u[None, :, None]]
    w3 = [pack_weight(m, "e2m1") for m in n((E, H, K)) / np.sqrt(H) / u[None, :, None]]
    return {
        "dyT": (n((N, T)) * s).astype(np.float32),
        "a1": n((H, E * C)).astype(np.float32),
        "a3": n((H, E * C)).astype(np.float32),
        "w2_words": np.stack([m[0] for m in w2]),
        "w2_scales": np.stack([m[1] for m in w2]),
        "w1_words": np.stack([m[0] for m in w1]),
        "w1_scales": np.stack([m[1] for m in w1]),
        "w3_words": np.stack([m[0] for m in w3]),
        "w3_scales": np.stack([m[1] for m in w3]),
        "gate": np.tile(np.random.uniform(0.2, 1.0, E * C), (N, 1)).astype(np.float32),
        "offs": striped(np.random.permutation(T)[:E * C]),
    }


def reference(dyT, a1, a3, w2_words, w2_scales, w1_words, w1_scales, w3_words, w3_scales, gate, offs):
    idx = unstriped(offs)
    w2 = np.stack([unpack_weight(w2_words[e], w2_scales[e], "e2m1") for e in range(E)])
    w1 = np.stack([unpack_weight(w1_words[e], w1_scales[e], "e2m1") for e in range(E)])
    w3 = np.stack([unpack_weight(w3_words[e], w3_scales[e], "e2m1") for e in range(E)])
    gq = mxq(f64(gate) * f64(dyT)[:, idx], 0, "e4m3")
    dh = by_expert(w2, gq)
    da1 = dh * f64(a3) * d_sigmoid(f64(a1))
    da3 = dh * sigmoid(f64(a1))
    dx = by_expert(w1, mxq(da1, 0, "e4m3")) + by_expert(w3, mxq(da3, 0, "e4m3"))
    out = np.zeros((K, T))
    out[:, idx] = dx
    return out

@@ -1,0 +1,267 @@
+from contextlib import ExitStack
+
+import concourse.mybir as mybir
+from concourse.masks import make_identity
+
+N, T, E, C, H, K = 512, 768, 4, 128, 1024, 256
+SLOTS = E * C
+P = 128
+
+FLOPS = 2 * SLOTS * H * (N + 2 * K)
+BYTES = 4 * (N * T + 2 * H * SLOTS + P * SLOTS + K * T) + 2 * P * SLOTS // 16 + E * (N * H + 2 * H * K) * 17 // 32
+
+F32 = mybir.dt.float32
+BF16 = mybir.dt.bfloat16
+I32 = mybir.dt.int32
+U32 = mybir.dt.uint32
+U16 = mybir.dt.uint16
+U8 = mybir.dt.uint8
+FP8X4 = mybir.dt.float8_e4m3fn_x4
+FP4X4 = mybir.dt.float4_e2m1fn_x4
+MULT = mybir.AluOpType.mult
+SUBTRACT = mybir.AluOpType.subtract
+SIGMOID = mybir.ActivationFunctionType.Sigmoid
+SQUARE = mybir.ActivationFunctionType.Square
+
+
+def tile_moe_bdx_glu_sigmoid_kernel(
+    tc, dyT, a1, a3, w2_words, w2_scales, w1_words, w1_scales, w3_words, w3_scales, gate, offs, out
+):
+    nc = tc.nc
+    with ExitStack() as ctx:
+        keep = ctx.enter_context(tc.tile_pool(name="keep", bufs=1))
+        ring = ctx.enter_context(tc.tile_pool(name="ring", bufs=3))
+        psum = ctx.enter_context(tc.psum_pool(name="psum", bufs=2))
+
+        offsets = keep.tile([P, SLOTS // 16], U16, name="offsets")
+        dy = [keep.tile([P, T], F32, name="dy%d" % t) for t in range(4)]
+        gates = keep.tile([P, SLOTS], F32, name="gates")
+        g4 = keep.tile([P, 4, SLOTS], F32, name="g4")
+        g_bf = keep.tile([P, SLOTS, 4], BF16, name="g_bf", align_bytes=64)
+        g_codes = keep.tile([P, SLOTS], U32, name="g_codes", align_bytes=64)
+        g_scales = keep.tile([P, SLOTS], U8, name="g_scales", align_bytes=64)
+        w2 = keep.tile([P, E, 2 * H], U8, name="w2", align_bytes=64)
+        w2_plane = keep.tile([P, E, H], U8, name="w2_plane", align_bytes=64)
+        w13 = keep.tile([P, 2, 2 * E, 2 * K], U8, name="w13", align_bytes=64)
+        w13_plane = keep.tile([P, 2, 2 * E, K], U8, name="w13_plane", align_bytes=64)
+        ident = keep.tile([P, P], F32, name="ident")
+        windows = [keep.tile([P, T], F32, name="window%d" % kt) for kt in range(2)]
+        warm = keep.tile([P, 1], F32, name="warm")
+        minus_half = keep.tile([P, 1], F32, name="minus_half")
+        saved = {}
+        for name in ("a1", "a3"):
+            for half in range(2):
+                saved[name, 0, half] = keep.tile([P, 4, 2 * C], F32, name="%s_0%d" % (name, half))
+            saved[name, 1] = keep.tile([P, 4, SLOTS], F32, name="%s_1" % name)
+        for name in ("sig", "sq", "nq"):
+            for e in range(E):
+                for s in range(2):
+                    saved[name, e, s] = keep.tile([P, C, 4], F32, name="%s_%d%d" % (name, e, s))
+
+        sources = {"a1": a1, "a3": a3}
+
+        def load_first_half(name, half):
+            nc.sync.dma_start(
+                out=saved[name, 0, half][:],
+                in_=sources[name][0:512, 2 * C * half : 2 * C * (half + 1)].rearrange("(p t) j -> p t j", t=4),
+            )
+
+        def load_second_half(name):
+            nc.sync.dma_start(
+                out=saved[name, 1][:], in_=sources[name][512:1024, :].rearrange("(p t) j -> p t j", t=4)
+            )
+
+        w2_src = w2_words.bitcast(I32)
+        w2_scale_src = w2_scales.bitcast(I32).rearrange("e s f i -> f (e s) i")
+        w2_dst = w2[:].rearrange("p e i -> p (e i)").bitcast(I32).rearrange("p (e i) -> p e i", e=E)
+        w2_plane_dst = w2_plane[:].rearrange("p e i -> p (e i)").bitcast(I32).rearrange("p (e i) -> p e i", e=E)
+        w13_dst = w13[:].rearrange("p a g k -> p (a g k)").bitcast(I32).rearrange("p (a g k) -> p a g k", a=2, g=2 * E)
+        w13_plane_dst = (
+            w13_plane[:].rearrange("p a g k -> p (a g k)").bitcast(I32).rearrange("p (a g k) -> p a g k", a=2, g=2 * E)
+        )
+
+        def load_w2(e):
+            nc.sync.dma_start(out=w2_dst[:, e, :], in_=w2_src[e, 0, :, :])
+
+        dy_rows = dyT.rearrange("(p t) j -> p t j", t=4)
+
+        def load_dy(t):
+            nc.sync.dma_start(out=dy[t][:], in_=dy_rows[:, t, :])
+
+        nc.sync.dma_start(offsets[:], offs)
+        nc.scalar.dma_start(out=gates[:], in_=gate[0:P, :])
+        nc.vector.memset(w2_plane[:].rearrange("p e i -> p (e i)").bitcast(I32), 0)
+        nc.vector.memset(minus_half[:], -0.5)
+        nc.vector.memset(warm[:], 0.0)
+        nc.scalar.activation(warm[:], warm[:], SIGMOID)
+        make_identity(nc, ident[:])
+        for kt in range(2):
+            nc.gpsimd.memset(windows[kt][:], 0.0)
+        nc.gpsimd.memset(w13_plane[:].rearrange("p a g k -> p (a g k)").bitcast(I32), 0)
+        for quad in range(4):
+            nc.scalar.dma_start(
+                out=w2_plane_dst[32 * quad : 32 * quad + 4, :, :],
+                in_=w2_scale_src[4 * quad : 4 * quad + 4, :, :],
+            )
+        for a, scales in ((0, w3_scales), (1, w1_scales)):
+            scale_src = scales.bitcast(I32).rearrange("e s f k -> f (e s) k")
+            for quad in range(4):
+                nc.gpsimd.dma_start(
+                    out=w13_plane_dst[32 * quad : 32 * quad + 4, a, :, :],
+                    in_=scale_src[4 * quad : 4 * quad + 4, :, :],
+                )
+        load_dy(0)
+        load_dy(1)
+        load_dy(2)
+        load_dy(3)
+        load_first_half("a1", 0)
+        load_w2(0)
+        load_first_half("a3", 0)
+        load_w2(1)
+        load_first_half("a1", 1)
+        load_first_half("a3", 1)
+        load_w2(2)
+        load_w2(3)
+        load_second_half("a1")
+        load_second_half("a3")
+        for a, words in ((0, w3_words), (1, w1_words)):
+            nc.sync.dma_start(out=w13_dst[:, a, :, :], in_=words.bitcast(I32).rearrange("e s p k -> p (e s) k"))
+
+        def gather(t, j0, j1):
+            nc.vector.tensor_tensor(
+                g4[:, t, j0:j1], dy[t][:].indirect(offsets[:, j0 // 16 : j1 // 16]), gates[:, j0:j1], MULT
+            )
+
+        def interleave(e, copy):
+            copy(
+                out=g_bf[:, C * e : C * (e + 1), :], in_=g4[:, :, C * e : C * (e + 1)].rearrange("p t j -> p j t")
+            )
+
+        def quantize_g(e):
+            cols = slice(C * e, C * (e + 1))
+            nc.vector.quantize_mx(
+                out=g_codes[:, cols].bitcast(FP8X4),
+                scales=g_scales[:, cols],
+                in_=g_bf[:, cols, :].rearrange("p j t -> p (j t)"),
+            )
+
+        turned = {}
+        codes = {}
+
+        def first_product(e, s):
+            dhT = psum.tile([P, 512], F32, name="dhT")
+            nc.tensor.matmul_mx(
+                out=dhT[:],
+                lhsT=g_codes[:, C * e : C * (e + 1)].bitcast(FP8X4),
+                lhsT_scale=g_scales[:, C * e : C * (e + 1)],
+                rhs=w2[:, e, 1024 * s : 1024 * (s + 1)].bitcast(FP4X4),
+                rhs_scale=w2_plane[:, e, 512 * s : 512 * (s + 1)],
+                start=True,
+                stop=True,
+            )
+            dhT_sb = ring.tile([P, 4, P], F32, name="dhT_sb")
+            nc.scalar.copy(out=dhT_sb[:], in_=dhT[:].rearrange("j (m t) -> j t m", t=4))
+            dh = psum.tile([P, 4, P], F32, name="dh", bufs=4)
+            for t in range(4):
+                nc.tensor.transpose(dh[:, t, :], dhT_sb[:, t, :], ident[:])
+            turned[e, s] = dh
+
+        def saved_slice(name, e, s):
+            if s == 0:
+                half, h = divmod(e, 2)
+                tile = saved[name, 0, half]
+            else:
+                h, tile = e, saved[name, 1]
+            return tile[:, :, C * h : C * (h + 1)].rearrange("p t j -> p j t")
+
+        def factors(e, s):
+            nc.scalar.activation(saved["sig", e, s][:], saved_slice("a1", e, s), SIGMOID)
+            nc.scalar.activation(saved["sq", e, s][:], saved["sig", e, s][:], SQUARE, bias=minus_half[:])
+
+        def factor_products(e, s):
+            nc.vector.scalar_tensor_tensor(
+                saved["nq", e, s][:], saved["sq", e, s][:], 0.25, saved_slice("a3", e, s), SUBTRACT, MULT
+            )
+
+        das = {}
+
+        def product_da(e, s):
+            da = ring.tile([P, 2, C, 4], BF16, name="da", align_bytes=64)
+            dh = turned[e, s][:].rearrange("p t j -> p j t")
+            nc.vector.tensor_tensor(da[:, 0, :, :], dh, saved["sig", e, s][:], MULT)
+            nc.vector.scalar_tensor_tensor(da[:, 1, :, :], dh, -1.0, saved["nq", e, s][:], MULT, MULT)
+            das[e, s] = da
+
+        def quantize_da(e, s):
+            da = das[e, s]
+            words = keep.tile([P, 2 * C], U32, name="da_codes_%d%d" % (e, s), align_bytes=64)
+            scales = keep.tile([P, 2 * C], U8, name="da_scales_%d%d" % (e, s), align_bytes=64)
+            nc.vector.quantize_mx(
+                out=words[:].bitcast(FP8X4), scales=scales[:], in_=da[:].rearrange("p a j t -> p (a j t)")
+            )
+            codes[e, s] = (words, scales)
+
+        def second_product(e):
+            dx_sb = ring.tile([P, 2, C], F32, name="dx_sb", bufs=4)
+            banks = []
+            for kt in range(2):
+                bank = psum.tile([P, C], F32, name="dx%d" % kt, bufs=1)
+                banks.append(bank)
+            for s in range(2):
+                words, scales = codes[e, s]
+                for kt in range(2):
+                    for a in range(2):
+                        nc.tensor.matmul_mx(
+                            out=banks[kt][:],
+                            lhsT=w13[:, a, 2 * e + s, 256 * kt : 256 * (kt + 1)].bitcast(FP4X4),
+                            lhsT_scale=w13_plane[:, a, 2 * e + s, P * kt : P * (kt + 1)],
+                            rhs=words[:, C * a : C * (a + 1)].bitcast(FP8X4),
+                            rhs_scale=scales[:, C * a : C * (a + 1)],
+                            start=(s == 0 and a == 0),
+                            stop=(s == 1 and a == 1),
+                        )
+            for kt in range(2):
+                nc.scalar.copy(out=dx_sb[:, kt, :], in_=banks[kt][:])
+            return dx_sb
+
+        def scatter(e, kt, dx_sb):
+            nc.vector.tensor_copy(windows[kt][:].indirect(offsets[:, 8 * e : 8 * (e + 1)]), dx_sb[:, kt, :])
+
+        steps = [(e, s) for s in range(2) for e in range(E)]
+        for t in range(3):
+            gather(t, 0, SLOTS)
+        factors(0, 0)
+        gather(3, 0, C)
+        gather(3, C, 2 * C)
+        interleave(0, nc.vector.tensor_copy)
+        gather(3, 2 * C, SLOTS)
+        quantize_g(0)
+        interleave(1, nc.vector.tensor_copy)
+        first_product(0, 0)
+        quantize_g(1)
+        first_product(1, 0)
+        factors(1, 0)
+        interleave(2, nc.vector.tensor_copy)
+        interleave(3, nc.vector.tensor_copy)
+        factor_products(0, 0)
+        quantize_g(2)
+        quantize_g(3)
+        factor_products(1, 0)
+        factors(2, 0)
+        dxs = {}
+        for i in range(len(steps)):
+            e, s = steps[i]
+            if i + 2 < len(steps):
+                first_product(*steps[i + 2])
+            if i + 3 < len(steps):
+                factors(*steps[i + 3])
+            product_da(e, s)
+            if i + 2 < len(steps):
+                factor_products(*steps[i + 2])
+            quantize_da(e, s)
+            if s == 1:
+                dxs[e] = second_product(e)
+        for kt in range(2):
+            for e in range(E):
+                scatter(e, kt, dxs[e])
+            nc.sync.dma_start(out=out[P * kt : P * (kt + 1), :], in_=windows[kt][:])

@@ -22,6 +22,15 @@ MULT = mybir.AluOpType.mult
 SUBTRACT = mybir.AluOpType.subtract
 SIGMOID = mybir.ActivationFunctionType.Sigmoid
 SQUARE = mybir.ActivationFunctionType.Square
+COPY = mybir.ActivationFunctionType.Copy
+
+
+def planes_by_pairs(ap):
+    return ap.rearrange("p t (c i) -> p c t i", i=2)
+
+
+def woven_by_pairs(ap):
+    return ap.rearrange("p (c i) t -> p c t i", i=2)
 
 
 def tile_moe_bdx_glu_sigmoid_kernel(
@@ -53,10 +62,12 @@ def tile_moe_bdx_glu_sigmoid_kernel(
             for half in range(2):
                 saved[name, 0, half] = keep.tile([P, 4, 2 * C], F32, name="%s_0%d" % (name, half))
             saved[name, 1] = keep.tile([P, 4, SLOTS], F32, name="%s_1" % name)
-        for name in ("sig", "sq", "nq"):
-            for e in range(E):
-                for s in range(2):
-                    saved[name, e, s] = keep.tile([P, C, 4], F32, name="%s_%d%d" % (name, e, s))
+        for e in range(E):
+            for s in range(2):
+                saved["sig", e, s] = keep.tile([P, C, 4], F32, name="sig_%d%d" % (e, s))
+                for name in ("sq", "nq"):
+                    saved[name, e, s] = keep.tile([P, 4, C], F32, name="%s_%d%d" % (name, e, s))
+        dx_sb = keep.tile([P, 2, SLOTS], F32, name="dx_sb")
 
         sources = {"a1": a1, "a3": a3}
 
@@ -134,7 +145,7 @@ def tile_moe_bdx_glu_sigmoid_kernel(
 
         def interleave(e, copy):
             copy(
-                out=g_bf[:, C * e : C * (e + 1), :], in_=g4[:, :, C * e : C * (e + 1)].rearrange("p t j -> p j t")
+                out=woven_by_pairs(g_bf[:, C * e : C * (e + 1), :]), in_=planes_by_pairs(g4[:, :, C * e : C * (e + 1)])
             )
 
         def quantize_g(e):
@@ -160,7 +171,7 @@ def tile_moe_bdx_glu_sigmoid_kernel(
                 stop=True,
             )
             dhT_sb = ring.tile([P, 4, P], F32, name="dhT_sb")
-            nc.scalar.copy(out=dhT_sb[:], in_=dhT[:].rearrange("j (m t) -> j t m", t=4))
+            nc.scalar.activation(dhT_sb[:], dhT[:].rearrange("j (m t) -> j t m", t=4), COPY, scale=-1.0)
             dh = psum.tile([P, 4, P], F32, name="dh", bufs=4)
             for t in range(4):
                 nc.tensor.transpose(dh[:, t, :], dhT_sb[:, t, :], ident[:])
@@ -172,11 +183,21 @@ def tile_moe_bdx_glu_sigmoid_kernel(
                 tile = saved[name, 0, half]
             else:
                 h, tile = e, saved[name, 1]
-            return tile[:, :, C * h : C * (h + 1)].rearrange("p t j -> p j t")
+            return tile[:, :, C * h : C * (h + 1)]
+
+        def sigmoid(e, s):
+            nc.scalar.activation(
+                woven_by_pairs(saved["sig", e, s][:]), planes_by_pairs(saved_slice("a1", e, s)), SIGMOID
+            )
+
+        def square(e, s):
+            nc.scalar.activation(
+                planes_by_pairs(saved["sq", e, s][:]), woven_by_pairs(saved["sig", e, s][:]), SQUARE, bias=minus_half[:]
+            )
 
         def factors(e, s):
-            nc.scalar.activation(saved["sig", e, s][:], saved_slice("a1", e, s), SIGMOID)
-            nc.scalar.activation(saved["sq", e, s][:], saved["sig", e, s][:], SQUARE, bias=minus_half[:])
+            sigmoid(e, s)
+            square(e, s)
 
         def factor_products(e, s):
             nc.vector.scalar_tensor_tensor(
@@ -187,9 +208,13 @@ def tile_moe_bdx_glu_sigmoid_kernel(
 
         def product_da(e, s):
             da = ring.tile([P, 2, C, 4], BF16, name="da", align_bytes=64)
-            dh = turned[e, s][:].rearrange("p t j -> p j t")
-            nc.vector.tensor_tensor(da[:, 0, :, :], dh, saved["sig", e, s][:], MULT)
-            nc.vector.scalar_tensor_tensor(da[:, 1, :, :], dh, -1.0, saved["nq", e, s][:], MULT, MULT)
+            minus_dh = turned[e, s][:]
+            nc.vector.scalar_tensor_tensor(
+                da[:, 0, :, :], minus_dh.rearrange("p t j -> p j t"), -1.0, saved["sig", e, s][:], MULT, MULT
+            )
+            nc.vector.tensor_tensor(
+                woven_by_pairs(da[:, 1, :, :]), planes_by_pairs(minus_dh), planes_by_pairs(saved["nq", e, s][:]), MULT
+            )
             das[e, s] = da
 
         def quantize_da(e, s):
@@ -202,7 +227,6 @@ def tile_moe_bdx_glu_sigmoid_kernel(
             codes[e, s] = (words, scales)
 
         def second_product(e):
-            dx_sb = ring.tile([P, 2, C], F32, name="dx_sb", bufs=4)
             banks = []
             for kt in range(2):
                 bank = psum.tile([P, C], F32, name="dx%d" % kt, bufs=1)
@@ -221,11 +245,10 @@ def tile_moe_bdx_glu_sigmoid_kernel(
                             stop=(s == 1 and a == 1),
                         )
             for kt in range(2):
-                nc.scalar.copy(out=dx_sb[:, kt, :], in_=banks[kt][:])
-            return dx_sb
+                nc.scalar.copy(out=dx_sb[:, kt, C * e : C * (e + 1)], in_=banks[kt][:])
 
-        def scatter(e, kt, dx_sb):
-            nc.vector.tensor_copy(windows[kt][:].indirect(offsets[:, 8 * e : 8 * (e + 1)]), dx_sb[:, kt, :])
+        def scatter(e0, e1, kt):
+            nc.vector.tensor_copy(windows[kt][:].indirect(offsets[:, 8 * e0 : 8 * e1]), dx_sb[:, kt, C * e0 : C * e1])
 
         steps = [(e, s) for s in range(2) for e in range(E)]
         for t in range(3):
@@ -248,20 +271,24 @@ def tile_moe_bdx_glu_sigmoid_kernel(
         quantize_g(3)
         factor_products(1, 0)
         factors(2, 0)
-        dxs = {}
         for i in range(len(steps)):
             e, s = steps[i]
+            if i + 3 < len(steps):
+                sigmoid(*steps[i + 3])
             if i + 2 < len(steps):
                 first_product(*steps[i + 2])
             if i + 3 < len(steps):
-                factors(*steps[i + 3])
+                square(*steps[i + 3])
             product_da(e, s)
             if i + 2 < len(steps):
                 factor_products(*steps[i + 2])
+            else:
+                scatter(0, 1, i + 2 - len(steps))
             quantize_da(e, s)
             if s == 1:
-                dxs[e] = second_product(e)
+                second_product(e)
         for kt in range(2):
-            for e in range(E):
-                scatter(e, kt, dxs[e])
+            scatter(1, 3, kt)
+        for kt in range(2):
+            scatter(3, 4, kt)
             nc.sync.dma_start(out=out[P * kt : P * (kt + 1), :], in_=windows[kt][:])

@@ -49,9 +49,17 @@ def tile_moe_bdx_glu_sigmoid_kernel(
         g_bf = keep.tile([P, SLOTS, 4], BF16, name="g_bf", align_bytes=64)
         g_codes = keep.tile([P, SLOTS], U32, name="g_codes", align_bytes=64)
         g_scales = keep.tile([P, SLOTS], U8, name="g_scales", align_bytes=64)
-        w2 = keep.tile([P, E, 2 * H], U8, name="w2", align_bytes=64)
-        w2_plane = keep.tile([P, E, H], U8, name="w2_plane", align_bytes=64)
-        w13 = keep.tile([P, 2, 2 * E, 2 * K], U8, name="w13", align_bytes=64)
+        w2 = {
+            (s, half): keep.tile([P, 2, H], U8, name="w2_%d%d" % (s, half), align_bytes=64)
+            for s in range(2)
+            for half in range(2)
+        }
+        w2_plane = [keep.tile([P, E, 512], U8, name="w2_plane%d" % s, align_bytes=64) for s in range(2)]
+        w13 = {
+            (a, half): keep.tile([P, 4, 2 * K], U8, name="w13_%d%d" % (a, half), align_bytes=64)
+            for a in range(2)
+            for half in range(2)
+        }
         w13_plane = keep.tile([P, 2, 2 * E, K], U8, name="w13_plane", align_bytes=64)
         ident = keep.tile([P, P], F32, name="ident")
         windows = [keep.tile([P, T], F32, name="window%d" % kt) for kt in range(2)]
@@ -59,40 +67,49 @@ def tile_moe_bdx_glu_sigmoid_kernel(
         minus_half = keep.tile([P, 1], F32, name="minus_half")
         saved = {}
         for name in ("a1", "a3"):
-            for half in range(2):
-                saved[name, 0, half] = keep.tile([P, 4, 2 * C], F32, name="%s_0%d" % (name, half))
-            saved[name, 1] = keep.tile([P, 4, SLOTS], F32, name="%s_1" % name)
-        for e in range(E):
             for s in range(2):
-                saved["sig", e, s] = keep.tile([P, C, 4], F32, name="sig_%d%d" % (e, s))
-                for name in ("sq", "nq"):
-                    saved[name, e, s] = keep.tile([P, 4, C], F32, name="%s_%d%d" % (name, e, s))
+                for half in range(2):
+                    saved[name, s, half] = keep.tile([P, 4, 2 * C], F32, name="%s_%d%d" % (name, s, half))
         dx_sb = keep.tile([P, 2, SLOTS], F32, name="dx_sb")
 
         sources = {"a1": a1, "a3": a3}
 
-        def load_first_half(name, half):
+        def load_saved(name, s, half):
             nc.sync.dma_start(
-                out=saved[name, 0, half][:],
-                in_=sources[name][0:512, 2 * C * half : 2 * C * (half + 1)].rearrange("(p t) j -> p t j", t=4),
+                out=saved[name, s, half][:],
+                in_=sources[name][512 * s : 512 * (s + 1), 2 * C * half : 2 * C * (half + 1)].rearrange(
+                    "(p t) j -> p t j", t=4
+                ),
             )
 
-        def load_second_half(name):
-            nc.sync.dma_start(
-                out=saved[name, 1][:], in_=sources[name][512:1024, :].rearrange("(p t) j -> p t j", t=4)
-            )
-
-        w2_src = w2_words.bitcast(I32)
+        w2_src = w2_words.bitcast(I32).rearrange("e s p i -> p (e s) i")
         w2_scale_src = w2_scales.bitcast(I32).rearrange("e s f i -> f (e s) i")
-        w2_dst = w2[:].rearrange("p e i -> p (e i)").bitcast(I32).rearrange("p (e i) -> p e i", e=E)
-        w2_plane_dst = w2_plane[:].rearrange("p e i -> p (e i)").bitcast(I32).rearrange("p (e i) -> p e i", e=E)
-        w13_dst = w13[:].rearrange("p a g k -> p (a g k)").bitcast(I32).rearrange("p (a g k) -> p a g k", a=2, g=2 * E)
         w13_plane_dst = (
             w13_plane[:].rearrange("p a g k -> p (a g k)").bitcast(I32).rearrange("p (a g k) -> p a g k", a=2, g=2 * E)
         )
 
-        def load_w2(e):
-            nc.sync.dma_start(out=w2_dst[:, e, :], in_=w2_src[e, 0, :, :])
+        def as_words(tile):
+            return tile[:].rearrange("p e i -> p (e i)").bitcast(I32).rearrange("p (e i) -> p e i", e=tile.shape[1])
+
+        def load_w2(s, half):
+            nc.sync.dma_start(
+                out=as_words(w2[s, half]), in_=w2_src[:, 2 * half : 2 * half + 2, 256 * s : 256 * (s + 1)]
+            )
+
+        def load_w2_scales(s):
+            for quad in range(4):
+                nc.sync.dma_start(
+                    out=as_words(w2_plane[s])[32 * quad : 32 * quad + 4, :, :],
+                    in_=w2_scale_src[4 * quad : 4 * quad + 4, :, 128 * s : 128 * (s + 1)],
+                )
+
+        def load_w13_scales(a, scales):
+            scale_src = scales.bitcast(I32).rearrange("e s f k -> f (e s) k")
+            for quad in range(4):
+                nc.sync.dma_start(
+                    out=w13_plane_dst[32 * quad : 32 * quad + 4, a, :, :],
+                    in_=scale_src[4 * quad : 4 * quad + 4, :, :],
+                )
 
         dy_rows = dyT.rearrange("(p t) j -> p t j", t=4)
 
@@ -101,7 +118,8 @@ def tile_moe_bdx_glu_sigmoid_kernel(
 
         nc.sync.dma_start(offsets[:], offs)
         nc.scalar.dma_start(out=gates[:], in_=gate[0:P, :])
-        nc.vector.memset(w2_plane[:].rearrange("p e i -> p (e i)").bitcast(I32), 0)
+        for s in range(2):
+            nc.vector.memset(as_words(w2_plane[s]), 0)
         nc.vector.memset(minus_half[:], -0.5)
         nc.vector.memset(warm[:], 0.0)
         nc.scalar.activation(warm[:], warm[:], SIGMOID)
@@ -109,34 +127,23 @@ def tile_moe_bdx_glu_sigmoid_kernel(
         for kt in range(2):
             nc.gpsimd.memset(windows[kt][:], 0.0)
         nc.gpsimd.memset(w13_plane[:].rearrange("p a g k -> p (a g k)").bitcast(I32), 0)
-        for quad in range(4):
-            nc.scalar.dma_start(
-                out=w2_plane_dst[32 * quad : 32 * quad + 4, :, :],
-                in_=w2_scale_src[4 * quad : 4 * quad + 4, :, :],
-            )
-        for a, scales in ((0, w3_scales), (1, w1_scales)):
-            scale_src = scales.bitcast(I32).rearrange("e s f k -> f (e s) k")
-            for quad in range(4):
-                nc.gpsimd.dma_start(
-                    out=w13_plane_dst[32 * quad : 32 * quad + 4, a, :, :],
-                    in_=scale_src[4 * quad : 4 * quad + 4, :, :],
-                )
-        load_dy(0)
-        load_dy(1)
-        load_dy(2)
-        load_dy(3)
-        load_first_half("a1", 0)
-        load_w2(0)
-        load_first_half("a3", 0)
-        load_w2(1)
-        load_first_half("a1", 1)
-        load_first_half("a3", 1)
-        load_w2(2)
-        load_w2(3)
-        load_second_half("a1")
-        load_second_half("a3")
-        for a, words in ((0, w3_words), (1, w1_words)):
-            nc.sync.dma_start(out=w13_dst[:, a, :, :], in_=words.bitcast(I32).rearrange("e s p k -> p (e s) k"))
+        for t in range(4):
+            load_dy(t)
+        for s in range(2):
+            load_saved("a1", s, 0)
+            load_w2(s, 0)
+            load_w2_scales(s)
+            load_saved("a3", s, 0)
+            load_saved("a1", s, 1)
+            load_w2(s, 1)
+            if s == 1:
+                load_w13_scales(0, w3_scales)
+            load_saved("a3", s, 1)
+        load_w13_scales(1, w1_scales)
+        for half in range(2):
+            for a, words in ((0, w3_words), (1, w1_words)):
+                src = words.bitcast(I32).rearrange("e s p k -> p (e s) k")
+                nc.sync.dma_start(out=as_words(w13[a, half]), in_=src[:, 4 * half : 4 * half + 4, :])
 
         def gather(t, j0, j1):
             nc.vector.tensor_tensor(
@@ -165,8 +172,8 @@ def tile_moe_bdx_glu_sigmoid_kernel(
                 out=dhT[:],
                 lhsT=g_codes[:, C * e : C * (e + 1)].bitcast(FP8X4),
                 lhsT_scale=g_scales[:, C * e : C * (e + 1)],
-                rhs=w2[:, e, 1024 * s : 1024 * (s + 1)].bitcast(FP4X4),
-                rhs_scale=w2_plane[:, e, 512 * s : 512 * (s + 1)],
+                rhs=w2[s, e // 2][:, e % 2, :].bitcast(FP4X4),
+                rhs_scale=w2_plane[s][:, e, :],
                 start=True,
                 stop=True,
             )
@@ -178,44 +185,44 @@ def tile_moe_bdx_glu_sigmoid_kernel(
             turned[e, s] = dh
 
         def saved_slice(name, e, s):
-            if s == 0:
-                half, h = divmod(e, 2)
-                tile = saved[name, 0, half]
-            else:
-                h, tile = e, saved[name, 1]
-            return tile[:, :, C * h : C * (h + 1)]
+            half, h = divmod(e, 2)
+            return saved[name, s, half][:, :, C * h : C * (h + 1)]
+
+        made = {}
 
         def sigmoid(e, s):
-            nc.scalar.activation(
-                woven_by_pairs(saved["sig", e, s][:]), planes_by_pairs(saved_slice("a1", e, s)), SIGMOID
-            )
+            sig = keep.tile([P, C, 4], F32, name="sig_%d%d" % (e, s))
+            nc.scalar.activation(woven_by_pairs(sig[:]), planes_by_pairs(saved_slice("a1", e, s)), SIGMOID)
+            made["sig", e, s] = sig
 
         def square(e, s):
+            sq = keep.tile([P, 4, C], F32, name="sq_%d%d" % (e, s))
             nc.scalar.activation(
-                planes_by_pairs(saved["sq", e, s][:]), woven_by_pairs(saved["sig", e, s][:]), SQUARE, bias=minus_half[:]
+                planes_by_pairs(sq[:]), woven_by_pairs(made["sig", e, s][:]), SQUARE, bias=minus_half[:]
             )
-
-        def factors(e, s):
-            sigmoid(e, s)
-            square(e, s)
+            made["sq", e, s] = sq
 
         def factor_products(e, s):
-            nc.vector.scalar_tensor_tensor(
-                saved["nq", e, s][:], saved["sq", e, s][:], 0.25, saved_slice("a3", e, s), SUBTRACT, MULT
-            )
+            nq = keep.tile([P, 4, C], F32, name="nq_%d%d" % (e, s))
+            nc.vector.scalar_tensor_tensor(nq[:], made["sq", e, s][:], 0.25, saved_slice("a3", e, s), SUBTRACT, MULT)
+            made["nq", e, s] = nq
 
         das = {}
 
-        def product_da(e, s):
+        def product_da3(e, s):
             da = ring.tile([P, 2, C, 4], BF16, name="da", align_bytes=64)
+            das[e, s] = da
             minus_dh = turned[e, s][:]
             nc.vector.scalar_tensor_tensor(
-                da[:, 0, :, :], minus_dh.rearrange("p t j -> p j t"), -1.0, saved["sig", e, s][:], MULT, MULT
+                da[:, 0, :, :], minus_dh.rearrange("p t j -> p j t"), -1.0, made["sig", e, s][:], MULT, MULT
             )
+
+        def product_da1(e, s):
+            da = das[e, s]
+            minus_dh = turned[e, s][:]
             nc.vector.tensor_tensor(
-                woven_by_pairs(da[:, 1, :, :]), planes_by_pairs(minus_dh), planes_by_pairs(saved["nq", e, s][:]), MULT
+                woven_by_pairs(da[:, 1, :, :]), planes_by_pairs(minus_dh), planes_by_pairs(made["nq", e, s][:]), MULT
             )
-            das[e, s] = da
 
         def quantize_da(e, s):
             da = das[e, s]
@@ -231,18 +238,18 @@ def tile_moe_bdx_glu_sigmoid_kernel(
             for kt in range(2):
                 bank = psum.tile([P, C], F32, name="dx%d" % kt, bufs=1)
                 banks.append(bank)
-            for s in range(2):
+            for s in (1, 0):
                 words, scales = codes[e, s]
                 for kt in range(2):
                     for a in range(2):
                         nc.tensor.matmul_mx(
                             out=banks[kt][:],
-                            lhsT=w13[:, a, 2 * e + s, 256 * kt : 256 * (kt + 1)].bitcast(FP4X4),
+                            lhsT=w13[a, e // 2][:, 2 * (e % 2) + s, 256 * kt : 256 * (kt + 1)].bitcast(FP4X4),
                             lhsT_scale=w13_plane[:, a, 2 * e + s, P * kt : P * (kt + 1)],
                             rhs=words[:, C * a : C * (a + 1)].bitcast(FP8X4),
                             rhs_scale=scales[:, C * a : C * (a + 1)],
-                            start=(s == 0 and a == 0),
-                            stop=(s == 1 and a == 1),
+                            start=(s == 1 and a == 0),
+                            stop=(s == 0 and a == 1),
                         )
             for kt in range(2):
                 nc.scalar.copy(out=dx_sb[:, kt, C * e : C * (e + 1)], in_=banks[kt][:])
@@ -253,7 +260,8 @@ def tile_moe_bdx_glu_sigmoid_kernel(
         steps = [(e, s) for s in range(2) for e in range(E)]
         for t in range(3):
             gather(t, 0, SLOTS)
-        factors(0, 0)
+        sigmoid(0, 0)
+        square(0, 0)
         gather(3, 0, C)
         gather(3, C, 2 * C)
         interleave(0, nc.vector.tensor_copy)
@@ -263,14 +271,16 @@ def tile_moe_bdx_glu_sigmoid_kernel(
         first_product(0, 0)
         quantize_g(1)
         first_product(1, 0)
-        factors(1, 0)
+        sigmoid(1, 0)
+        square(1, 0)
         interleave(2, nc.vector.tensor_copy)
         interleave(3, nc.vector.tensor_copy)
         factor_products(0, 0)
         quantize_g(2)
         quantize_g(3)
         factor_products(1, 0)
-        factors(2, 0)
+        sigmoid(2, 0)
+        square(2, 0)
         for i in range(len(steps)):
             e, s = steps[i]
             if i + 3 < len(steps):
@@ -279,7 +289,8 @@ def tile_moe_bdx_glu_sigmoid_kernel(
                 first_product(*steps[i + 2])
             if i + 3 < len(steps):
                 square(*steps[i + 3])
-            product_da(e, s)
+            product_da3(e, s)
+            product_da1(e, s)
             if i + 2 < len(steps):
                 factor_products(*steps[i + 2])
             else:
@@ -287,8 +298,9 @@ def tile_moe_bdx_glu_sigmoid_kernel(
             quantize_da(e, s)
             if s == 1:
                 second_product(e)
-        for kt in range(2):
-            scatter(1, 3, kt)
+        for e in (1, 2):
+            for kt in range(2):
+                scatter(e, e + 1, kt)
         for kt in range(2):
             scatter(3, 4, kt)
             nc.sync.dma_start(out=out[P * kt : P * (kt + 1), :], in_=windows[kt][:])

@@ -44,8 +44,11 @@ def tile_moe_bdx_glu_sigmoid_kernel(
 
         offsets = keep.tile([P, SLOTS // 16], U16, name="offsets")
         dy = [keep.tile([P, T], F32, name="dy%d" % t) for t in range(4)]
-        gates = keep.tile([P, SLOTS], F32, name="gates")
-        g4 = keep.tile([P, 4, SLOTS], F32, name="g4")
+        gates = [keep.tile([P, 2 * C], F32, name="gates%d" % half) for half in range(2)]
+        g_all = keep.tile([P, 7 * 2 * C], F32, name="g_all")
+        g4 = [
+            g_all[:, 2 * C * first : 2 * C * (first + 4)].rearrange("p (t j) -> p t j", t=4) for first in (3, 0)
+        ]
         g_bf = keep.tile([P, SLOTS, 4], BF16, name="g_bf", align_bytes=64)
         g_codes = keep.tile([P, SLOTS], U32, name="g_codes", align_bytes=64)
         g_scales = keep.tile([P, SLOTS], U8, name="g_scales", align_bytes=64)
@@ -116,8 +119,10 @@ def tile_moe_bdx_glu_sigmoid_kernel(
         def load_dy(t):
             nc.sync.dma_start(out=dy[t][:], in_=dy_rows[:, t, :])
 
+        load_dy(0)
         nc.sync.dma_start(offsets[:], offs)
-        nc.scalar.dma_start(out=gates[:], in_=gate[0:P, :])
+        for half in range(2):
+            nc.sync.dma_start(out=gates[half][:], in_=gate[0:P, 2 * C * half : 2 * C * (half + 1)])
         for s in range(2):
             nc.vector.memset(as_words(w2_plane[s]), 0)
         nc.vector.memset(minus_half[:], -0.5)
@@ -127,7 +132,7 @@ def tile_moe_bdx_glu_sigmoid_kernel(
         for kt in range(2):
             nc.gpsimd.memset(windows[kt][:], 0.0)
         nc.gpsimd.memset(w13_plane[:].rearrange("p a g k -> p (a g k)").bitcast(I32), 0)
-        for t in range(4):
+        for t in range(1, 4):
             load_dy(t)
         for s in range(2):
             load_saved("a1", s, 0)
@@ -145,18 +150,19 @@ def tile_moe_bdx_glu_sigmoid_kernel(
                 src = words.bitcast(I32).rearrange("e s p k -> p (e s) k")
                 nc.sync.dma_start(out=as_words(w13[a, half]), in_=src[:, 4 * half : 4 * half + 4, :])
 
-        def gather(t, j0, j1):
+        def gather(t, half):
+            j0, j1 = 2 * C * half, 2 * C * (half + 1)
             nc.vector.tensor_tensor(
-                g4[:, t, j0:j1], dy[t][:].indirect(offsets[:, j0 // 16 : j1 // 16]), gates[:, j0:j1], MULT
+                g4[half][:, t, :], dy[t][:].indirect(offsets[:, j0 // 16 : j1 // 16]), gates[half][:], MULT
             )
 
-        def interleave(e, copy):
-            copy(
-                out=woven_by_pairs(g_bf[:, C * e : C * (e + 1), :]), in_=planes_by_pairs(g4[:, :, C * e : C * (e + 1)])
+        def interleave(e0, e1):
+            nc.vector.tensor_copy(
+                out=woven_by_pairs(g_bf[:, C * e0 : C * e1, :]), in_=planes_by_pairs(g4[e0 // 2][:, :, C * (e0 % 2) : C * (e0 % 2 + e1 - e0)])
             )
 
-        def quantize_g(e):
-            cols = slice(C * e, C * (e + 1))
+        def quantize_g(e0, e1):
+            cols = slice(C * e0, C * e1)
             nc.vector.quantize_mx(
                 out=g_codes[:, cols].bitcast(FP8X4),
                 scales=g_scales[:, cols],
@@ -207,10 +213,20 @@ def tile_moe_bdx_glu_sigmoid_kernel(
             nc.vector.scalar_tensor_tensor(nq[:], made["sq", e, s][:], 0.25, saved_slice("a3", e, s), SUBTRACT, MULT)
             made["nq", e, s] = nq
 
+        def shift(e, s):
+            minus_d = keep.tile([P, 4, C], F32, name="minus_d_%d%d" % (e, s))
+            nc.scalar.activation(minus_d[:], made["sq", e, s][:], COPY, bias=-0.25)
+            made["minus_d", e, s] = minus_d
+
+        def factor_products_gpsimd(e, s, slot):
+            nq = keep.tile([P, 4, C], F32, name=slot, align_bytes=64)
+            nc.gpsimd.tensor_tensor(nq[:], made["minus_d", e, s][:], saved_slice("a3", e, s), MULT)
+            made["nq", e, s] = nq
+
         das = {}
 
         def product_da3(e, s):
-            da = ring.tile([P, 2, C, 4], BF16, name="da", align_bytes=64)
+            da = keep.tile([P, 2, C, 4], BF16, name="da_%d%d" % (e, s), align_bytes=64)
             das[e, s] = da
             minus_dh = turned[e, s][:]
             nc.vector.scalar_tensor_tensor(
@@ -234,70 +250,76 @@ def tile_moe_bdx_glu_sigmoid_kernel(
             codes[e, s] = (words, scales)
 
         def second_product(e):
-            banks = []
+            bank = psum.tile([P, 2, C], F32, name="dx")
             for kt in range(2):
-                bank = psum.tile([P, C], F32, name="dx%d" % kt, bufs=1)
-                banks.append(bank)
-            for s in (1, 0):
-                words, scales = codes[e, s]
-                for kt in range(2):
+                for s in (1, 0):
+                    words, scales = codes[e, s]
                     for a in range(2):
+                        cols = slice(C * a, C * (a + 1))
                         nc.tensor.matmul_mx(
-                            out=banks[kt][:],
+                            out=bank[:, kt, :],
                             lhsT=w13[a, e // 2][:, 2 * (e % 2) + s, 256 * kt : 256 * (kt + 1)].bitcast(FP4X4),
                             lhsT_scale=w13_plane[:, a, 2 * e + s, P * kt : P * (kt + 1)],
-                            rhs=words[:, C * a : C * (a + 1)].bitcast(FP8X4),
-                            rhs_scale=scales[:, C * a : C * (a + 1)],
+                            rhs=words[:, cols].bitcast(FP8X4),
+                            rhs_scale=scales[:, cols],
                             start=(s == 1 and a == 0),
                             stop=(s == 0 and a == 1),
                         )
-            for kt in range(2):
-                nc.scalar.copy(out=dx_sb[:, kt, C * e : C * (e + 1)], in_=banks[kt][:])
+            nc.scalar.copy(out=dx_sb[:, :, C * e : C * (e + 1)], in_=bank[:])
 
         def scatter(e0, e1, kt):
             nc.vector.tensor_copy(windows[kt][:].indirect(offsets[:, 8 * e0 : 8 * e1]), dx_sb[:, kt, C * e0 : C * e1])
 
         steps = [(e, s) for s in range(2) for e in range(E)]
         for t in range(3):
-            gather(t, 0, SLOTS)
+            for half in range(2):
+                gather(t, half)
+        gather(3, 0)
         sigmoid(0, 0)
-        square(0, 0)
-        gather(3, 0, C)
-        gather(3, C, 2 * C)
-        interleave(0, nc.vector.tensor_copy)
-        gather(3, 2 * C, SLOTS)
-        quantize_g(0)
-        interleave(1, nc.vector.tensor_copy)
-        first_product(0, 0)
-        quantize_g(1)
-        first_product(1, 0)
         sigmoid(1, 0)
+        square(0, 0)
         square(1, 0)
-        interleave(2, nc.vector.tensor_copy)
-        interleave(3, nc.vector.tensor_copy)
+        interleave(0, 1)
+        interleave(1, 2)
+        quantize_g(0, 1)
+        first_product(0, 0)
+        gather(3, 1)
+        quantize_g(1, 2)
+        first_product(1, 0)
+        interleave(2, 4)
         factor_products(0, 0)
-        quantize_g(2)
-        quantize_g(3)
+        quantize_g(2, 4)
         factor_products(1, 0)
-        sigmoid(2, 0)
-        square(2, 0)
-        for i in range(len(steps)):
-            e, s = steps[i]
-            if i + 3 < len(steps):
-                sigmoid(*steps[i + 3])
-            if i + 2 < len(steps):
-                first_product(*steps[i + 2])
-            if i + 3 < len(steps):
-                square(*steps[i + 3])
-            product_da3(e, s)
-            product_da1(e, s)
-            if i + 2 < len(steps):
-                factor_products(*steps[i + 2])
+        for i in range(0, len(steps), 2):
+            first, second = steps[i], steps[i + 1]
+            ahead = steps[i + 2 : i + 4]
+            if ahead:
+                sigmoid(*ahead[0])
+                sigmoid(*ahead[1])
+                square(*ahead[0])
+                square(*ahead[1])
+                first_product(*ahead[0])
+                if i + 2 >= 4:
+                    shift(*ahead[1])
+                first_product(*ahead[1])
+            if i >= 4:
+                factor_products_gpsimd(*second, "da_%d%d" % steps[i - 1])
+            product_da3(*first)
+            product_da1(*first)
+            product_da3(*second)
+            quantize_da(*first)
+            product_da1(*second)
+            if ahead:
+                factor_products(*ahead[0])
             else:
-                scatter(0, 1, i + 2 - len(steps))
-            quantize_da(e, s)
-            if s == 1:
-                second_product(e)
+                scatter(0, 1, 0)
+            quantize_da(*second)
+            if ahead and not i + 2 >= 4:
+                factor_products(*ahead[1])
+            for e, s in (first, second):
+                if s == 1:
+                    second_product(e)
+        scatter(0, 1, 1)
         for e in (1, 2):
             for kt in range(2):
                 scatter(e, e + 1, kt)

@@ -131,7 +131,7 @@ def tile_moe_bdx_glu_sigmoid_kernel(
         make_identity(nc, ident[:])
         for kt in range(2):
             nc.gpsimd.memset(windows[kt][:], 0.0)
-        nc.gpsimd.memset(w13_plane[:].rearrange("p a g k -> p (a g k)").bitcast(I32), 0)
+        nc.vector.memset(w13_plane[:].rearrange("p a g k -> p (a g k)").bitcast(I32), 0)
         for t in range(1, 4):
             load_dy(t)
         for s in range(2):
@@ -213,20 +213,10 @@ def tile_moe_bdx_glu_sigmoid_kernel(
             nc.vector.scalar_tensor_tensor(nq[:], made["sq", e, s][:], 0.25, saved_slice("a3", e, s), SUBTRACT, MULT)
             made["nq", e, s] = nq
 
-        def shift(e, s):
-            minus_d = keep.tile([P, 4, C], F32, name="minus_d_%d%d" % (e, s))
-            nc.scalar.activation(minus_d[:], made["sq", e, s][:], COPY, bias=-0.25)
-            made["minus_d", e, s] = minus_d
-
-        def factor_products_gpsimd(e, s, slot):
-            nq = keep.tile([P, 4, C], F32, name=slot, align_bytes=64)
-            nc.gpsimd.tensor_tensor(nq[:], made["minus_d", e, s][:], saved_slice("a3", e, s), MULT)
-            made["nq", e, s] = nq
-
         das = {}
 
         def product_da3(e, s):
-            da = keep.tile([P, 2, C, 4], BF16, name="da_%d%d" % (e, s), align_bytes=64)
+            da = ring.tile([P, 2, C, 4], BF16, name="da", align_bytes=64)
             das[e, s] = da
             minus_dh = turned[e, s][:]
             nc.vector.scalar_tensor_tensor(
@@ -293,17 +283,12 @@ def tile_moe_bdx_glu_sigmoid_kernel(
         for i in range(0, len(steps), 2):
             first, second = steps[i], steps[i + 1]
             ahead = steps[i + 2 : i + 4]
-            if ahead:
-                sigmoid(*ahead[0])
-                sigmoid(*ahead[1])
-                square(*ahead[0])
-                square(*ahead[1])
-                first_product(*ahead[0])
-                if i + 2 >= 4:
-                    shift(*ahead[1])
-                first_product(*ahead[1])
-            if i >= 4:
-                factor_products_gpsimd(*second, "da_%d%d" % steps[i - 1])
+            for step in ahead:
+                sigmoid(*step)
+            for step in ahead:
+                square(*step)
+            for step in ahead:
+                first_product(*step)
             product_da3(*first)
             product_da1(*first)
             product_da3(*second)
@@ -314,7 +299,7 @@ def tile_moe_bdx_glu_sigmoid_kernel(
             else:
                 scatter(0, 1, 0)
             quantize_da(*second)
-            if ahead and not i + 2 >= 4:
+            if ahead:
                 factor_products(*ahead[1])
             for e, s in (first, second):
                 if s == 1:

@@ -100,19 +100,16 @@ def tile_moe_bdx_glu_sigmoid_kernel(
             )
 
         def load_w2_scales(s):
-            for quad in range(4):
+            for r in range(4):
                 nc.sync.dma_start(
-                    out=as_words(w2_plane[s])[32 * quad : 32 * quad + 4, :, :],
-                    in_=w2_scale_src[4 * quad : 4 * quad + 4, :, 128 * s : 128 * (s + 1)],
+                    out=as_words(w2_plane[s])[r:P:32, :, :],
+                    in_=w2_scale_src[r:16:4, :, 128 * s : 128 * (s + 1)],
                 )
 
         def load_w13_scales(a, scales):
             scale_src = scales.bitcast(I32).rearrange("e s f k -> f (e s) k")
-            for quad in range(4):
-                nc.sync.dma_start(
-                    out=w13_plane_dst[32 * quad : 32 * quad + 4, a, :, :],
-                    in_=scale_src[4 * quad : 4 * quad + 4, :, :],
-                )
+            for r in range(4):
+                nc.sync.dma_start(out=w13_plane_dst[r:P:32, a, :, :], in_=scale_src[r:16:4, :, :])
 
         dy_rows = dyT.rearrange("(p t) j -> p t j", t=4)
 

@@ -6,6 +6,8 @@ from concourse.masks import make_identity
 N, T, E, C, H, K = 512, 768, 4, 128, 1024, 256
 SLOTS = E * C
 P = 128
+W13_LOADS = ((0, 2), (2, 3), (3, 4))
+W13_FIRST = (0, 0, 2, 3)
 
 FLOPS = 2 * SLOTS * H * (N + 2 * K)
 BYTES = 4 * (N * T + 2 * H * SLOTS + P * SLOTS + K * T) + 2 * P * SLOTS // 16 + E * (N * H + 2 * H * K) * 17 // 32
@@ -33,6 +35,10 @@ def woven_by_pairs(ap):
     return ap.rearrange("p (c i) t -> p c t i", i=2)
 
 
+def as_words(tile):
+    return tile[:].rearrange("p r b -> p (r b)").bitcast(I32).rearrange("p (r w) -> p r w", r=tile.shape[1])
+
+
 def tile_moe_bdx_glu_sigmoid_kernel(
     tc, dyT, a1, a3, w2_words, w2_scales, w1_words, w1_scales, w3_words, w3_scales, gate, offs, out
 ):
@@ -44,11 +50,8 @@ def tile_moe_bdx_glu_sigmoid_kernel(
 
         offsets = keep.tile([P, SLOTS // 16], U16, name="offsets")
         dy = [keep.tile([P, T], F32, name="dy%d" % t) for t in range(4)]
-        gates = [keep.tile([P, 2 * C], F32, name="gates%d" % half) for half in range(2)]
-        g_all = keep.tile([P, 7 * 2 * C], F32, name="g_all")
-        g4 = [
-            g_all[:, 2 * C * first : 2 * C * (first + 4)].rearrange("p (t j) -> p t j", t=4) for first in (3, 0)
-        ]
+        gates = keep.tile([P, SLOTS], F32, name="gates")
+        g4 = keep.tile([P, 4, SLOTS], F32, name="g4")
         g_bf = keep.tile([P, SLOTS, 4], BF16, name="g_bf", align_bytes=64)
         g_codes = keep.tile([P, SLOTS], U32, name="g_codes", align_bytes=64)
         g_scales = keep.tile([P, SLOTS], U8, name="g_scales", align_bytes=64)
@@ -57,17 +60,17 @@ def tile_moe_bdx_glu_sigmoid_kernel(
             for s in range(2)
             for half in range(2)
         }
-        w2_plane = [keep.tile([P, E, 512], U8, name="w2_plane%d" % s, align_bytes=64) for s in range(2)]
+        w2_scale_rows = [keep.tile([P, E, 512], U8, name="w2_scale_rows%d" % s, align_bytes=64) for s in range(2)]
         w13 = {
-            (a, half): keep.tile([P, 4, 2 * K], U8, name="w13_%d%d" % (a, half), align_bytes=64)
+            (a, e0): keep.tile([P, 2 * (e1 - e0), 2 * K], U8, name="w13_%d%d" % (a, e0), align_bytes=64)
             for a in range(2)
-            for half in range(2)
+            for e0, e1 in W13_LOADS
         }
-        w13_plane = keep.tile([P, 2, 2 * E, K], U8, name="w13_plane", align_bytes=64)
+        w13_scale_rows = keep.tile([P, 2, 2 * E, K], U8, name="w13_scale_rows", align_bytes=64)
         ident = keep.tile([P, P], F32, name="ident")
         windows = [keep.tile([P, T], F32, name="window%d" % kt) for kt in range(2)]
-        warm = keep.tile([P, 1], F32, name="warm")
-        minus_half = keep.tile([P, 1], F32, name="minus_half")
+        zero = keep.tile([P, 1], F32, name="zero")
+        one_half = keep.tile([P, 1], F32, name="one_half")
         saved = {}
         for name in ("a1", "a3"):
             for s in range(2):
@@ -76,6 +79,18 @@ def tile_moe_bdx_glu_sigmoid_kernel(
         dx_sb = keep.tile([P, 2, SLOTS], F32, name="dx_sb")
 
         sources = {"a1": a1, "a3": a3}
+        dy_rows = dyT.rearrange("(p t) j -> p t j", t=4)
+        w2_src = w2_words.bitcast(I32).rearrange("e s p i -> p (e s) i")
+        w2_scale_src = w2_scales.bitcast(I32).rearrange("e s f i -> f (e s) i")
+        w13_scale_dst = (
+            w13_scale_rows[:]
+            .rearrange("p a g k -> p (a g k)")
+            .bitcast(I32)
+            .rearrange("p (a g k) -> p a g k", a=2, g=2 * E)
+        )
+
+        def load_dy(t):
+            nc.sync.dma_start(out=dy[t][:], in_=dy_rows[:, t, :])
 
         def load_saved(name, s, half):
             nc.sync.dma_start(
@@ -85,15 +100,6 @@ def tile_moe_bdx_glu_sigmoid_kernel(
                 ),
             )
 
-        w2_src = w2_words.bitcast(I32).rearrange("e s p i -> p (e s) i")
-        w2_scale_src = w2_scales.bitcast(I32).rearrange("e s f i -> f (e s) i")
-        w13_plane_dst = (
-            w13_plane[:].rearrange("p a g k -> p (a g k)").bitcast(I32).rearrange("p (a g k) -> p a g k", a=2, g=2 * E)
-        )
-
-        def as_words(tile):
-            return tile[:].rearrange("p e i -> p (e i)").bitcast(I32).rearrange("p (e i) -> p e i", e=tile.shape[1])
-
         def load_w2(s, half):
             nc.sync.dma_start(
                 out=as_words(w2[s, half]), in_=w2_src[:, 2 * half : 2 * half + 2, 256 * s : 256 * (s + 1)]
@@ -102,33 +108,28 @@ def tile_moe_bdx_glu_sigmoid_kernel(
         def load_w2_scales(s):
             for r in range(4):
                 nc.sync.dma_start(
-                    out=as_words(w2_plane[s])[r:P:32, :, :],
+                    out=as_words(w2_scale_rows[s])[r:P:32, :, :],
                     in_=w2_scale_src[r:16:4, :, 128 * s : 128 * (s + 1)],
                 )
 
         def load_w13_scales(a, scales):
             scale_src = scales.bitcast(I32).rearrange("e s f k -> f (e s) k")
             for r in range(4):
-                nc.sync.dma_start(out=w13_plane_dst[r:P:32, a, :, :], in_=scale_src[r:16:4, :, :])
-
-        dy_rows = dyT.rearrange("(p t) j -> p t j", t=4)
-
-        def load_dy(t):
-            nc.sync.dma_start(out=dy[t][:], in_=dy_rows[:, t, :])
+                nc.sync.dma_start(out=w13_scale_dst[r:P:32, a, :, :], in_=scale_src[r:16:4, :, :])
 
         load_dy(0)
         nc.sync.dma_start(offsets[:], offs)
         for half in range(2):
-            nc.sync.dma_start(out=gates[half][:], in_=gate[0:P, 2 * C * half : 2 * C * (half + 1)])
+            cols = slice(2 * C * half, 2 * C * (half + 1))
+            nc.sync.dma_start(out=gates[:, cols], in_=gate[0:P, cols])
         for s in range(2):
-            nc.vector.memset(as_words(w2_plane[s]), 0)
-        nc.vector.memset(minus_half[:], -0.5)
-        nc.vector.memset(warm[:], 0.0)
-        nc.scalar.activation(warm[:], warm[:], SIGMOID)
+            nc.vector.memset(as_words(w2_scale_rows[s]), 0)
+        nc.vector.memset(zero[:], 0.0)
+        nc.scalar.activation(one_half[:], zero[:], SIGMOID)
         make_identity(nc, ident[:])
         for kt in range(2):
             nc.gpsimd.memset(windows[kt][:], 0.0)
-        nc.vector.memset(w13_plane[:].rearrange("p a g k -> p (a g k)").bitcast(I32), 0)
+        nc.vector.memset(w13_scale_rows[:].rearrange("p a g k -> p (a g k)").bitcast(I32), 0)
         for t in range(1, 4):
             load_dy(t)
         for s in range(2):
@@ -142,20 +143,20 @@ def tile_moe_bdx_glu_sigmoid_kernel(
                 load_w13_scales(0, w3_scales)
             load_saved("a3", s, 1)
         load_w13_scales(1, w1_scales)
-        for half in range(2):
+        for e0, e1 in W13_LOADS:
             for a, words in ((0, w3_words), (1, w1_words)):
                 src = words.bitcast(I32).rearrange("e s p k -> p (e s) k")
-                nc.sync.dma_start(out=as_words(w13[a, half]), in_=src[:, 4 * half : 4 * half + 4, :])
+                nc.sync.dma_start(out=as_words(w13[a, e0]), in_=src[:, 2 * e0 : 2 * e1, :])
 
-        def gather(t, half):
-            j0, j1 = 2 * C * half, 2 * C * (half + 1)
+        def gather(t, e0, e1):
+            j0, j1 = C * e0, C * e1
             nc.vector.tensor_tensor(
-                g4[half][:, t, :], dy[t][:].indirect(offsets[:, j0 // 16 : j1 // 16]), gates[half][:], MULT
+                g4[:, t, j0:j1], dy[t][:].indirect(offsets[:, j0 // 16 : j1 // 16]), gates[:, j0:j1], MULT
             )
 
         def interleave(e0, e1):
             nc.vector.tensor_copy(
-                out=woven_by_pairs(g_bf[:, C * e0 : C * e1, :]), in_=planes_by_pairs(g4[e0 // 2][:, :, C * (e0 % 2) : C * (e0 % 2 + e1 - e0)])
+                out=woven_by_pairs(g_bf[:, C * e0 : C * e1, :]), in_=planes_by_pairs(g4[:, :, C * e0 : C * e1])
             )
 
         def quantize_g(e0, e1):
@@ -166,8 +167,7 @@ def tile_moe_bdx_glu_sigmoid_kernel(
                 in_=g_bf[:, cols, :].rearrange("p j t -> p (j t)"),
             )
 
-        turned = {}
-        codes = {}
+        made = {}
 
         def first_product(e, s):
             dhT = psum.tile([P, 512], F32, name="dhT")
@@ -176,22 +176,20 @@ def tile_moe_bdx_glu_sigmoid_kernel(
                 lhsT=g_codes[:, C * e : C * (e + 1)].bitcast(FP8X4),
                 lhsT_scale=g_scales[:, C * e : C * (e + 1)],
                 rhs=w2[s, e // 2][:, e % 2, :].bitcast(FP4X4),
-                rhs_scale=w2_plane[s][:, e, :],
+                rhs_scale=w2_scale_rows[s][:, e, :],
                 start=True,
                 stop=True,
             )
             dhT_sb = ring.tile([P, 4, P], F32, name="dhT_sb")
             nc.scalar.activation(dhT_sb[:], dhT[:].rearrange("j (m t) -> j t m", t=4), COPY, scale=-1.0)
-            dh = psum.tile([P, 4, P], F32, name="dh", bufs=4)
+            minus_dh = psum.tile([P, 4, P], F32, name="minus_dh", bufs=4)
             for t in range(4):
-                nc.tensor.transpose(dh[:, t, :], dhT_sb[:, t, :], ident[:])
-            turned[e, s] = dh
+                nc.tensor.transpose(minus_dh[:, t, :], dhT_sb[:, t, :], ident[:])
+            made["minus_dh", e, s] = minus_dh
 
         def saved_slice(name, e, s):
             half, h = divmod(e, 2)
             return saved[name, s, half][:, :, C * h : C * (h + 1)]
-
-        made = {}
 
         def sigmoid(e, s):
             sig = keep.tile([P, C, 4], F32, name="sig_%d%d" % (e, s))
@@ -201,53 +199,58 @@ def tile_moe_bdx_glu_sigmoid_kernel(
         def square(e, s):
             sq = keep.tile([P, 4, C], F32, name="sq_%d%d" % (e, s))
             nc.scalar.activation(
-                planes_by_pairs(sq[:]), woven_by_pairs(made["sig", e, s][:]), SQUARE, bias=minus_half[:]
+                planes_by_pairs(sq[:]), woven_by_pairs(made["sig", e, s][:]), SQUARE, bias=one_half[:], scale=-1.0
             )
             made["sq", e, s] = sq
 
-        def factor_products(e, s):
+        def da1_factor(e, s):
             nq = keep.tile([P, 4, C], F32, name="nq_%d%d" % (e, s))
             nc.vector.scalar_tensor_tensor(nq[:], made["sq", e, s][:], 0.25, saved_slice("a3", e, s), SUBTRACT, MULT)
             made["nq", e, s] = nq
 
-        das = {}
-
         def product_da3(e, s):
             da = ring.tile([P, 2, C, 4], BF16, name="da", align_bytes=64)
-            das[e, s] = da
-            minus_dh = turned[e, s][:]
+            made["da", e, s] = da
             nc.vector.scalar_tensor_tensor(
-                da[:, 0, :, :], minus_dh.rearrange("p t j -> p j t"), -1.0, made["sig", e, s][:], MULT, MULT
+                da[:, 0, :, :],
+                made["minus_dh", e, s][:].rearrange("p t j -> p j t"),
+                -1.0,
+                made["sig", e, s][:],
+                MULT,
+                MULT,
             )
 
         def product_da1(e, s):
-            da = das[e, s]
-            minus_dh = turned[e, s][:]
             nc.vector.tensor_tensor(
-                woven_by_pairs(da[:, 1, :, :]), planes_by_pairs(minus_dh), planes_by_pairs(made["nq", e, s][:]), MULT
+                woven_by_pairs(made["da", e, s][:, 1, :, :]),
+                planes_by_pairs(made["minus_dh", e, s][:]),
+                planes_by_pairs(made["nq", e, s][:]),
+                MULT,
             )
 
         def quantize_da(e, s):
-            da = das[e, s]
-            words = keep.tile([P, 2 * C], U32, name="da_codes_%d%d" % (e, s), align_bytes=64)
+            codes = keep.tile([P, 2 * C], U32, name="da_codes_%d%d" % (e, s), align_bytes=64)
             scales = keep.tile([P, 2 * C], U8, name="da_scales_%d%d" % (e, s), align_bytes=64)
             nc.vector.quantize_mx(
-                out=words[:].bitcast(FP8X4), scales=scales[:], in_=da[:].rearrange("p a j t -> p (a j t)")
+                out=codes[:].bitcast(FP8X4),
+                scales=scales[:],
+                in_=made["da", e, s][:].rearrange("p a j t -> p (a j t)"),
             )
-            codes[e, s] = (words, scales)
+            made["da_mx", e, s] = (codes, scales)
 
         def second_product(e):
             bank = psum.tile([P, 2, C], F32, name="dx")
             for kt in range(2):
                 for s in (1, 0):
-                    words, scales = codes[e, s]
+                    codes, scales = made["da_mx", e, s]
                     for a in range(2):
                         cols = slice(C * a, C * (a + 1))
+                        row = 2 * (e - W13_FIRST[e]) + s
                         nc.tensor.matmul_mx(
                             out=bank[:, kt, :],
-                            lhsT=w13[a, e // 2][:, 2 * (e % 2) + s, 256 * kt : 256 * (kt + 1)].bitcast(FP4X4),
-                            lhsT_scale=w13_plane[:, a, 2 * e + s, P * kt : P * (kt + 1)],
-                            rhs=words[:, cols].bitcast(FP8X4),
+                            lhsT=w13[a, W13_FIRST[e]][:, row, 256 * kt : 256 * (kt + 1)].bitcast(FP4X4),
+                            lhsT_scale=w13_scale_rows[:, a, 2 * e + s, P * kt : P * (kt + 1)],
+                            rhs=codes[:, cols].bitcast(FP8X4),
                             rhs_scale=scales[:, cols],
                             start=(s == 1 and a == 0),
                             stop=(s == 0 and a == 1),
@@ -257,11 +260,12 @@ def tile_moe_bdx_glu_sigmoid_kernel(
         def scatter(e0, e1, kt):
             nc.vector.tensor_copy(windows[kt][:].indirect(offsets[:, 8 * e0 : 8 * e1]), dx_sb[:, kt, C * e0 : C * e1])
 
-        steps = [(e, s) for s in range(2) for e in range(E)]
-        for t in range(3):
-            for half in range(2):
-                gather(t, half)
-        gather(3, 0)
+        gather(0, 0, 2)
+        gather(0, 2, 4)
+        gather(1, 0, 4)
+        gather(2, 0, 4)
+        gather(3, 0, 2)
+        gather(3, 2, 4)
         sigmoid(0, 0)
         sigmoid(1, 0)
         square(0, 0)
@@ -270,13 +274,14 @@ def tile_moe_bdx_glu_sigmoid_kernel(
         interleave(1, 2)
         quantize_g(0, 1)
         first_product(0, 0)
-        gather(3, 1)
         quantize_g(1, 2)
         first_product(1, 0)
         interleave(2, 4)
-        factor_products(0, 0)
+        da1_factor(0, 0)
         quantize_g(2, 4)
-        factor_products(1, 0)
+        da1_factor(1, 0)
+
+        steps = [(e, s) for s in range(2) for e in range(E)]
         for i in range(0, len(steps), 2):
             first, second = steps[i], steps[i + 1]
             ahead = steps[i + 2 : i + 4]
@@ -292,19 +297,19 @@ def tile_moe_bdx_glu_sigmoid_kernel(
             quantize_da(*first)
             product_da1(*second)
             if ahead:
-                factor_products(*ahead[0])
+                da1_factor(*ahead[0])
             else:
                 scatter(0, 1, 0)
             quantize_da(*second)
             if ahead:
-                factor_products(*ahead[1])
+                da1_factor(*ahead[1])
             for e, s in (first, second):
                 if s == 1:
                     second_product(e)
-        scatter(0, 1, 1)
-        for e in (1, 2):
-            for kt in range(2):
-                scatter(e, e + 1, kt)
-        for kt in range(2):
-            scatter(3, 4, kt)
-            nc.sync.dma_start(out=out[P * kt : P * (kt + 1), :], in_=windows[kt][:])
+
+        scatter(0, 2, 1)
+        scatter(1, 3, 0)
+        scatter(2, 4, 1)
+        nc.sync.dma_start(out=out[P : 2 * P, :], in_=windows[1][:])
+        scatter(3, 4, 0)
+        nc.sync.dma_start(out=out[0:P, :], in_=windows[0][:])

@@ -8,6 +8,9 @@ SLOTS = E * C
 P = 128
 W13_LOADS = ((0, 2), (2, 3), (3, 4))
 W13_FIRST = (0, 0, 2, 3)
+PIECES = (((0, 0),), ((1, 0),), ((0, 1), (1, 1)), ((2, 0), (2, 1)), ((3, 0), (3, 1)))
+PIECE_OF = {step: piece for piece in PIECES for step in piece}
+NO_SQUARE = (PIECES[2],)
 
 FLOPS = 2 * SLOTS * H * (N + 2 * K)
 BYTES = 4 * (N * T + 2 * H * SLOTS + P * SLOTS + K * T) + 2 * P * SLOTS // 16 + E * (N * H + 2 * H * K) * 17 // 32
@@ -50,17 +53,13 @@ def tile_moe_bdx_glu_sigmoid_kernel(
 
         offsets = keep.tile([P, SLOTS // 16], U16, name="offsets")
         dy = [keep.tile([P, T], F32, name="dy%d" % t) for t in range(4)]
-        gates = keep.tile([P, SLOTS], F32, name="gates")
-        g4 = keep.tile([P, 4, SLOTS], F32, name="g4")
+        gates = [keep.tile([P, 2 * C], F32, name="gates%d" % half) for half in range(2)]
+        g4 = [keep.tile([P, 4, 2 * C], F32, name="g4_%d" % half) for half in range(2)]
         g_bf = keep.tile([P, SLOTS, 4], BF16, name="g_bf", align_bytes=64)
         g_codes = keep.tile([P, SLOTS], U32, name="g_codes", align_bytes=64)
         g_scales = keep.tile([P, SLOTS], U8, name="g_scales", align_bytes=64)
-        w2 = {
-            (s, half): keep.tile([P, 2, H], U8, name="w2_%d%d" % (s, half), align_bytes=64)
-            for s in range(2)
-            for half in range(2)
-        }
-        w2_scale_rows = [keep.tile([P, E, 512], U8, name="w2_scale_rows%d" % s, align_bytes=64) for s in range(2)]
+        w2 = [keep.tile([P, 2, H], U8, name="w2_%d" % n, align_bytes=64) for n in range(4)]
+        w2_scale_rows = [keep.tile([P, 2, H], U8, name="w2_scale_rows%d" % half, align_bytes=64) for half in range(2)]
         w13 = {
             (a, e0): keep.tile([P, 2 * (e1 - e0), 2 * K], U8, name="w13_%d%d" % (a, e0), align_bytes=64)
             for a in range(2)
@@ -73,9 +72,8 @@ def tile_moe_bdx_glu_sigmoid_kernel(
         one_half = keep.tile([P, 1], F32, name="one_half")
         saved = {}
         for name in ("a1", "a3"):
-            for s in range(2):
-                for half in range(2):
-                    saved[name, s, half] = keep.tile([P, 4, 2 * C], F32, name="%s_%d%d" % (name, s, half))
+            for piece in PIECES:
+                saved[name, piece] = keep.tile([P, 4, len(piece) * C], F32, name="%s_%d%d" % ((name,) + piece[0]))
         dx_sb = keep.tile([P, 2, SLOTS], F32, name="dx_sb")
 
         sources = {"a1": a1, "a3": a3}
@@ -92,24 +90,29 @@ def tile_moe_bdx_glu_sigmoid_kernel(
         def load_dy(t):
             nc.sync.dma_start(out=dy[t][:], in_=dy_rows[:, t, :])
 
-        def load_saved(name, s, half):
-            nc.sync.dma_start(
-                out=saved[name, s, half][:],
-                in_=sources[name][512 * s : 512 * (s + 1), 2 * C * half : 2 * C * (half + 1)].rearrange(
-                    "(p t) j -> p t j", t=4
-                ),
-            )
+        def load_saved(name, piece):
+            (e0, s0), (e1, s1) = piece[0], piece[-1]
+            if s0 == s1:
+                rows = sources[name][512 * s0 : 512 * (s0 + 1), C * e0 : C * (e1 + 1)]
+                nc.sync.dma_start(out=saved[name, piece][:], in_=rows.rearrange("(p t) j -> p t j", t=4))
+            else:
+                rows = sources[name][:, C * e0 : C * (e0 + 1)]
+                nc.sync.dma_start(
+                    out=saved[name, piece][:].rearrange("p t (s j) -> p t s j", s=2),
+                    in_=rows.rearrange("(s p t) j -> p t s j", s=2, t=4),
+                )
 
-        def load_w2(s, half):
-            nc.sync.dma_start(
-                out=as_words(w2[s, half]), in_=w2_src[:, 2 * half : 2 * half + 2, 256 * s : 256 * (s + 1)]
-            )
+        def load_w2(n):
+            if n < 2:
+                nc.sync.dma_start(out=as_words(w2[n]), in_=w2_src[:, 0:2, 256 * n : 256 * (n + 1)])
+            else:
+                nc.sync.dma_start(out=as_words(w2[n]), in_=w2_src[:, n, :].rearrange("p (s i) -> p s i", s=2))
 
-        def load_w2_scales(s):
+        def load_w2_scales(half):
             for r in range(4):
                 nc.sync.dma_start(
-                    out=as_words(w2_scale_rows[s])[r:P:32, :, :],
-                    in_=w2_scale_src[r:16:4, :, 128 * s : 128 * (s + 1)],
+                    out=as_words(w2_scale_rows[half])[r:P:32, :, :],
+                    in_=w2_scale_src[r:16:4, 2 * half : 2 * half + 2, :],
                 )
 
         def load_w13_scales(a, scales):
@@ -117,46 +120,71 @@ def tile_moe_bdx_glu_sigmoid_kernel(
             for r in range(4):
                 nc.sync.dma_start(out=w13_scale_dst[r:P:32, a, :, :], in_=scale_src[r:16:4, :, :])
 
+        def load_gate(half):
+            cols = slice(2 * C * half, 2 * C * (half + 1))
+            nc.sync.dma_start(out=gates[half][:], in_=gate[0:P, cols])
+
+        def load_w13(e0, e1):
+            for a, words in ((0, w3_words), (1, w1_words)):
+                src = words.bitcast(I32).rearrange("e s p k -> p (e s) k")
+                nc.sync.dma_start(out=as_words(w13[a, e0]), in_=src[:, 2 * e0 : 2 * e1, :])
+
         load_dy(0)
         nc.sync.dma_start(offsets[:], offs)
-        for half in range(2):
-            cols = slice(2 * C * half, 2 * C * (half + 1))
-            nc.sync.dma_start(out=gates[:, cols], in_=gate[0:P, cols])
-        for s in range(2):
-            nc.vector.memset(as_words(w2_scale_rows[s]), 0)
+        load_gate(0)
         nc.vector.memset(zero[:], 0.0)
         nc.scalar.activation(one_half[:], zero[:], SIGMOID)
         make_identity(nc, ident[:])
         for kt in range(2):
             nc.gpsimd.memset(windows[kt][:], 0.0)
-        nc.vector.memset(w13_scale_rows[:].rearrange("p a g k -> p (a g k)").bitcast(I32), 0)
         for t in range(1, 4):
             load_dy(t)
-        for s in range(2):
-            load_saved("a1", s, 0)
-            load_w2(s, 0)
-            load_w2_scales(s)
-            load_saved("a3", s, 0)
-            load_saved("a1", s, 1)
-            load_w2(s, 1)
-            if s == 1:
-                load_w13_scales(0, w3_scales)
-            load_saved("a3", s, 1)
+        load_saved("a1", PIECES[0])
+        load_w2_scales(0)
+        load_w2(0)
+        load_gate(1)
+        load_saved("a3", PIECES[0])
+        load_saved("a1", PIECES[1])
+        load_saved("a3", PIECES[1])
+        load_saved("a1", PIECES[2])
+        load_w2(1)
+        load_saved("a3", PIECES[2])
+        load_saved("a1", PIECES[3])
+        load_w2_scales(1)
+        load_w2(2)
+        load_saved("a3", PIECES[3])
+        load_saved("a1", PIECES[4])
+        load_w2(3)
+        load_w13_scales(0, w3_scales)
         load_w13_scales(1, w1_scales)
-        for e0, e1 in W13_LOADS:
-            for a, words in ((0, w3_words), (1, w1_words)):
-                src = words.bitcast(I32).rearrange("e s p k -> p (e s) k")
-                nc.sync.dma_start(out=as_words(w13[a, e0]), in_=src[:, 2 * e0 : 2 * e1, :])
+        load_w13(*W13_LOADS[0])
+        load_saved("a3", PIECES[4])
+        load_w13(*W13_LOADS[1])
+        load_w13(*W13_LOADS[2])
 
-        def gather(t, e0, e1):
+        def gather_times_gate(t, e0, e1):
             j0, j1 = C * e0, C * e1
             nc.vector.tensor_tensor(
-                g4[:, t, j0:j1], dy[t][:].indirect(offsets[:, j0 // 16 : j1 // 16]), gates[:, j0:j1], MULT
+                g4[0][:, t, j0:j1], dy[t][:].indirect(offsets[:, j0 // 16 : j1 // 16]), gates[0][:, j0:j1], MULT
             )
 
-        def interleave(e0, e1):
+        def gather_plain(t):
+            nc.scalar.activation(g4[1][:, t, :], dy[t][:].indirect(offsets[:, 16:32]), COPY)
+
+        def interleave(e):
             nc.vector.tensor_copy(
-                out=woven_by_pairs(g_bf[:, C * e0 : C * e1, :]), in_=planes_by_pairs(g4[:, :, C * e0 : C * e1])
+                out=woven_by_pairs(g_bf[:, C * e : C * (e + 1), :]),
+                in_=planes_by_pairs(g4[0][:, :, C * e : C * (e + 1)]),
+            )
+
+        def interleave_times_gate(e):
+            cols = slice(C * (e - 2), C * (e - 1))
+            gate_by_pairs = gates[1][:, cols].rearrange("p (c i) -> p c i", i=2).unsqueeze(2)
+            nc.vector.tensor_tensor(
+                woven_by_pairs(g_bf[:, C * e : C * (e + 1), :]),
+                planes_by_pairs(g4[1][:, :, cols]),
+                gate_by_pairs.to_broadcast([P, C // 2, 4, 2]),
+                MULT,
             )
 
         def quantize_g(e0, e1):
@@ -175,37 +203,77 @@ def tile_moe_bdx_glu_sigmoid_kernel(
                 out=dhT[:],
                 lhsT=g_codes[:, C * e : C * (e + 1)].bitcast(FP8X4),
                 lhsT_scale=g_scales[:, C * e : C * (e + 1)],
-                rhs=w2[s, e // 2][:, e % 2, :].bitcast(FP4X4),
-                rhs_scale=w2_scale_rows[s][:, e, :],
+                rhs=(w2[s][:, e, :] if e < 2 else w2[e][:, s, :]).bitcast(FP4X4),
+                rhs_scale=w2_scale_rows[e // 2][:, e % 2, 512 * s : 512 * (s + 1)],
                 start=True,
                 stop=True,
             )
             dhT_sb = ring.tile([P, 4, P], F32, name="dhT_sb")
-            nc.scalar.activation(dhT_sb[:], dhT[:].rearrange("j (m t) -> j t m", t=4), COPY, scale=-1.0)
             minus_dh = psum.tile([P, 4, P], F32, name="minus_dh", bufs=4)
-            for t in range(4):
-                nc.tensor.transpose(minus_dh[:, t, :], dhT_sb[:, t, :], ident[:])
+            width = 2 if (e, s) == (0, 0) else 4
+            for t0 in range(0, 4, width):
+                nc.scalar.activation(
+                    dhT_sb[:, t0 : t0 + width, :],
+                    dhT[:].rearrange("j (m t) -> j t m", t=4)[:, t0 : t0 + width, :],
+                    COPY,
+                    scale=-1.0,
+                )
+                for t in range(t0, t0 + width):
+                    nc.tensor.transpose(minus_dh[:, t, :], dhT_sb[:, t, :], ident[:])
             made["minus_dh", e, s] = minus_dh
 
         def saved_slice(name, e, s):
-            half, h = divmod(e, 2)
-            return saved[name, s, half][:, :, C * h : C * (h + 1)]
+            h = PIECE_OF[e, s].index((e, s))
+            return saved[name, PIECE_OF[e, s]][:, :, C * h : C * (h + 1)]
 
-        def sigmoid(e, s):
-            sig = keep.tile([P, C, 4], F32, name="sig_%d%d" % (e, s))
-            nc.scalar.activation(woven_by_pairs(sig[:]), planes_by_pairs(saved_slice("a1", e, s)), SIGMOID)
-            made["sig", e, s] = sig
+        def sigmoid(piece):
+            sig = keep.tile([P, len(piece) * C, 4], F32, name="sig_%d%d" % piece[0])
+            nc.scalar.activation(woven_by_pairs(sig[:]), planes_by_pairs(saved["a1", piece][:]), SIGMOID)
+            made["sig", piece] = sig
+            for h, (e, s) in enumerate(piece):
+                made["sig", e, s] = sig[:, C * h : C * (h + 1), :]
 
-        def square(e, s):
-            sq = keep.tile([P, 4, C], F32, name="sq_%d%d" % (e, s))
-            nc.scalar.activation(
-                planes_by_pairs(sq[:]), woven_by_pairs(made["sig", e, s][:]), SQUARE, bias=one_half[:], scale=-1.0
+        def sigmoid_planes(piece):
+            sig = keep.tile([P, 4, len(piece) * C], F32, name="sig_%d%d" % piece[0])
+            nc.scalar.activation(sig[:], saved["a1", piece][:], SIGMOID)
+            for h, (e, s) in enumerate(piece):
+                made["sig", e, s] = sig[:, :, C * h : C * (h + 1)]
+
+        def late_factor(e, s):
+            nw = keep.tile([P, 4, C], F32, name="nw_%d%d" % (e, s))
+            nc.vector.scalar_tensor_tensor(nw[:], made["sig", e, s], 1.0, saved_slice("a3", e, s), SUBTRACT, MULT)
+            made["nw", e, s] = nw
+
+        def minus_da3(e, s):
+            nu = ring.tile([P, 4, C], F32, name="nu", bufs=2)
+            nc.vector.tensor_tensor(nu[:], made["minus_dh", e, s][:], made["sig", e, s], MULT)
+            made["nu", e, s] = nu
+            made["da", e, s] = ring.tile([P, 2, C, 4], BF16, name="da", align_bytes=64)
+
+        def round_da3(e, s):
+            nc.vector.tensor_scalar(
+                woven_by_pairs(made["da", e, s][:, 0, :, :]), planes_by_pairs(made["nu", e, s][:]), -1.0, None, MULT
             )
-            made["sq", e, s] = sq
+
+        def late_da1(e, s):
+            nc.vector.tensor_tensor(
+                woven_by_pairs(made["da", e, s][:, 1, :, :]),
+                planes_by_pairs(made["nu", e, s][:]),
+                planes_by_pairs(made["nw", e, s][:]),
+                MULT,
+            )
+
+        def square(piece):
+            sq = keep.tile([P, 4, len(piece) * C], F32, name="sq_%d%d" % piece[0])
+            nc.scalar.activation(
+                planes_by_pairs(sq[:]), woven_by_pairs(made["sig", piece][:]), SQUARE, bias=one_half[:], scale=-1.0
+            )
+            for h, (e, s) in enumerate(piece):
+                made["sq", e, s] = sq[:, :, C * h : C * (h + 1)]
 
         def da1_factor(e, s):
             nq = keep.tile([P, 4, C], F32, name="nq_%d%d" % (e, s))
-            nc.vector.scalar_tensor_tensor(nq[:], made["sq", e, s][:], 0.25, saved_slice("a3", e, s), SUBTRACT, MULT)
+            nc.vector.scalar_tensor_tensor(nq[:], made["sq", e, s], 0.25, saved_slice("a3", e, s), SUBTRACT, MULT)
             made["nq", e, s] = nq
 
         def product_da3(e, s):
@@ -215,7 +283,7 @@ def tile_moe_bdx_glu_sigmoid_kernel(
                 da[:, 0, :, :],
                 made["minus_dh", e, s][:].rearrange("p t j -> p j t"),
                 -1.0,
-                made["sig", e, s][:],
+                made["sig", e, s],
                 MULT,
                 MULT,
             )
@@ -228,88 +296,117 @@ def tile_moe_bdx_glu_sigmoid_kernel(
                 MULT,
             )
 
-        def quantize_da(e, s):
-            codes = keep.tile([P, 2 * C], U32, name="da_codes_%d%d" % (e, s), align_bytes=64)
-            scales = keep.tile([P, 2 * C], U8, name="da_scales_%d%d" % (e, s), align_bytes=64)
+        def quantize_da(e, s, a0=0, a1=2):
+            if a0 == 0:
+                codes = keep.tile([P, 2 * C], U32, name="da_codes_%d%d" % (e, s), align_bytes=64)
+                scales = keep.tile([P, 2 * C], U8, name="da_scales_%d%d" % (e, s), align_bytes=64)
+                made["da_mx", e, s] = (codes, scales)
+            codes, scales = made["da_mx", e, s]
             nc.vector.quantize_mx(
-                out=codes[:].bitcast(FP8X4),
-                scales=scales[:],
-                in_=made["da", e, s][:].rearrange("p a j t -> p (a j t)"),
+                out=codes[:, C * a0 : C * a1].bitcast(FP8X4),
+                scales=scales[:, C * a0 : C * a1],
+                in_=made["da", e, s][:, a0:a1].rearrange("p a j t -> p (a j t)"),
             )
-            made["da_mx", e, s] = (codes, scales)
+
+        def second_passes(dx, e, kt, s, a, start, stop):
+            codes, scales = made["da_mx", e, s]
+            cols = slice(C * a, C * (a + 1))
+            row = 2 * (e - W13_FIRST[e]) + s
+            nc.tensor.matmul_mx(
+                out=dx,
+                lhsT=w13[a, W13_FIRST[e]][:, row, 256 * kt : 256 * (kt + 1)].bitcast(FP4X4),
+                lhsT_scale=w13_scale_rows[:, a, 2 * e + s, P * kt : P * (kt + 1)],
+                rhs=codes[:, cols].bitcast(FP8X4),
+                rhs_scale=scales[:, cols],
+                start=start,
+                stop=stop,
+            )
 
         def second_product(e):
-            bank = psum.tile([P, 2, C], F32, name="dx")
+            bank = psum.tile([P, 2, C], F32, name="dx_%d" % e, tag="dhT" if e == 2 else "dx")
             for kt in range(2):
                 for s in (1, 0):
-                    codes, scales = made["da_mx", e, s]
                     for a in range(2):
-                        cols = slice(C * a, C * (a + 1))
-                        row = 2 * (e - W13_FIRST[e]) + s
-                        nc.tensor.matmul_mx(
-                            out=bank[:, kt, :],
-                            lhsT=w13[a, W13_FIRST[e]][:, row, 256 * kt : 256 * (kt + 1)].bitcast(FP4X4),
-                            lhsT_scale=w13_scale_rows[:, a, 2 * e + s, P * kt : P * (kt + 1)],
-                            rhs=codes[:, cols].bitcast(FP8X4),
-                            rhs_scale=scales[:, cols],
-                            start=(s == 1 and a == 0),
-                            stop=(s == 0 and a == 1),
-                        )
-            nc.scalar.copy(out=dx_sb[:, :, C * e : C * (e + 1)], in_=bank[:])
+                        second_passes(bank[:, kt, :], e, kt, s, a, s == 1 and a == 0, s == 0 and a == 1)
+            return bank
 
-        def scatter(e0, e1, kt):
-            nc.vector.tensor_copy(windows[kt][:].indirect(offsets[:, 8 * e0 : 8 * e1]), dx_sb[:, kt, C * e0 : C * e1])
+        def scatter_on_vector(e, kt, values):
+            nc.vector.tensor_copy(windows[kt][:].indirect(offsets[:, 8 * e : 8 * (e + 1)]), values)
 
-        gather(0, 0, 2)
-        gather(0, 2, 4)
-        gather(1, 0, 4)
-        gather(2, 0, 4)
-        gather(3, 0, 2)
-        gather(3, 2, 4)
-        sigmoid(0, 0)
-        sigmoid(1, 0)
-        square(0, 0)
-        square(1, 0)
-        interleave(0, 1)
-        interleave(1, 2)
+        def scatter_on_scalar(e0, e1, kt):
+            nc.scalar.activation(
+                windows[kt][:].indirect(offsets[:, 8 * e0 : 8 * e1]), dx_sb[:, kt, C * e0 : C * e1], COPY
+            )
+
+        for t in range(3):
+            gather_times_gate(t, 0, 2)
+            gather_plain(t)
+        gather_times_gate(3, 0, 1)
+        interleave(0)
         quantize_g(0, 1)
-        first_product(0, 0)
+        gather_times_gate(3, 1, 2)
+        interleave(1)
         quantize_g(1, 2)
+        gather_plain(3)
+        sigmoid(PIECES[0])
+        square(PIECES[0])
+        first_product(0, 0)
         first_product(1, 0)
-        interleave(2, 4)
+        sigmoid(PIECES[1])
+        square(PIECES[1])
         da1_factor(0, 0)
-        quantize_g(2, 4)
-        da1_factor(1, 0)
 
-        steps = [(e, s) for s in range(2) for e in range(E)]
-        for i in range(0, len(steps), 2):
-            first, second = steps[i], steps[i + 1]
-            ahead = steps[i + 2 : i + 4]
-            for step in ahead:
-                sigmoid(*step)
-            for step in ahead:
-                square(*step)
-            for step in ahead:
-                first_product(*step)
-            product_da3(*first)
-            product_da1(*first)
-            product_da3(*second)
-            quantize_da(*first)
-            product_da1(*second)
-            if ahead:
-                da1_factor(*ahead[0])
+        def prepare(piece):
+            if piece in NO_SQUARE:
+                sigmoid_planes(piece)
             else:
-                scatter(0, 1, 0)
-            quantize_da(*second)
-            if ahead:
-                da1_factor(*ahead[1])
-            for e, s in (first, second):
-                if s == 1:
-                    second_product(e)
+                sigmoid(piece)
+            for step in piece:
+                first_product(*step)
+            if piece not in NO_SQUARE:
+                square(piece)
 
-        scatter(0, 2, 1)
-        scatter(1, 3, 0)
-        scatter(2, 4, 1)
-        nc.sync.dma_start(out=out[P : 2 * P, :], in_=windows[1][:])
-        scatter(3, 4, 0)
+        def products(piece):
+            if piece in NO_SQUARE:
+                kinds = (late_factor, minus_da3, round_da3, late_da1, quantize_da)
+            else:
+                kinds = (product_da3, da1_factor, product_da1, quantize_da)
+            for kind in kinds:
+                for step in piece:
+                    kind(*step)
+
+        prepare(PIECES[2])
+        product_da3(0, 0)
+        product_da1(0, 0)
+        product_da3(1, 0)
+        quantize_da(0, 0)
+        da1_factor(1, 0)
+        interleave_times_gate(2)
+        product_da1(1, 0)
+        interleave_times_gate(3)
+        quantize_da(1, 0)
+        quantize_g(2, 4)
+        prepare(PIECES[3])
+        products(PIECES[2])
+        prepare(PIECES[4])
+        products(PIECES[3])
+        for e in range(2):
+            nc.scalar.copy(out=dx_sb[:, :, C * e : C * (e + 1)], in_=second_product(e)[:])
+        scatter_on_scalar(0, 2, 0)
+        scatter_on_scalar(0, 2, 1)
+        nc.scalar.copy(out=dx_sb[:, :, 2 * C : 3 * C], in_=second_product(2)[:])
+        scatter_on_scalar(2, 3, 0)
+        scatter_on_scalar(2, 3, 1)
+        products(PIECES[4])
+
+        banks_3 = [psum.tile([P, C], F32, name="dx3_%d" % kt, tag="dx") for kt in range(2)]
+        for s in range(2):
+            for a in range(2):
+                for kt in range(2):
+                    second_passes(banks_3[kt][:], 3, kt, s, a, s == 0 and a == 0, s == 1 and a == 1)
+        nc.vector.tensor_copy(out=dx_sb[:, 0, 3 * C : 4 * C], in_=banks_3[0][:])
+        nc.scalar.copy(out=dx_sb[:, 1, 3 * C : 4 * C], in_=banks_3[1][:])
+        scatter_on_vector(3, 0, dx_sb[:, 0, 3 * C : 4 * C])
+        scatter_on_scalar(3, 4, 1)
         nc.sync.dma_start(out=out[0:P, :], in_=windows[0][:])
+        nc.sync.dma_start(out=out[P : 2 * P, :], in_=windows[1][:])

@@ -296,6 +296,19 @@ def tile_moe_bdx_glu_sigmoid_kernel(
                 MULT,
             )
 
+        def slope_times_dh(e, s):
+            y = ring.tile([P, 4, C], F32, name="y")
+            nc.vector.scalar_tensor_tensor(y[:], made["sq", e, s], 0.25, made["minus_dh", e, s][:], SUBTRACT, MULT)
+            made["y", e, s] = y
+
+        def times_a3(e, s):
+            nc.vector.tensor_tensor(
+                woven_by_pairs(made["da", e, s][:, 1, :, :]),
+                planes_by_pairs(made["y", e, s][:]),
+                planes_by_pairs(saved_slice("a3", e, s)),
+                MULT,
+            )
+
         def quantize_da(e, s, a0=0, a1=2):
             if a0 == 0:
                 codes = keep.tile([P, 2 * C], U32, name="da_codes_%d%d" % (e, s), align_bytes=64)
@@ -370,7 +383,7 @@ def tile_moe_bdx_glu_sigmoid_kernel(
             if piece in NO_SQUARE:
                 kinds = (late_factor, minus_da3, round_da3, late_da1, quantize_da)
             else:
-                kinds = (product_da3, da1_factor, product_da1, quantize_da)
+                kinds = (product_da3, slope_times_dh, times_a3, quantize_da)
             for kind in kinds:
                 for step in piece:
                     kind(*step)
@@ -380,9 +393,9 @@ def tile_moe_bdx_glu_sigmoid_kernel(
         product_da1(0, 0)
         product_da3(1, 0)
         quantize_da(0, 0)
-        da1_factor(1, 0)
+        slope_times_dh(1, 0)
         interleave_times_gate(2)
-        product_da1(1, 0)
+        times_a3(1, 0)
         interleave_times_gate(3)
         quantize_da(1, 0)
         quantize_g(2, 4)
@@ -397,11 +410,19 @@ def tile_moe_bdx_glu_sigmoid_kernel(
         nc.scalar.copy(out=dx_sb[:, :, 2 * C : 3 * C], in_=second_product(2)[:])
         scatter_on_scalar(2, 3, 0)
         scatter_on_scalar(2, 3, 1)
-        products(PIECES[4])
+        for step in PIECES[4]:
+            product_da3(*step)
+        for step in PIECES[4]:
+            slope_times_dh(*step)
+            quantize_da(*step, 0, 1)
+        for step in PIECES[4]:
+            times_a3(*step)
+        for step in PIECES[4]:
+            quantize_da(*step, 1, 2)
 
         banks_3 = [psum.tile([P, C], F32, name="dx3_%d" % kt, tag="dx") for kt in range(2)]
-        for s in range(2):
-            for a in range(2):
+        for a in range(2):
+            for s in range(2):
                 for kt in range(2):
                     second_passes(banks_3[kt][:], 3, kt, s, a, s == 0 and a == 0, s == 1 and a == 1)
         nc.vector.tensor_copy(out=dx_sb[:, 0, 3 * C : 4 * C], in_=banks_3[0][:])

@@ -6,11 +6,10 @@ from concourse.masks import make_identity
 N, T, E, C, H, K = 512, 768, 4, 128, 1024, 256
 SLOTS = E * C
 P = 128
-W13_LOADS = ((0, 2), (2, 3), (3, 4))
-W13_FIRST = (0, 0, 2, 3)
-PIECES = (((0, 0),), ((1, 0),), ((0, 1), (1, 1)), ((2, 0), (2, 1)), ((3, 0), (3, 1)))
+W13_LOADS = ((0, 1), (1, 2), (2, 3), (3, 4))
+W13_FIRST = (0, 1, 2, 3)
+PIECES = tuple(((2 * half, s), (2 * half + 1, s)) for half in range(2) for s in range(2))
 PIECE_OF = {step: piece for piece in PIECES for step in piece}
-NO_SQUARE = (PIECES[2],)
 
 FLOPS = 2 * SLOTS * H * (N + 2 * K)
 BYTES = 4 * (N * T + 2 * H * SLOTS + P * SLOTS + K * T) + 2 * P * SLOTS // 16 + E * (N * H + 2 * H * K) * 17 // 32
@@ -54,11 +53,11 @@ def tile_moe_bdx_glu_sigmoid_kernel(
         offsets = keep.tile([P, SLOTS // 16], U16, name="offsets")
         dy = [keep.tile([P, T], F32, name="dy%d" % t) for t in range(4)]
         gates = [keep.tile([P, 2 * C], F32, name="gates%d" % half) for half in range(2)]
-        g4 = [keep.tile([P, 4, 2 * C], F32, name="g4_%d" % half) for half in range(2)]
-        g_bf = keep.tile([P, SLOTS, 4], BF16, name="g_bf", align_bytes=64)
+        g4 = [keep.tile([P, 4, 2 * C], F32, name="g4_%d" % half, align_bytes=64) for half in range(2)]
+        g_bf = {0: keep.tile([P, 2 * C, 4], BF16, name="g_bf0", align_bytes=64)}
         g_codes = keep.tile([P, SLOTS], U32, name="g_codes", align_bytes=64)
         g_scales = keep.tile([P, SLOTS], U8, name="g_scales", align_bytes=64)
-        w2 = [keep.tile([P, 2, H], U8, name="w2_%d" % n, align_bytes=64) for n in range(4)]
+        w2 = {piece: keep.tile([P, 2, H], U8, name="w2_%d%d" % piece[0], align_bytes=64) for piece in PIECES}
         w2_scale_rows = [keep.tile([P, 2, H], U8, name="w2_scale_rows%d" % half, align_bytes=64) for half in range(2)]
         w13 = {
             (a, e0): keep.tile([P, 2 * (e1 - e0), 2 * K], U8, name="w13_%d%d" % (a, e0), align_bytes=64)
@@ -91,22 +90,13 @@ def tile_moe_bdx_glu_sigmoid_kernel(
             nc.sync.dma_start(out=dy[t][:], in_=dy_rows[:, t, :])
 
         def load_saved(name, piece):
-            (e0, s0), (e1, s1) = piece[0], piece[-1]
-            if s0 == s1:
-                rows = sources[name][512 * s0 : 512 * (s0 + 1), C * e0 : C * (e1 + 1)]
-                nc.sync.dma_start(out=saved[name, piece][:], in_=rows.rearrange("(p t) j -> p t j", t=4))
-            else:
-                rows = sources[name][:, C * e0 : C * (e0 + 1)]
-                nc.sync.dma_start(
-                    out=saved[name, piece][:].rearrange("p t (s j) -> p t s j", s=2),
-                    in_=rows.rearrange("(s p t) j -> p t s j", s=2, t=4),
-                )
+            e0, s = piece[0]
+            rows = sources[name][512 * s : 512 * (s + 1), C * e0 : C * (e0 + 2)]
+            nc.sync.dma_start(out=saved[name, piece][:], in_=rows.rearrange("(p t) j -> p t j", t=4))
 
-        def load_w2(n):
-            if n < 2:
-                nc.sync.dma_start(out=as_words(w2[n]), in_=w2_src[:, 0:2, 256 * n : 256 * (n + 1)])
-            else:
-                nc.sync.dma_start(out=as_words(w2[n]), in_=w2_src[:, n, :].rearrange("p (s i) -> p s i", s=2))
+        def load_w2(piece):
+            e0, s = piece[0]
+            nc.sync.dma_start(out=as_words(w2[piece]), in_=w2_src[:, e0 : e0 + 2, 256 * s : 256 * (s + 1)])
 
         def load_w2_scales(half):
             for r in range(4):
@@ -120,14 +110,13 @@ def tile_moe_bdx_glu_sigmoid_kernel(
             for r in range(4):
                 nc.sync.dma_start(out=w13_scale_dst[r:P:32, a, :, :], in_=scale_src[r:16:4, :, :])
 
-        def load_gate(half):
-            cols = slice(2 * C * half, 2 * C * (half + 1))
-            nc.sync.dma_start(out=gates[half][:], in_=gate[0:P, cols])
-
         def load_w13(e0, e1):
             for a, words in ((0, w3_words), (1, w1_words)):
                 src = words.bitcast(I32).rearrange("e s p k -> p (e s) k")
                 nc.sync.dma_start(out=as_words(w13[a, e0]), in_=src[:, 2 * e0 : 2 * e1, :])
+
+        def load_gate(half):
+            nc.sync.dma_start(out=gates[half][:], in_=gate[0:P, 2 * C * half : 2 * C * (half + 1)])
 
         load_dy(0)
         nc.sync.dma_start(offsets[:], offs)
@@ -139,28 +128,27 @@ def tile_moe_bdx_glu_sigmoid_kernel(
             nc.gpsimd.memset(windows[kt][:], 0.0)
         for t in range(1, 4):
             load_dy(t)
-        load_saved("a1", PIECES[0])
-        load_w2_scales(0)
-        load_w2(0)
+        load_w2(PIECES[0])
         load_gate(1)
+        load_w2_scales(0)
+        load_saved("a1", PIECES[0])
         load_saved("a3", PIECES[0])
+        load_w2(PIECES[1])
         load_saved("a1", PIECES[1])
+        load_w2(PIECES[2])
+        load_w2_scales(1)
         load_saved("a3", PIECES[1])
         load_saved("a1", PIECES[2])
-        load_w2(1)
         load_saved("a3", PIECES[2])
+        load_w2(PIECES[3])
         load_saved("a1", PIECES[3])
-        load_w2_scales(1)
-        load_w2(2)
-        load_saved("a3", PIECES[3])
-        load_saved("a1", PIECES[4])
-        load_w2(3)
         load_w13_scales(0, w3_scales)
         load_w13_scales(1, w1_scales)
         load_w13(*W13_LOADS[0])
-        load_saved("a3", PIECES[4])
         load_w13(*W13_LOADS[1])
+        load_saved("a3", PIECES[3])
         load_w13(*W13_LOADS[2])
+        load_w13(*W13_LOADS[3])
 
         def gather_times_gate(t, e0, e1):
             j0, j1 = C * e0, C * e1
@@ -173,7 +161,7 @@ def tile_moe_bdx_glu_sigmoid_kernel(
 
         def interleave(e):
             nc.vector.tensor_copy(
-                out=woven_by_pairs(g_bf[:, C * e : C * (e + 1), :]),
+                out=woven_by_pairs(g_bf[0][:, C * e : C * (e + 1), :]),
                 in_=planes_by_pairs(g4[0][:, :, C * e : C * (e + 1)]),
             )
 
@@ -181,7 +169,7 @@ def tile_moe_bdx_glu_sigmoid_kernel(
             cols = slice(C * (e - 2), C * (e - 1))
             gate_by_pairs = gates[1][:, cols].rearrange("p (c i) -> p c i", i=2).unsqueeze(2)
             nc.vector.tensor_tensor(
-                woven_by_pairs(g_bf[:, C * e : C * (e + 1), :]),
+                woven_by_pairs(g_bf[1][:, cols, :]),
                 planes_by_pairs(g4[1][:, :, cols]),
                 gate_by_pairs.to_broadcast([P, C // 2, 4, 2]),
                 MULT,
@@ -192,7 +180,7 @@ def tile_moe_bdx_glu_sigmoid_kernel(
             nc.vector.quantize_mx(
                 out=g_codes[:, cols].bitcast(FP8X4),
                 scales=g_scales[:, cols],
-                in_=g_bf[:, cols, :].rearrange("p j t -> p (j t)"),
+                in_=g_bf[e0 // 2][:, C * (e0 % 2) : C * (e1 - e0 + e0 % 2), :].rearrange("p j t -> p (j t)"),
             )
 
         made = {}
@@ -203,12 +191,15 @@ def tile_moe_bdx_glu_sigmoid_kernel(
                 out=dhT[:],
                 lhsT=g_codes[:, C * e : C * (e + 1)].bitcast(FP8X4),
                 lhsT_scale=g_scales[:, C * e : C * (e + 1)],
-                rhs=(w2[s][:, e, :] if e < 2 else w2[e][:, s, :]).bitcast(FP4X4),
+                rhs=w2[PIECE_OF[e, s]][:, e % 2, :].bitcast(FP4X4),
                 rhs_scale=w2_scale_rows[e // 2][:, e % 2, 512 * s : 512 * (s + 1)],
                 start=True,
                 stop=True,
             )
-            dhT_sb = ring.tile([P, 4, P], F32, name="dhT_sb")
+            if (e, s) == (1, 0):
+                dhT_sb = keep.tile([P, 4, P], F32, name="dhT_second", tag="a1_00")
+            else:
+                dhT_sb = ring.tile([P, 4, P], F32, name="dhT_sb")
             minus_dh = psum.tile([P, 4, P], F32, name="minus_dh", bufs=4)
             width = 2 if (e, s) == (0, 0) else 4
             for t0 in range(0, 4, width):
@@ -226,18 +217,15 @@ def tile_moe_bdx_glu_sigmoid_kernel(
             h = PIECE_OF[e, s].index((e, s))
             return saved[name, PIECE_OF[e, s]][:, :, C * h : C * (h + 1)]
 
-        def sigmoid(piece):
-            sig = keep.tile([P, len(piece) * C, 4], F32, name="sig_%d%d" % piece[0])
-            nc.scalar.activation(woven_by_pairs(sig[:]), planes_by_pairs(saved["a1", piece][:]), SIGMOID)
-            made["sig", piece] = sig
-            for h, (e, s) in enumerate(piece):
-                made["sig", e, s] = sig[:, C * h : C * (h + 1), :]
+        def sigmoid(e, s):
+            sig = keep.tile([P, C, 4], F32, name="sig_%d%d" % (e, s))
+            nc.scalar.activation(woven_by_pairs(sig[:]), planes_by_pairs(saved_slice("a1", e, s)), SIGMOID)
+            made["sig", e, s] = sig[:]
 
-        def sigmoid_planes(piece):
-            sig = keep.tile([P, 4, len(piece) * C], F32, name="sig_%d%d" % piece[0])
-            nc.scalar.activation(sig[:], saved["a1", piece][:], SIGMOID)
-            for h, (e, s) in enumerate(piece):
-                made["sig", e, s] = sig[:, :, C * h : C * (h + 1)]
+        def sigmoid_planes(e, s):
+            sig = keep.tile([P, 4, C], F32, name="sig_%d%d" % (e, s), align_bytes=64)
+            nc.scalar.activation(sig[:], saved_slice("a1", e, s), SIGMOID)
+            made["sig", e, s] = sig[:]
 
         def late_factor(e, s):
             nw = keep.tile([P, 4, C], F32, name="nw_%d%d" % (e, s))
@@ -248,7 +236,10 @@ def tile_moe_bdx_glu_sigmoid_kernel(
             nu = ring.tile([P, 4, C], F32, name="nu", bufs=2)
             nc.vector.tensor_tensor(nu[:], made["minus_dh", e, s][:], made["sig", e, s], MULT)
             made["nu", e, s] = nu
-            made["da", e, s] = ring.tile([P, 2, C, 4], BF16, name="da", align_bytes=64)
+            if e == 0:
+                made["da", e, s] = keep.tile([P, 2, C, 4], BF16, name="da_first", tag="sig_00", align_bytes=64)
+            else:
+                made["da", e, s] = ring.tile([P, 2, C, 4], BF16, name="da", align_bytes=64)
 
         def round_da3(e, s):
             nc.vector.tensor_scalar(
@@ -263,18 +254,12 @@ def tile_moe_bdx_glu_sigmoid_kernel(
                 MULT,
             )
 
-        def square(piece):
-            sq = keep.tile([P, 4, len(piece) * C], F32, name="sq_%d%d" % piece[0])
+        def square(e, s):
+            sq = keep.tile([P, 4, C], F32, name="sq_%d%d" % (e, s))
             nc.scalar.activation(
-                planes_by_pairs(sq[:]), woven_by_pairs(made["sig", piece][:]), SQUARE, bias=one_half[:], scale=-1.0
+                planes_by_pairs(sq[:]), woven_by_pairs(made["sig", e, s]), SQUARE, bias=one_half[:], scale=-1.0
             )
-            for h, (e, s) in enumerate(piece):
-                made["sq", e, s] = sq[:, :, C * h : C * (h + 1)]
-
-        def da1_factor(e, s):
-            nq = keep.tile([P, 4, C], F32, name="nq_%d%d" % (e, s))
-            nc.vector.scalar_tensor_tensor(nq[:], made["sq", e, s], 0.25, saved_slice("a3", e, s), SUBTRACT, MULT)
-            made["nq", e, s] = nq
+            made["sq", e, s] = sq[:]
 
         def product_da3(e, s):
             da = ring.tile([P, 2, C, 4], BF16, name="da", align_bytes=64)
@@ -285,14 +270,6 @@ def tile_moe_bdx_glu_sigmoid_kernel(
                 -1.0,
                 made["sig", e, s],
                 MULT,
-                MULT,
-            )
-
-        def product_da1(e, s):
-            nc.vector.tensor_tensor(
-                woven_by_pairs(made["da", e, s][:, 1, :, :]),
-                planes_by_pairs(made["minus_dh", e, s][:]),
-                planes_by_pairs(made["nq", e, s][:]),
                 MULT,
             )
 
@@ -336,7 +313,7 @@ def tile_moe_bdx_glu_sigmoid_kernel(
             )
 
         def second_product(e):
-            bank = psum.tile([P, 2, C], F32, name="dx_%d" % e, tag="dhT" if e == 2 else "dx")
+            bank = psum.tile([P, 2, C], F32, name="dx_%d" % e, tag="dx")
             for kt in range(2):
                 for s in (1, 0):
                     for a in range(2):
@@ -361,73 +338,61 @@ def tile_moe_bdx_glu_sigmoid_kernel(
         interleave(1)
         quantize_g(1, 2)
         gather_plain(3)
-        sigmoid(PIECES[0])
-        square(PIECES[0])
-        first_product(0, 0)
-        first_product(1, 0)
-        sigmoid(PIECES[1])
-        square(PIECES[1])
-        da1_factor(0, 0)
+        g_bf[1] = keep.tile([P, 2 * C, 4], BF16, name="g_bf1", tag="g4_0", align_bytes=64)
 
-        def prepare(piece):
-            if piece in NO_SQUARE:
-                sigmoid_planes(piece)
-            else:
-                sigmoid(piece)
-            for step in piece:
-                first_product(*step)
-            if piece not in NO_SQUARE:
-                square(piece)
-
-        def products(piece):
-            if piece in NO_SQUARE:
-                kinds = (late_factor, minus_da3, round_da3, late_da1, quantize_da)
-            else:
-                kinds = (product_da3, slope_times_dh, times_a3, quantize_da)
+        def in_turn(kinds, piece):
             for kind in kinds:
                 for step in piece:
                     kind(*step)
 
-        prepare(PIECES[2])
-        product_da3(0, 0)
-        product_da1(0, 0)
-        product_da3(1, 0)
-        quantize_da(0, 0)
-        slope_times_dh(1, 0)
-        interleave_times_gate(2)
-        times_a3(1, 0)
-        interleave_times_gate(3)
-        quantize_da(1, 0)
-        quantize_g(2, 4)
-        prepare(PIECES[3])
-        products(PIECES[2])
-        prepare(PIECES[4])
-        products(PIECES[3])
-        for e in range(2):
+        def finish(e):
             nc.scalar.copy(out=dx_sb[:, :, C * e : C * (e + 1)], in_=second_product(e)[:])
-        scatter_on_scalar(0, 2, 0)
-        scatter_on_scalar(0, 2, 1)
-        nc.scalar.copy(out=dx_sb[:, :, 2 * C : 3 * C], in_=second_product(2)[:])
-        scatter_on_scalar(2, 3, 0)
-        scatter_on_scalar(2, 3, 1)
-        for step in PIECES[4]:
-            product_da3(*step)
-        for step in PIECES[4]:
-            slope_times_dh(*step)
-            quantize_da(*step, 0, 1)
-        for step in PIECES[4]:
-            times_a3(*step)
-        for step in PIECES[4]:
-            quantize_da(*step, 1, 2)
+            scatter_on_scalar(e, e + 1, 0)
+            scatter_on_scalar(e, e + 1, 1)
 
-        banks_3 = [psum.tile([P, C], F32, name="dx3_%d" % kt, tag="dx") for kt in range(2)]
-        for a in range(2):
+        first_product(0, 0)
+        sigmoid_planes(0, 0)
+        sigmoid_planes(1, 0)
+        first_product(1, 0)
+        in_turn((first_product, sigmoid, square), PIECES[1])
+        minus_da3(0, 0)
+        late_factor(0, 0)
+        round_da3(0, 0)
+        late_da1(0, 0)
+        minus_da3(1, 0)
+        quantize_da(0, 0)
+        late_factor(1, 0)
+        round_da3(1, 0)
+        late_da1(1, 0)
+        quantize_da(1, 0, 0, 1)
+        quantize_da(1, 0, 1, 2)
+        interleave_times_gate(2)
+        interleave_times_gate(3)
+        quantize_g(2, 4)
+        for n in (1, 2):
+            in_turn((first_product, sigmoid, square), PIECES[n + 1])
+            in_turn((product_da3, slope_times_dh, times_a3, quantize_da), PIECES[n])
+        finish(0)
+        finish(1)
+
+        in_turn((product_da3, slope_times_dh), PIECES[3])
+        for step in PIECES[3]:
+            quantize_da(*step, 0, 1)
+        in_turn((times_a3,), PIECES[3])
+        for step in PIECES[3]:
+            quantize_da(*step, 1, 2)
+        banks = {}
+        for e, tag in ((2, "dhT"), (3, "dx")):
+            for kt in range(2):
+                banks[e, kt] = psum.tile([P, C], F32, name="dx%d_%d" % (e, kt), tag=tag)
             for s in range(2):
-                for kt in range(2):
-                    second_passes(banks_3[kt][:], 3, kt, s, a, s == 0 and a == 0, s == 1 and a == 1)
-        nc.vector.tensor_copy(out=dx_sb[:, 0, 3 * C : 4 * C], in_=banks_3[0][:])
-        nc.scalar.copy(out=dx_sb[:, 1, 3 * C : 4 * C], in_=banks_3[1][:])
-        scatter_on_vector(3, 0, dx_sb[:, 0, 3 * C : 4 * C])
-        scatter_on_scalar(3, 4, 1)
+                for a in range(2):
+                    for kt in range(2):
+                        second_passes(banks[e, kt][:], e, kt, s, a, s == 0 and a == 0, s == 1 and a == 1)
+            cols = slice(C * e, C * (e + 1))
+            nc.vector.tensor_copy(out=dx_sb[:, 0, cols], in_=banks[e, 0][:])
+            nc.scalar.copy(out=dx_sb[:, 1, cols], in_=banks[e, 1][:])
+            scatter_on_vector(e, 0, dx_sb[:, 0, cols])
+            scatter_on_scalar(e, e + 1, 1)
         nc.sync.dma_start(out=out[0:P, :], in_=windows[0][:])
         nc.sync.dma_start(out=out[P : 2 * P, :], in_=windows[1][:])

@@ -10,6 +10,8 @@ W13_LOADS = ((0, 1), (1, 2), (2, 3), (3, 4))
 W13_FIRST = (0, 1, 2, 3)
 PIECES = tuple(((2 * half, s), (2 * half + 1, s)) for half in range(2) for s in range(2))
 PIECE_OF = {step: piece for piece in PIECES for step in piece}
+SAVED_PIECES = (((0, 0),), ((1, 0),)) + PIECES[1:]
+SAVED_PIECE_OF = {step: piece for piece in SAVED_PIECES for step in piece}
 
 FLOPS = 2 * SLOTS * H * (N + 2 * K)
 BYTES = 4 * (N * T + 2 * H * SLOTS + P * SLOTS + K * T) + 2 * P * SLOTS // 16 + E * (N * H + 2 * H * K) * 17 // 32
@@ -71,7 +73,7 @@ def tile_moe_bdx_glu_sigmoid_kernel(
         one_half = keep.tile([P, 1], F32, name="one_half")
         saved = {}
         for name in ("a1", "a3"):
-            for piece in PIECES:
+            for piece in SAVED_PIECES:
                 saved[name, piece] = keep.tile([P, 4, len(piece) * C], F32, name="%s_%d%d" % ((name,) + piece[0]))
         dx_sb = keep.tile([P, 2, SLOTS], F32, name="dx_sb")
 
@@ -91,7 +93,7 @@ def tile_moe_bdx_glu_sigmoid_kernel(
 
         def load_saved(name, piece):
             e0, s = piece[0]
-            rows = sources[name][512 * s : 512 * (s + 1), C * e0 : C * (e0 + 2)]
+            rows = sources[name][512 * s : 512 * (s + 1), C * e0 : C * (e0 + len(piece))]
             nc.sync.dma_start(out=saved[name, piece][:], in_=rows.rearrange("(p t) j -> p t j", t=4))
 
         def load_w2(piece):
@@ -128,11 +130,13 @@ def tile_moe_bdx_glu_sigmoid_kernel(
             nc.gpsimd.memset(windows[kt][:], 0.0)
         for t in range(1, 4):
             load_dy(t)
+        load_saved("a1", SAVED_PIECES[0])
+        load_w2_scales(0)
         load_w2(PIECES[0])
         load_gate(1)
-        load_w2_scales(0)
-        load_saved("a1", PIECES[0])
-        load_saved("a3", PIECES[0])
+        load_saved("a3", SAVED_PIECES[0])
+        load_saved("a1", SAVED_PIECES[1])
+        load_saved("a3", SAVED_PIECES[1])
         load_w2(PIECES[1])
         load_saved("a1", PIECES[1])
         load_w2(PIECES[2])
@@ -196,10 +200,7 @@ def tile_moe_bdx_glu_sigmoid_kernel(
                 start=True,
                 stop=True,
             )
-            if (e, s) == (1, 0):
-                dhT_sb = keep.tile([P, 4, P], F32, name="dhT_second", tag="a1_00")
-            else:
-                dhT_sb = ring.tile([P, 4, P], F32, name="dhT_sb")
+            dhT_sb = ring.tile([P, 4, P], F32, name="dhT_sb")
             minus_dh = psum.tile([P, 4, P], F32, name="minus_dh", bufs=4)
             width = 2 if (e, s) == (0, 0) else 4
             for t0 in range(0, 4, width):
@@ -214,45 +215,13 @@ def tile_moe_bdx_glu_sigmoid_kernel(
             made["minus_dh", e, s] = minus_dh
 
         def saved_slice(name, e, s):
-            h = PIECE_OF[e, s].index((e, s))
-            return saved[name, PIECE_OF[e, s]][:, :, C * h : C * (h + 1)]
+            h = SAVED_PIECE_OF[e, s].index((e, s))
+            return saved[name, SAVED_PIECE_OF[e, s]][:, :, C * h : C * (h + 1)]
 
         def sigmoid(e, s):
             sig = keep.tile([P, C, 4], F32, name="sig_%d%d" % (e, s))
             nc.scalar.activation(woven_by_pairs(sig[:]), planes_by_pairs(saved_slice("a1", e, s)), SIGMOID)
             made["sig", e, s] = sig[:]
-
-        def sigmoid_planes(e, s):
-            sig = keep.tile([P, 4, C], F32, name="sig_%d%d" % (e, s), align_bytes=64)
-            nc.scalar.activation(sig[:], saved_slice("a1", e, s), SIGMOID)
-            made["sig", e, s] = sig[:]
-
-        def late_factor(e, s):
-            nw = keep.tile([P, 4, C], F32, name="nw_%d%d" % (e, s))
-            nc.vector.scalar_tensor_tensor(nw[:], made["sig", e, s], 1.0, saved_slice("a3", e, s), SUBTRACT, MULT)
-            made["nw", e, s] = nw
-
-        def minus_da3(e, s):
-            nu = ring.tile([P, 4, C], F32, name="nu", bufs=2)
-            nc.vector.tensor_tensor(nu[:], made["minus_dh", e, s][:], made["sig", e, s], MULT)
-            made["nu", e, s] = nu
-            if e == 0:
-                made["da", e, s] = keep.tile([P, 2, C, 4], BF16, name="da_first", tag="sig_00", align_bytes=64)
-            else:
-                made["da", e, s] = ring.tile([P, 2, C, 4], BF16, name="da", align_bytes=64)
-
-        def round_da3(e, s):
-            nc.vector.tensor_scalar(
-                woven_by_pairs(made["da", e, s][:, 0, :, :]), planes_by_pairs(made["nu", e, s][:]), -1.0, None, MULT
-            )
-
-        def late_da1(e, s):
-            nc.vector.tensor_tensor(
-                woven_by_pairs(made["da", e, s][:, 1, :, :]),
-                planes_by_pairs(made["nu", e, s][:]),
-                planes_by_pairs(made["nw", e, s][:]),
-                MULT,
-            )
 
         def square(e, s):
             sq = keep.tile([P, 4, C], F32, name="sq_%d%d" % (e, s))
@@ -270,6 +239,19 @@ def tile_moe_bdx_glu_sigmoid_kernel(
                 -1.0,
                 made["sig", e, s],
                 MULT,
+                MULT,
+            )
+
+        def da1_factor(e, s):
+            nq = keep.tile([P, 4, C], F32, name="nq_%d%d" % (e, s))
+            nc.vector.scalar_tensor_tensor(nq[:], made["sq", e, s], 0.25, saved_slice("a3", e, s), SUBTRACT, MULT)
+            made["nq", e, s] = nq
+
+        def product_da1(e, s):
+            nc.vector.tensor_tensor(
+                woven_by_pairs(made["da", e, s][:, 1, :, :]),
+                planes_by_pairs(made["minus_dh", e, s][:]),
+                planes_by_pairs(made["nq", e, s][:]),
                 MULT,
             )
 
@@ -350,28 +332,28 @@ def tile_moe_bdx_glu_sigmoid_kernel(
             scatter_on_scalar(e, e + 1, 0)
             scatter_on_scalar(e, e + 1, 1)
 
+        sigmoid(0, 0)
+        square(0, 0)
         first_product(0, 0)
-        sigmoid_planes(0, 0)
-        sigmoid_planes(1, 0)
         first_product(1, 0)
+        sigmoid(1, 0)
+        square(1, 0)
+        da1_factor(0, 0)
         in_turn((first_product, sigmoid, square), PIECES[1])
-        minus_da3(0, 0)
-        late_factor(0, 0)
-        round_da3(0, 0)
-        late_da1(0, 0)
-        minus_da3(1, 0)
+        product_da3(0, 0)
+        product_da1(0, 0)
+        product_da3(1, 0)
         quantize_da(0, 0)
-        late_factor(1, 0)
-        round_da3(1, 0)
-        late_da1(1, 0)
-        quantize_da(1, 0, 0, 1)
-        quantize_da(1, 0, 1, 2)
+        slope_times_dh(1, 0)
         interleave_times_gate(2)
+        times_a3(1, 0)
         interleave_times_gate(3)
+        quantize_da(1, 0)
         quantize_g(2, 4)
-        for n in (1, 2):
-            in_turn((first_product, sigmoid, square), PIECES[n + 1])
-            in_turn((product_da3, slope_times_dh, times_a3, quantize_da), PIECES[n])
+        in_turn((first_product, sigmoid, square), PIECES[2])
+        in_turn((product_da3, slope_times_dh, times_a3, quantize_da), PIECES[1])
+        in_turn((first_product, sigmoid, square), PIECES[3])
+        in_turn((product_da3, slope_times_dh, times_a3, quantize_da), PIECES[2])
         finish(0)
         finish(1)
 

@@ -224,6 +224,11 @@ def tile_moe_bdx_glu_sigmoid_kernel(
             made["sig", e, s] = sig[:]
 
         def square(e, s):
+            sq = keep.tile([P, C, 4], F32, name="sq_%d%d" % (e, s))
+            nc.scalar.activation(sq[:], made["sig", e, s], SQUARE, bias=one_half[:], scale=-1.0)
+            made["sq", e, s] = sq[:]
+
+        def square_as_planes(e, s):
             sq = keep.tile([P, 4, C], F32, name="sq_%d%d" % (e, s))
             nc.scalar.activation(
                 planes_by_pairs(sq[:]), woven_by_pairs(made["sig", e, s]), SQUARE, bias=one_half[:], scale=-1.0
@@ -256,14 +261,16 @@ def tile_moe_bdx_glu_sigmoid_kernel(
             )
 
         def slope_times_dh(e, s):
-            y = ring.tile([P, 4, C], F32, name="y")
-            nc.vector.scalar_tensor_tensor(y[:], made["sq", e, s], 0.25, made["minus_dh", e, s][:], SUBTRACT, MULT)
+            y = ring.tile([P, C, 4], F32, name="y")
+            nc.vector.scalar_tensor_tensor(
+                y[:], made["sq", e, s], 0.25, made["minus_dh", e, s][:].rearrange("p t j -> p j t"), SUBTRACT, MULT
+            )
             made["y", e, s] = y
 
         def times_a3(e, s):
             nc.vector.tensor_tensor(
                 woven_by_pairs(made["da", e, s][:, 1, :, :]),
-                planes_by_pairs(made["y", e, s][:]),
+                woven_by_pairs(made["y", e, s][:]),
                 planes_by_pairs(saved_slice("a3", e, s)),
                 MULT,
             )
@@ -333,7 +340,7 @@ def tile_moe_bdx_glu_sigmoid_kernel(
             scatter_on_scalar(e, e + 1, 1)
 
         sigmoid(0, 0)
-        square(0, 0)
+        square_as_planes(0, 0)
         first_product(0, 0)
         first_product(1, 0)
         sigmoid(1, 0)

@@ -9,9 +9,9 @@ P = 128
 W13_LOADS = ((0, 1), (1, 2), (2, 3), (3, 4))
 W13_FIRST = (0, 1, 2, 3)
 PIECES = tuple(((2 * half, s), (2 * half + 1, s)) for half in range(2) for s in range(2))
-PIECE_OF = {step: piece for piece in PIECES for step in piece}
 SAVED_PIECES = (((0, 0),), ((1, 0),)) + PIECES[1:]
-SAVED_PIECE_OF = {step: piece for piece in SAVED_PIECES for step in piece}
+A3_PIECES = SAVED_PIECES[:3] + (((2, 0), (2, 1)), ((3, 0), (3, 1)))
+LOADED_IN = {"a1": SAVED_PIECES, "a3": A3_PIECES}
 
 FLOPS = 2 * SLOTS * H * (N + 2 * K)
 BYTES = 4 * (N * T + 2 * H * SLOTS + P * SLOTS + K * T) + 2 * P * SLOTS // 16 + E * (N * H + 2 * H * K) * 17 // 32
@@ -73,7 +73,7 @@ def tile_moe_bdx_glu_sigmoid_kernel(
         one_half = keep.tile([P, 1], F32, name="one_half")
         saved = {}
         for name in ("a1", "a3"):
-            for piece in SAVED_PIECES:
+            for piece in LOADED_IN[name]:
                 saved[name, piece] = keep.tile([P, 4, len(piece) * C], F32, name="%s_%d%d" % ((name,) + piece[0]))
         dx_sb = keep.tile([P, 2, SLOTS], F32, name="dx_sb")
 
@@ -92,9 +92,12 @@ def tile_moe_bdx_glu_sigmoid_kernel(
             nc.sync.dma_start(out=dy[t][:], in_=dy_rows[:, t, :])
 
         def load_saved(name, piece):
-            e0, s = piece[0]
-            rows = sources[name][512 * s : 512 * (s + 1), C * e0 : C * (e0 + len(piece))]
-            nc.sync.dma_start(out=saved[name, piece][:], in_=rows.rearrange("(p t) j -> p t j", t=4))
+            (e0, s0), (e1, s1) = piece[0], piece[-1]
+            rows = sources[name][512 * s0 : 512 * (s1 + 1), C * e0 : C * (e1 + 1)]
+            nc.sync.dma_start(
+                out=saved[name, piece][:].rearrange("p t (s j) -> p t s j", s=s1 - s0 + 1),
+                in_=rows.rearrange("(s p t) j -> p t s j", p=P, t=4),
+            )
 
         def load_w2(piece):
             e0, s = piece[0]
@@ -134,23 +137,23 @@ def tile_moe_bdx_glu_sigmoid_kernel(
         load_w2_scales(0)
         load_w2(PIECES[0])
         load_gate(1)
-        load_saved("a3", SAVED_PIECES[0])
+        load_saved("a3", A3_PIECES[0])
         load_saved("a1", SAVED_PIECES[1])
-        load_saved("a3", SAVED_PIECES[1])
         load_w2(PIECES[1])
+        load_saved("a3", A3_PIECES[1])
         load_saved("a1", PIECES[1])
         load_w2(PIECES[2])
         load_w2_scales(1)
         load_saved("a3", PIECES[1])
         load_saved("a1", PIECES[2])
-        load_saved("a3", PIECES[2])
         load_w2(PIECES[3])
-        load_saved("a1", PIECES[3])
         load_w13_scales(0, w3_scales)
+        load_saved("a1", PIECES[3])
         load_w13_scales(1, w1_scales)
         load_w13(*W13_LOADS[0])
+        load_saved("a3", A3_PIECES[3])
         load_w13(*W13_LOADS[1])
-        load_saved("a3", PIECES[3])
+        load_saved("a3", A3_PIECES[4])
         load_w13(*W13_LOADS[2])
         load_w13(*W13_LOADS[3])
 
@@ -195,7 +198,7 @@ def tile_moe_bdx_glu_sigmoid_kernel(
                 out=dhT[:],
                 lhsT=g_codes[:, C * e : C * (e + 1)].bitcast(FP8X4),
                 lhsT_scale=g_scales[:, C * e : C * (e + 1)],
-                rhs=w2[PIECE_OF[e, s]][:, e % 2, :].bitcast(FP4X4),
+                rhs=w2[PIECES[2 * (e // 2) + s]][:, e % 2, :].bitcast(FP4X4),
                 rhs_scale=w2_scale_rows[e // 2][:, e % 2, 512 * s : 512 * (s + 1)],
                 start=True,
                 stop=True,
@@ -215,8 +218,9 @@ def tile_moe_bdx_glu_sigmoid_kernel(
             made["minus_dh", e, s] = minus_dh
 
         def saved_slice(name, e, s):
-            h = SAVED_PIECE_OF[e, s].index((e, s))
-            return saved[name, SAVED_PIECE_OF[e, s]][:, :, C * h : C * (h + 1)]
+            piece = [piece for piece in LOADED_IN[name] if (e, s) in piece][0]
+            h = piece.index((e, s))
+            return saved[name, piece][:, :, C * h : C * (h + 1)]
 
         def sigmoid(e, s):
             sig = keep.tile([P, C, 4], F32, name="sig_%d%d" % (e, s))
@@ -236,7 +240,7 @@ def tile_moe_bdx_glu_sigmoid_kernel(
             made["sq", e, s] = sq[:]
 
         def product_da3(e, s):
-            da = ring.tile([P, 2, C, 4], BF16, name="da", align_bytes=64)
+            da = ring.tile([P, 2, C, 4], BF16, name="da", bufs=4, align_bytes=64)
             made["da", e, s] = da
             nc.vector.scalar_tensor_tensor(
                 da[:, 0, :, :],
@@ -261,7 +265,7 @@ def tile_moe_bdx_glu_sigmoid_kernel(
             )
 
         def slope_times_dh(e, s):
-            y = ring.tile([P, C, 4], F32, name="y")
+            y = ring.tile([P, C, 4], F32, name="y", bufs=4)
             nc.vector.scalar_tensor_tensor(
                 y[:], made["sq", e, s], 0.25, made["minus_dh", e, s][:].rearrange("p t j -> p j t"), SUBTRACT, MULT
             )
@@ -335,9 +339,11 @@ def tile_moe_bdx_glu_sigmoid_kernel(
                     kind(*step)
 
         def finish(e):
-            nc.scalar.copy(out=dx_sb[:, :, C * e : C * (e + 1)], in_=second_product(e)[:])
-            scatter_on_scalar(e, e + 1, 0)
-            scatter_on_scalar(e, e + 1, 1)
+            bank = second_product(e)
+            for kt in range(2):
+                nc.scalar.copy(out=dx_sb[:, kt, C * e : C * (e + 1)], in_=bank[:, kt, :])
+            for kt in range(2):
+                scatter_on_scalar(e, e + 1, kt)
 
         sigmoid(0, 0)
         square_as_planes(0, 0)
@@ -360,28 +366,35 @@ def tile_moe_bdx_glu_sigmoid_kernel(
         in_turn((first_product, sigmoid, square), PIECES[2])
         in_turn((product_da3, slope_times_dh, times_a3, quantize_da), PIECES[1])
         in_turn((first_product, sigmoid, square), PIECES[3])
-        in_turn((product_da3, slope_times_dh, times_a3, quantize_da), PIECES[2])
+        in_turn((product_da3, slope_times_dh), PIECES[2])
+        in_turn((product_da3, slope_times_dh), PIECES[3])
         finish(0)
         finish(1)
+        in_turn((times_a3, quantize_da), A3_PIECES[3])
+        banks_2 = [psum.tile([P, C], F32, name="dx2_%d" % kt, tag="minus_dh", bufs=4) for kt in range(2)]
+        for kt in range(2):
+            for a in range(2):
+                for s in range(2):
+                    second_passes(banks_2[kt][:], 2, kt, s, a, s == 0 and a == 0, s == 1 and a == 1)
+        nc.scalar.copy(out=dx_sb[:, 1, 2 * C : 3 * C], in_=banks_2[1][:])
+        scatter_on_scalar(2, 3, 1)
 
-        in_turn((product_da3, slope_times_dh), PIECES[3])
-        for step in PIECES[3]:
+        for step in A3_PIECES[4]:
             quantize_da(*step, 0, 1)
-        in_turn((times_a3,), PIECES[3])
-        for step in PIECES[3]:
+        in_turn((times_a3,), A3_PIECES[4])
+        for step in A3_PIECES[4]:
             quantize_da(*step, 1, 2)
-        banks = {}
-        for e, tag in ((2, "dhT"), (3, "dx")):
-            for kt in range(2):
-                banks[e, kt] = psum.tile([P, C], F32, name="dx%d_%d" % (e, kt), tag=tag)
+        banks = [psum.tile([P, C], F32, name="dx3_%d" % kt, tag="dhT") for kt in range(2)]
+        for a in range(2):
             for s in range(2):
-                for a in range(2):
-                    for kt in range(2):
-                        second_passes(banks[e, kt][:], e, kt, s, a, s == 0 and a == 0, s == 1 and a == 1)
-            cols = slice(C * e, C * (e + 1))
-            nc.vector.tensor_copy(out=dx_sb[:, 0, cols], in_=banks[e, 0][:])
-            nc.scalar.copy(out=dx_sb[:, 1, cols], in_=banks[e, 1][:])
-            scatter_on_vector(e, 0, dx_sb[:, 0, cols])
-            scatter_on_scalar(e, e + 1, 1)
+                for kt in range(2):
+                    second_passes(banks[kt][:], 3, kt, s, a, s == 0 and a == 0, s == 1 and a == 1)
+        cols = slice(3 * C, 4 * C)
+        nc.vector.tensor_copy(out=dx_sb[:, 0, 2 * C : 3 * C], in_=banks_2[0][:])
+        scatter_on_vector(2, 0, dx_sb[:, 0, 2 * C : 3 * C])
+        nc.vector.tensor_copy(out=dx_sb[:, 0, cols], in_=banks[0][:])
+        nc.scalar.copy(out=dx_sb[:, 1, cols], in_=banks[1][:])
+        scatter_on_vector(3, 0, dx_sb[:, 0, cols])
+        scatter_on_scalar(3, 4, 1)
         nc.sync.dma_start(out=out[0:P, :], in_=windows[0][:])
-        nc.sync.dma_start(out=out[P : 2 * P, :], in_=windows[1][:])
+        nc.scalar.dma_start(out=out[P : 2 * P, :], in_=windows[1][:])

@@ -306,12 +306,12 @@ def tile_moe_bdx_glu_sigmoid_kernel(
             )
 
         def second_product(e):
-            bank = psum.tile([P, 2, C], F32, name="dx_%d" % e, tag="dx")
-            for kt in range(2):
-                for s in (1, 0):
-                    for a in range(2):
-                        second_passes(bank[:, kt, :], e, kt, s, a, s == 1 and a == 0, s == 0 and a == 1)
-            return bank
+            banks = [psum.tile([P, C], F32, name="dx_%d%d" % (e, kt), tag="dx") for kt in range(2)]
+            for a in range(2):
+                for kt in range(2):
+                    for s in range(2):
+                        second_passes(banks[kt][:], e, kt, s, a, s == 0 and a == 0, s == 1 and a == 1)
+            return banks
 
         def scatter_on_vector(e, kt, values):
             nc.vector.tensor_copy(windows[kt][:].indirect(offsets[:, 8 * e : 8 * (e + 1)]), values)
@@ -339,9 +339,9 @@ def tile_moe_bdx_glu_sigmoid_kernel(
                     kind(*step)
 
         def finish(e):
-            bank = second_product(e)
+            banks = second_product(e)
             for kt in range(2):
-                nc.scalar.copy(out=dx_sb[:, kt, C * e : C * (e + 1)], in_=bank[:, kt, :])
+                nc.scalar.copy(out=dx_sb[:, kt, C * e : C * (e + 1)], in_=banks[kt][:])
             for kt in range(2):
                 scatter_on_scalar(e, e + 1, kt)
 
@@ -370,13 +370,18 @@ def tile_moe_bdx_glu_sigmoid_kernel(
         in_turn((product_da3, slope_times_dh), PIECES[3])
         finish(0)
         finish(1)
-        in_turn((times_a3, quantize_da), A3_PIECES[3])
+        for step in A3_PIECES[3]:
+            quantize_da(*step, 0, 1)
+        in_turn((times_a3,), A3_PIECES[3])
+        for step in A3_PIECES[3]:
+            quantize_da(*step, 1, 2)
         banks_2 = [psum.tile([P, C], F32, name="dx2_%d" % kt, tag="minus_dh", bufs=4) for kt in range(2)]
         for kt in range(2):
             for a in range(2):
                 for s in range(2):
                     second_passes(banks_2[kt][:], 2, kt, s, a, s == 0 and a == 0, s == 1 and a == 1)
-        nc.scalar.copy(out=dx_sb[:, 1, 2 * C : 3 * C], in_=banks_2[1][:])
+        for kt in (1, 0):
+            nc.scalar.copy(out=dx_sb[:, kt, 2 * C : 3 * C], in_=banks_2[kt][:])
         scatter_on_scalar(2, 3, 1)
 
         for step in A3_PIECES[4]:
@@ -390,7 +395,6 @@ def tile_moe_bdx_glu_sigmoid_kernel(
                 for kt in range(2):
                     second_passes(banks[kt][:], 3, kt, s, a, s == 0 and a == 0, s == 1 and a == 1)
         cols = slice(3 * C, 4 * C)
-        nc.vector.tensor_copy(out=dx_sb[:, 0, 2 * C : 3 * C], in_=banks_2[0][:])
         scatter_on_vector(2, 0, dx_sb[:, 0, 2 * C : 3 * C])
         nc.vector.tensor_copy(out=dx_sb[:, 0, cols], in_=banks[0][:])
         nc.scalar.copy(out=dx_sb[:, 1, cols], in_=banks[1][:])

@@ -342,8 +342,9 @@ def tile_moe_bdx_glu_sigmoid_kernel(
             banks = second_product(e)
             for kt in range(2):
                 nc.scalar.copy(out=dx_sb[:, kt, C * e : C * (e + 1)], in_=banks[kt][:])
-            for kt in range(2):
-                scatter_on_scalar(e, e + 1, kt)
+            if e == 0:
+                scatter_on_scalar(e, e + 1, 0)
+            scatter_on_scalar(e, e + 1, 1)
 
         sigmoid(0, 0)
         square_as_planes(0, 0)
@@ -380,6 +381,7 @@ def tile_moe_bdx_glu_sigmoid_kernel(
             for a in range(2):
                 for s in range(2):
                     second_passes(banks_2[kt][:], 2, kt, s, a, s == 0 and a == 0, s == 1 and a == 1)
+        scatter_on_vector(1, 0, dx_sb[:, 0, C : 2 * C])
         for kt in (1, 0):
             nc.scalar.copy(out=dx_sb[:, kt, 2 * C : 3 * C], in_=banks_2[kt][:])
         scatter_on_scalar(2, 3, 1)

@@ -1,17 +1,11 @@
 from contextlib import ExitStack
 
 import concourse.mybir as mybir
-from concourse.masks import make_identity
 
 N, T, E, C, H, K = 512, 768, 4, 128, 1024, 256
 SLOTS = E * C
 P = 128
-W13_LOADS = ((0, 1), (1, 2), (2, 3), (3, 4))
-W13_FIRST = (0, 1, 2, 3)
-PIECES = tuple(((2 * half, s), (2 * half + 1, s)) for half in range(2) for s in range(2))
-SAVED_PIECES = (((0, 0),), ((1, 0),)) + PIECES[1:]
-A3_PIECES = SAVED_PIECES[:3] + (((2, 0), (2, 1)), ((3, 0), (3, 1)))
-LOADED_IN = {"a1": SAVED_PIECES, "a3": A3_PIECES}
+SORTED_ON_SCALAR = (1, 2)
 
 FLOPS = 2 * SLOTS * H * (N + 2 * K)
 BYTES = 4 * (N * T + 2 * H * SLOTS + P * SLOTS + K * T) + 2 * P * SLOTS // 16 + E * (N * H + 2 * H * K) * 17 // 32
@@ -49,113 +43,114 @@ def tile_moe_bdx_glu_sigmoid_kernel(
     nc = tc.nc
     with ExitStack() as ctx:
         keep = ctx.enter_context(tc.tile_pool(name="keep", bufs=1))
-        ring = ctx.enter_context(tc.tile_pool(name="ring", bufs=3))
-        psum = ctx.enter_context(tc.psum_pool(name="psum", bufs=2))
+        psum = ctx.enter_context(tc.psum_pool(name="psum", bufs=4))
 
         offsets = keep.tile([P, SLOTS // 16], U16, name="offsets")
         dy = [keep.tile([P, T], F32, name="dy%d" % t) for t in range(4)]
         gates = [keep.tile([P, 2 * C], F32, name="gates%d" % half) for half in range(2)]
         g4 = [keep.tile([P, 4, 2 * C], F32, name="g4_%d" % half, align_bytes=64) for half in range(2)]
-        g_bf = {0: keep.tile([P, 2 * C, 4], BF16, name="g_bf0", align_bytes=64)}
+        g_bf = [keep.tile([P, 2 * C, 4], BF16, name="g_bf%d" % half, align_bytes=64) for half in range(2)]
         g_codes = keep.tile([P, SLOTS], U32, name="g_codes", align_bytes=64)
         g_scales = keep.tile([P, SLOTS], U8, name="g_scales", align_bytes=64)
-        w2 = {piece: keep.tile([P, 2, H], U8, name="w2_%d%d" % piece[0], align_bytes=64) for piece in PIECES}
-        w2_scale_rows = [keep.tile([P, 2, H], U8, name="w2_scale_rows%d" % half, align_bytes=64) for half in range(2)]
+        w2_raw = {}
+        w2 = [keep.tile([P, 2 * H], U8, name="w2_%d" % e, align_bytes=64) for e in range(E)]
+        staged = keep.tile([P, 512], U8, name="staged")
+        staged_sorted = keep.tile([P, 512], U8, name="staged_sorted")
+        w2_scale_rows = keep.tile([P, 2 * E, 512], U8, name="w2_scale_rows", align_bytes=64)
         w13 = {
-            (a, e0): keep.tile([P, 2 * (e1 - e0), 2 * K], U8, name="w13_%d%d" % (a, e0), align_bytes=64)
+            (a, e): keep.tile([P, 2, 2 * K], U8, name="w13_%d%d" % (a, e), align_bytes=64)
             for a in range(2)
-            for e0, e1 in W13_LOADS
+            for e in range(E)
         }
-        w13_scale_rows = keep.tile([P, 2, 2 * E, K], U8, name="w13_scale_rows", align_bytes=64)
-        ident = keep.tile([P, P], F32, name="ident")
+        w13_scale_rows = [
+            keep.tile([P, 2 * E, K], U8, name="w13_scale_rows%d" % a, align_bytes=64) for a in range(2)
+        ]
         windows = [keep.tile([P, T], F32, name="window%d" % kt) for kt in range(2)]
         zero = keep.tile([P, 1], F32, name="zero")
         one_half = keep.tile([P, 1], F32, name="one_half")
+        dx_sb = keep.tile([P, E, 2, C], F32, name="dx_sb")
         saved = {}
-        for name in ("a1", "a3"):
-            for piece in LOADED_IN[name]:
-                saved[name, piece] = keep.tile([P, 4, len(piece) * C], F32, name="%s_%d%d" % ((name,) + piece[0]))
-        dx_sb = keep.tile([P, 2, SLOTS], F32, name="dx_sb")
 
         sources = {"a1": a1, "a3": a3}
         dy_rows = dyT.rearrange("(p t) j -> p t j", t=4)
-        w2_src = w2_words.bitcast(I32).rearrange("e s p i -> p (e s) i")
-        w2_scale_src = w2_scales.bitcast(I32).rearrange("e s f i -> f (e s) i")
-        w13_scale_dst = (
-            w13_scale_rows[:]
-            .rearrange("p a g k -> p (a g k)")
-            .bitcast(I32)
-            .rearrange("p (a g k) -> p a g k", a=2, g=2 * E)
-        )
 
         def load_dy(t):
             nc.sync.dma_start(out=dy[t][:], in_=dy_rows[:, t, :])
 
-        def load_saved(name, piece):
-            (e0, s0), (e1, s1) = piece[0], piece[-1]
-            rows = sources[name][512 * s0 : 512 * (s1 + 1), C * e0 : C * (e1 + 1)]
+        def load_saved(name, e, s0=0, s1=2):
+            tile = keep.tile([P, 4, (s1 - s0) * C], F32, name="%s_%d%d" % (name, e, s0))
+            rows = sources[name][512 * s0 : 512 * s1, C * e : C * (e + 1)]
             nc.sync.dma_start(
-                out=saved[name, piece][:].rearrange("p t (s j) -> p t s j", s=s1 - s0 + 1),
+                out=tile[:].rearrange("p t (s j) -> p t s j", s=s1 - s0),
                 in_=rows.rearrange("(s p t) j -> p t s j", p=P, t=4),
             )
+            saved[name, e, s0, s1] = tile[:]
+            for s in range(s0, s1):
+                saved[name, e, s] = tile[:, :, C * (s - s0) : C * (s - s0 + 1)]
 
-        def load_w2(piece):
-            e0, s = piece[0]
-            nc.sync.dma_start(out=as_words(w2[piece]), in_=w2_src[:, e0 : e0 + 2, 256 * s : 256 * (s + 1)])
+        def load_w2(e0, e1):
+            raw = keep.tile([P, (e1 - e0) * 2 * H], U8, name="w2_raw%d" % e0)
+            nc.sync.dma_start(
+                out=raw[:].bitcast(I32).rearrange("p (e i) -> p e i", e=e1 - e0),
+                in_=w2_words.bitcast(I32)[e0:e1].rearrange("e o p i -> p (e o) i"),
+            )
+            for e in range(e0, e1):
+                w2_raw[e] = raw[:, 2 * H * (e - e0) : 2 * H * (e - e0 + 1)]
 
-        def load_w2_scales(half):
-            for r in range(4):
-                nc.sync.dma_start(
-                    out=as_words(w2_scale_rows[half])[r:P:32, :, :],
-                    in_=w2_scale_src[r:16:4, 2 * half : 2 * half + 2, :],
-                )
+        def load_w13_scales(a, r0):
+            scale_src = (w3_scales, w1_scales)[a].bitcast(I32).rearrange("e s f k -> f (e s) k")
+            for r in (r0, r0 + 1):
+                nc.sync.dma_start(out=as_words(w13_scale_rows[a])[r:P:32, :, :], in_=scale_src[r:16:4, :, :])
 
-        def load_w13_scales(a, scales):
-            scale_src = scales.bitcast(I32).rearrange("e s f k -> f (e s) k")
-            for r in range(4):
-                nc.sync.dma_start(out=w13_scale_dst[r:P:32, a, :, :], in_=scale_src[r:16:4, :, :])
-
-        def load_w13(e0, e1):
+        def load_w13(e):
             for a, words in ((0, w3_words), (1, w1_words)):
-                src = words.bitcast(I32).rearrange("e s p k -> p (e s) k")
-                nc.sync.dma_start(out=as_words(w13[a, e0]), in_=src[:, 2 * e0 : 2 * e1, :])
+                nc.sync.dma_start(out=as_words(w13[a, e]), in_=words.bitcast(I32)[e].rearrange("s p k -> p s k"))
 
         def load_gate(half):
             nc.sync.dma_start(out=gates[half][:], in_=gate[0:P, 2 * C * half : 2 * C * (half + 1)])
 
+        staged_src = w2_scales.bitcast(I32).rearrange("e o f (s i) -> s f (e o) i", s=2)
+        for s in range(2):
+            nc.sync.dma_start(out=staged[:].bitcast(I32)[s:P:2, :], in_=staged_src[s])
         load_dy(0)
         nc.sync.dma_start(offsets[:], offs)
         load_gate(0)
         nc.vector.memset(zero[:], 0.0)
         nc.scalar.activation(one_half[:], zero[:], SIGMOID)
-        make_identity(nc, ident[:])
         for kt in range(2):
             nc.gpsimd.memset(windows[kt][:], 0.0)
-        for t in range(1, 4):
-            load_dy(t)
-        load_saved("a1", SAVED_PIECES[0])
-        load_w2_scales(0)
-        load_w2(PIECES[0])
+        nc.vector.tensor_copy(
+            out=staged_sorted[:].rearrange("p (t m) -> p t m", t=4), in_=staged[:].rearrange("p (m t) -> p t m", t=4)
+        )
+        load_dy(1)
+        load_dy(2)
+        load_dy(3)
+        load_w2(0, 1)
+        for quadrant in (0, 2, 1, 3):
+            p0 = 32 * quadrant
+            nc.sync.dma_start(
+                out=as_words(w2_scale_rows)[p0 : p0 + 4, :, :], in_=staged_sorted[p0 : p0 + 32, :].bitcast(I32)
+            )
+        load_saved("a1", 0, 0, 1)
         load_gate(1)
-        load_saved("a3", A3_PIECES[0])
-        load_saved("a1", SAVED_PIECES[1])
-        load_w2(PIECES[1])
-        load_saved("a3", A3_PIECES[1])
-        load_saved("a1", PIECES[1])
-        load_w2(PIECES[2])
-        load_w2_scales(1)
-        load_saved("a3", PIECES[1])
-        load_saved("a1", PIECES[2])
-        load_w2(PIECES[3])
-        load_w13_scales(0, w3_scales)
-        load_saved("a1", PIECES[3])
-        load_w13_scales(1, w1_scales)
-        load_w13(*W13_LOADS[0])
-        load_saved("a3", A3_PIECES[3])
-        load_w13(*W13_LOADS[1])
-        load_saved("a3", A3_PIECES[4])
-        load_w13(*W13_LOADS[2])
-        load_w13(*W13_LOADS[3])
+        load_saved("a1", 0, 1, 2)
+        load_saved("a3", 0)
+        load_w2(1, 2)
+        load_saved("a1", 1)
+        load_w13_scales(0, 0)
+        load_saved("a3", 1)
+        load_w2(2, 4)
+        load_saved("a1", 2)
+        load_w13_scales(0, 2)
+        load_saved("a1", 3)
+        load_w13_scales(1, 0)
+        load_saved("a3", 2)
+        load_w13_scales(1, 2)
+        load_w13(0)
+        load_w13(1)
+        load_saved("a3", 3)
+        load_w13(2)
+        load_w13(3)
 
         def gather_times_gate(t, e0, e1):
             j0, j1 = C * e0, C * e1
@@ -166,13 +161,13 @@ def tile_moe_bdx_glu_sigmoid_kernel(
         def gather_plain(t):
             nc.scalar.activation(g4[1][:, t, :], dy[t][:].indirect(offsets[:, 16:32]), COPY)
 
-        def interleave(e):
+        def weave(e):
             nc.vector.tensor_copy(
                 out=woven_by_pairs(g_bf[0][:, C * e : C * (e + 1), :]),
                 in_=planes_by_pairs(g4[0][:, :, C * e : C * (e + 1)]),
             )
 
-        def interleave_times_gate(e):
+        def weave_times_gate(e):
             cols = slice(C * (e - 2), C * (e - 1))
             gate_by_pairs = gates[1][:, cols].rearrange("p (c i) -> p c i", i=2).unsqueeze(2)
             nc.vector.tensor_tensor(
@@ -190,217 +185,159 @@ def tile_moe_bdx_glu_sigmoid_kernel(
                 in_=g_bf[e0 // 2][:, C * (e0 % 2) : C * (e1 - e0 + e0 % 2), :].rearrange("p j t -> p (j t)"),
             )
 
+        def sort_w2(e):
+            move = nc.scalar.copy if e in SORTED_ON_SCALAR else nc.vector.tensor_copy
+            move(
+                out=w2[e][:].bitcast(U16).rearrange("p (s t m) -> p s t m", s=2, t=4),
+                in_=w2_raw[e].bitcast(U16).rearrange("p (s m t) -> p s t m", s=2, t=4),
+            )
+
         made = {}
 
         def first_product(e, s):
-            dhT = psum.tile([P, 512], F32, name="dhT")
-            nc.tensor.matmul_mx(
-                out=dhT[:],
-                lhsT=g_codes[:, C * e : C * (e + 1)].bitcast(FP8X4),
-                lhsT_scale=g_scales[:, C * e : C * (e + 1)],
-                rhs=w2[PIECES[2 * (e // 2) + s]][:, e % 2, :].bitcast(FP4X4),
-                rhs_scale=w2_scale_rows[e // 2][:, e % 2, 512 * s : 512 * (s + 1)],
-                start=True,
-                stop=True,
-            )
-            dhT_sb = ring.tile([P, 4, P], F32, name="dhT_sb")
-            minus_dh = psum.tile([P, 4, P], F32, name="minus_dh", bufs=4)
-            width = 2 if (e, s) == (0, 0) else 4
-            for t0 in range(0, 4, width):
-                nc.scalar.activation(
-                    dhT_sb[:, t0 : t0 + width, :],
-                    dhT[:].rearrange("j (m t) -> j t m", t=4)[:, t0 : t0 + width, :],
-                    COPY,
-                    scale=-1.0,
+            dh = psum.tile([P, 4, C], F32, name="dh")
+            for t in range(4):
+                nc.tensor.matmul_mx(
+                    out=dh[:, t, :],
+                    lhsT=w2[e][:, H * s + 256 * t : H * s + 256 * (t + 1)].bitcast(FP4X4),
+                    lhsT_scale=w2_scale_rows[:, 2 * e + s, P * t : P * (t + 1)],
+                    rhs=g_codes[:, C * e : C * (e + 1)].bitcast(FP8X4),
+                    rhs_scale=g_scales[:, C * e : C * (e + 1)],
+                    start=True,
+                    stop=True,
                 )
-                for t in range(t0, t0 + width):
-                    nc.tensor.transpose(minus_dh[:, t, :], dhT_sb[:, t, :], ident[:])
-            made["minus_dh", e, s] = minus_dh
+            made["dh", e, s] = dh[:].rearrange("p t j -> p j t")
 
-        def saved_slice(name, e, s):
-            piece = [piece for piece in LOADED_IN[name] if (e, s) in piece][0]
-            h = piece.index((e, s))
-            return saved[name, piece][:, :, C * h : C * (h + 1)]
+        def sigmoid(e, s0, s1):
+            sig = keep.tile([P, (s1 - s0) * C, 4], F32, name="sig_%d%d" % (e, s0))
+            nc.scalar.activation(woven_by_pairs(sig[:]), planes_by_pairs(saved["a1", e, s0, s1]), SIGMOID)
+            made["sig", e, s0, s1] = sig
+            for s in range(s0, s1):
+                made["sig", e, s] = sig[:, C * (s - s0) : C * (s - s0 + 1), :]
 
-        def sigmoid(e, s):
-            sig = keep.tile([P, C, 4], F32, name="sig_%d%d" % (e, s))
-            nc.scalar.activation(woven_by_pairs(sig[:]), planes_by_pairs(saved_slice("a1", e, s)), SIGMOID)
-            made["sig", e, s] = sig[:]
-
-        def square(e, s):
-            sq = keep.tile([P, C, 4], F32, name="sq_%d%d" % (e, s))
-            nc.scalar.activation(sq[:], made["sig", e, s], SQUARE, bias=one_half[:], scale=-1.0)
-            made["sq", e, s] = sq[:]
-
-        def square_as_planes(e, s):
-            sq = keep.tile([P, 4, C], F32, name="sq_%d%d" % (e, s))
+        def square(e, s0, s1):
+            sq = keep.tile([P, (s1 - s0) * 512], F32, name="sq_%d%d" % (e, s0), align_bytes=64)
             nc.scalar.activation(
-                planes_by_pairs(sq[:]), woven_by_pairs(made["sig", e, s]), SQUARE, bias=one_half[:], scale=-1.0
+                sq[:], made["sig", e, s0, s1][:].rearrange("p j t -> p (j t)"), SQUARE, bias=one_half[:], scale=-1.0
             )
-            made["sq", e, s] = sq[:]
+            for s in range(s0, s1):
+                step = sq[:, 512 * (s - s0) : 512 * (s - s0 + 1)]
+                made["sq", e, s] = step.rearrange("p (j t) -> p j t", t=4)
+                made["da", e, s] = step.bitcast(BF16).rearrange("p (a j t) -> p a j t", a=2, t=4)
 
         def product_da3(e, s):
-            da = ring.tile([P, 2, C, 4], BF16, name="da", bufs=4, align_bytes=64)
-            made["da", e, s] = da
             nc.vector.scalar_tensor_tensor(
-                da[:, 0, :, :],
-                made["minus_dh", e, s][:].rearrange("p t j -> p j t"),
-                -1.0,
-                made["sig", e, s],
-                MULT,
-                MULT,
-            )
-
-        def da1_factor(e, s):
-            nq = keep.tile([P, 4, C], F32, name="nq_%d%d" % (e, s))
-            nc.vector.scalar_tensor_tensor(nq[:], made["sq", e, s], 0.25, saved_slice("a3", e, s), SUBTRACT, MULT)
-            made["nq", e, s] = nq
-
-        def product_da1(e, s):
-            nc.vector.tensor_tensor(
-                woven_by_pairs(made["da", e, s][:, 1, :, :]),
-                planes_by_pairs(made["minus_dh", e, s][:]),
-                planes_by_pairs(made["nq", e, s][:]),
-                MULT,
+                made["da", e, s][:, 0, :, :], made["dh", e, s], -1.0, made["sig", e, s], MULT, MULT
             )
 
         def slope_times_dh(e, s):
-            y = ring.tile([P, C, 4], F32, name="y", bufs=4)
-            nc.vector.scalar_tensor_tensor(
-                y[:], made["sq", e, s], 0.25, made["minus_dh", e, s][:].rearrange("p t j -> p j t"), SUBTRACT, MULT
-            )
+            y = keep.tile([P, C, 4], F32, name="y_%d%d" % (e, s))
+            nc.vector.scalar_tensor_tensor(y[:], made["sq", e, s], 0.25, made["dh", e, s], SUBTRACT, MULT)
             made["y", e, s] = y
 
-        def times_a3(e, s):
-            nc.vector.tensor_tensor(
+        def times_a3(e, s, engine=nc.vector):
+            engine.tensor_tensor(
                 woven_by_pairs(made["da", e, s][:, 1, :, :]),
                 woven_by_pairs(made["y", e, s][:]),
-                planes_by_pairs(saved_slice("a3", e, s)),
+                planes_by_pairs(saved["a3", e, s]),
                 MULT,
             )
 
-        def quantize_da(e, s, a0=0, a1=2):
-            if a0 == 0:
-                codes = keep.tile([P, 2 * C], U32, name="da_codes_%d%d" % (e, s), align_bytes=64)
-                scales = keep.tile([P, 2 * C], U8, name="da_scales_%d%d" % (e, s), align_bytes=64)
-                made["da_mx", e, s] = (codes, scales)
-            codes, scales = made["da_mx", e, s]
+        def quantize_da(e, s):
+            codes = keep.tile([P, 2 * C], U32, name="da_codes_%d%d" % (e, s), align_bytes=64)
+            scales = keep.tile([P, 2 * C], U8, name="da_scales_%d%d" % (e, s), align_bytes=64)
+            made["da_mx", e, s] = (codes, scales)
             nc.vector.quantize_mx(
-                out=codes[:, C * a0 : C * a1].bitcast(FP8X4),
-                scales=scales[:, C * a0 : C * a1],
-                in_=made["da", e, s][:, a0:a1].rearrange("p a j t -> p (a j t)"),
+                out=codes[:].bitcast(FP8X4),
+                scales=scales[:],
+                in_=made["da", e, s].rearrange("p a j t -> p (a j t)"),
             )
 
-        def second_passes(dx, e, kt, s, a, start, stop):
+        def second_pass(dx, e, kt, s, a):
             codes, scales = made["da_mx", e, s]
             cols = slice(C * a, C * (a + 1))
-            row = 2 * (e - W13_FIRST[e]) + s
             nc.tensor.matmul_mx(
                 out=dx,
-                lhsT=w13[a, W13_FIRST[e]][:, row, 256 * kt : 256 * (kt + 1)].bitcast(FP4X4),
-                lhsT_scale=w13_scale_rows[:, a, 2 * e + s, P * kt : P * (kt + 1)],
+                lhsT=w13[a, e][:, s, 256 * kt : 256 * (kt + 1)].bitcast(FP4X4),
+                lhsT_scale=w13_scale_rows[a][:, 2 * e + s, P * kt : P * (kt + 1)],
                 rhs=codes[:, cols].bitcast(FP8X4),
                 rhs_scale=scales[:, cols],
-                start=start,
-                stop=stop,
+                start=s == 0 and a == 0,
+                stop=s == 1 and a == 1,
             )
 
-        def second_product(e):
-            banks = [psum.tile([P, C], F32, name="dx_%d%d" % (e, kt), tag="dx") for kt in range(2)]
-            for a in range(2):
-                for kt in range(2):
-                    for s in range(2):
-                        second_passes(banks[kt][:], e, kt, s, a, s == 0 and a == 0, s == 1 and a == 1)
-            return banks
+        def scatter_on_scalar(e, kt):
+            nc.scalar.activation(windows[kt][:].indirect(offsets[:, 8 * e : 8 * (e + 1)]), dx_sb[:, e, kt, :], COPY)
 
-        def scatter_on_vector(e, kt, values):
-            nc.vector.tensor_copy(windows[kt][:].indirect(offsets[:, 8 * e : 8 * (e + 1)]), values)
+        def finish(e):
+            dx = psum.tile([P, 2, C], F32, name="dx", bufs=2)
+            for kt in range(2):
+                for s in range(2):
+                    for a in range(2):
+                        second_pass(dx[:, kt, :], e, kt, s, a)
+            nc.scalar.activation(dx_sb[:, e, :, :], dx[:], COPY, scale=-1.0)
+            for kt in range(2):
+                scatter_on_scalar(e, kt)
 
-        def scatter_on_scalar(e0, e1, kt):
-            nc.scalar.activation(
-                windows[kt][:].indirect(offsets[:, 8 * e0 : 8 * e1]), dx_sb[:, kt, C * e0 : C * e1], COPY
-            )
+        def finish_last(e):
+            banks = [psum.tile([P, C], F32, name="dx_last", bufs=2) for kt in range(2)]
+            for s in range(2):
+                for a in range(2):
+                    for kt in range(2):
+                        second_pass(banks[kt][:], e, kt, s, a)
+            nc.vector.tensor_scalar(dx_sb[:, e, 0, :], banks[0][:], -1.0, None, MULT)
+            nc.scalar.activation(dx_sb[:, e, 1, :], banks[1][:], COPY, scale=-1.0)
+            nc.vector.tensor_copy(windows[0][:].indirect(offsets[:, 8 * e : 8 * (e + 1)]), dx_sb[:, e, 0, :])
+            scatter_on_scalar(e, 1)
+
+        def products(e):
+            slope_times_dh(e, 0)
+            times_a3(e, 0, nc.gpsimd)
+            if e == 0:
+                product_da3(e, 0)
+                slope_times_dh(e, 1)
+            else:
+                slope_times_dh(e, 1)
+                product_da3(e, 0)
+            product_da3(e, 1)
+            if e == 1:
+                sort_w2(3)
+            times_a3(e, 1)
+            for s in range(2):
+                quantize_da(e, s)
 
         for t in range(3):
             gather_times_gate(t, 0, 2)
             gather_plain(t)
         gather_times_gate(3, 0, 1)
-        interleave(0)
+        weave(0)
+        sort_w2(0)
         quantize_g(0, 1)
         gather_times_gate(3, 1, 2)
-        interleave(1)
-        quantize_g(1, 2)
         gather_plain(3)
-        g_bf[1] = keep.tile([P, 2 * C, 4], BF16, name="g_bf1", tag="g4_0", align_bytes=64)
-
-        def in_turn(kinds, piece):
-            for kind in kinds:
-                for step in piece:
-                    kind(*step)
-
-        def finish(e):
-            banks = second_product(e)
-            for kt in range(2):
-                nc.scalar.copy(out=dx_sb[:, kt, C * e : C * (e + 1)], in_=banks[kt][:])
-            if e == 0:
-                scatter_on_scalar(e, e + 1, 0)
-            scatter_on_scalar(e, e + 1, 1)
-
-        sigmoid(0, 0)
-        square_as_planes(0, 0)
         first_product(0, 0)
-        first_product(1, 0)
-        sigmoid(1, 0)
-        square(1, 0)
-        da1_factor(0, 0)
-        in_turn((first_product, sigmoid, square), PIECES[1])
-        product_da3(0, 0)
-        product_da1(0, 0)
-        product_da3(1, 0)
-        quantize_da(0, 0)
-        slope_times_dh(1, 0)
-        interleave_times_gate(2)
-        times_a3(1, 0)
-        interleave_times_gate(3)
-        quantize_da(1, 0)
+        sigmoid(0, 0, 1)
+        square(0, 0, 1)
+        weave(1)
+        quantize_g(1, 2)
+        first_product(0, 1)
+        sigmoid(0, 1, 2)
+        square(0, 1, 2)
+        weave_times_gate(2)
+        weave_times_gate(3)
         quantize_g(2, 4)
-        in_turn((first_product, sigmoid, square), PIECES[2])
-        in_turn((product_da3, slope_times_dh, times_a3, quantize_da), PIECES[1])
-        in_turn((first_product, sigmoid, square), PIECES[3])
-        in_turn((product_da3, slope_times_dh), PIECES[2])
-        in_turn((product_da3, slope_times_dh), PIECES[3])
-        finish(0)
-        finish(1)
-        for step in A3_PIECES[3]:
-            quantize_da(*step, 0, 1)
-        in_turn((times_a3,), A3_PIECES[3])
-        for step in A3_PIECES[3]:
-            quantize_da(*step, 1, 2)
-        banks_2 = [psum.tile([P, C], F32, name="dx2_%d" % kt, tag="minus_dh", bufs=4) for kt in range(2)]
-        for kt in range(2):
-            for a in range(2):
-                for s in range(2):
-                    second_passes(banks_2[kt][:], 2, kt, s, a, s == 0 and a == 0, s == 1 and a == 1)
-        scatter_on_vector(1, 0, dx_sb[:, 0, C : 2 * C])
-        for kt in (1, 0):
-            nc.scalar.copy(out=dx_sb[:, kt, 2 * C : 3 * C], in_=banks_2[kt][:])
-        scatter_on_scalar(2, 3, 1)
 
-        for step in A3_PIECES[4]:
-            quantize_da(*step, 0, 1)
-        in_turn((times_a3,), A3_PIECES[4])
-        for step in A3_PIECES[4]:
-            quantize_da(*step, 1, 2)
-        banks = [psum.tile([P, C], F32, name="dx3_%d" % kt, tag="dhT") for kt in range(2)]
-        for a in range(2):
-            for s in range(2):
-                for kt in range(2):
-                    second_passes(banks[kt][:], 3, kt, s, a, s == 0 and a == 0, s == 1 and a == 1)
-        cols = slice(3 * C, 4 * C)
-        scatter_on_vector(2, 0, dx_sb[:, 0, 2 * C : 3 * C])
-        nc.vector.tensor_copy(out=dx_sb[:, 0, cols], in_=banks[0][:])
-        nc.scalar.copy(out=dx_sb[:, 1, cols], in_=banks[1][:])
-        scatter_on_vector(3, 0, dx_sb[:, 0, cols])
-        scatter_on_scalar(3, 4, 1)
+        for e in range(E):
+            products(e)
+            if e + 1 < E:
+                if e + 1 in SORTED_ON_SCALAR:
+                    sort_w2(e + 1)
+                for s in range(2):
+                    first_product(e + 1, s)
+                sigmoid(e + 1, 0, 2)
+                square(e + 1, 0, 2)
+            if e >= 1:
+                finish(e - 1)
+        finish_last(E - 1)
         nc.sync.dma_start(out=out[0:P, :], in_=windows[0][:])
         nc.scalar.dma_start(out=out[P : 2 * P, :], in_=windows[1][:])

@@ -5,7 +5,7 @@ import concourse.mybir as mybir
 N, T, E, C, H, K = 512, 768, 4, 128, 1024, 256
 SLOTS = E * C
 P = 128
-SORTED_ON_SCALAR = (1, 2)
+SORTED_ON_SCALAR = (1, 2, 3)
 
 FLOPS = 2 * SLOTS * H * (N + 2 * K)
 BYTES = 4 * (N * T + 2 * H * SLOTS + P * SLOTS + K * T) + 2 * P * SLOTS // 16 + E * (N * H + 2 * H * K) * 17 // 32
@@ -54,9 +54,8 @@ def tile_moe_bdx_glu_sigmoid_kernel(
         g_scales = keep.tile([P, SLOTS], U8, name="g_scales", align_bytes=64)
         w2_raw = {}
         w2 = [keep.tile([P, 2 * H], U8, name="w2_%d" % e, align_bytes=64) for e in range(E)]
-        staged = keep.tile([P, 512], U8, name="staged")
-        staged_sorted = keep.tile([P, 512], U8, name="staged_sorted")
-        w2_scale_rows = keep.tile([P, 2 * E, 512], U8, name="w2_scale_rows", align_bytes=64)
+        w2_scale_raw = [keep.tile([P, 2, H], U8, name="w2_scale_raw%d" % half) for half in range(2)]
+        w2_scale_rows = [keep.tile([P, H], U8, name="w2_scale_rows%d" % e, align_bytes=64) for e in range(E)]
         w13 = {
             (a, e): keep.tile([P, 2, 2 * K], U8, name="w13_%d%d" % (a, e), align_bytes=64)
             for a in range(2)
@@ -109,38 +108,39 @@ def tile_moe_bdx_glu_sigmoid_kernel(
         def load_gate(half):
             nc.sync.dma_start(out=gates[half][:], in_=gate[0:P, 2 * C * half : 2 * C * (half + 1)])
 
-        staged_src = w2_scales.bitcast(I32).rearrange("e o f (s i) -> s f (e o) i", s=2)
-        for s in range(2):
-            nc.sync.dma_start(out=staged[:].bitcast(I32)[s:P:2, :], in_=staged_src[s])
+        def load_w2_scales(half):
+            scale_src = w2_scales.bitcast(I32).rearrange("e s f i -> f (e s) i")
+            for r in range(4):
+                nc.sync.dma_start(
+                    out=as_words(w2_scale_raw[half])[r:P:32, :, :],
+                    in_=scale_src[r:16:4, 2 * half : 2 * half + 2, :],
+                )
+
+        for half in range(2):
+            nc.gpsimd.memset(w2_scale_raw[half][:].rearrange("p e i -> p (e i)").bitcast(I32), 0)
         load_dy(0)
+        load_w2_scales(0)
         nc.sync.dma_start(offsets[:], offs)
         load_gate(0)
         nc.vector.memset(zero[:], 0.0)
         nc.scalar.activation(one_half[:], zero[:], SIGMOID)
         for kt in range(2):
             nc.gpsimd.memset(windows[kt][:], 0.0)
-        nc.vector.tensor_copy(
-            out=staged_sorted[:].rearrange("p (t m) -> p t m", t=4), in_=staged[:].rearrange("p (m t) -> p t m", t=4)
-        )
         load_dy(1)
         load_dy(2)
         load_dy(3)
         load_w2(0, 1)
-        for quadrant in (0, 2, 1, 3):
-            p0 = 32 * quadrant
-            nc.sync.dma_start(
-                out=as_words(w2_scale_rows)[p0 : p0 + 4, :, :], in_=staged_sorted[p0 : p0 + 32, :].bitcast(I32)
-            )
         load_saved("a1", 0, 0, 1)
         load_gate(1)
         load_saved("a1", 0, 1, 2)
         load_saved("a3", 0)
         load_w2(1, 2)
         load_saved("a1", 1)
-        load_w13_scales(0, 0)
+        load_w2_scales(1)
         load_saved("a3", 1)
         load_w2(2, 4)
         load_saved("a1", 2)
+        load_w13_scales(0, 0)
         load_w13_scales(0, 2)
         load_saved("a1", 3)
         load_w13_scales(1, 0)
@@ -188,8 +188,14 @@ def tile_moe_bdx_glu_sigmoid_kernel(
         def sort_w2(e):
             move = nc.scalar.copy if e in SORTED_ON_SCALAR else nc.vector.tensor_copy
             move(
-                out=w2[e][:].bitcast(U16).rearrange("p (s t m) -> p s t m", s=2, t=4),
-                in_=w2_raw[e].bitcast(U16).rearrange("p (s m t) -> p s t m", s=2, t=4),
+                out=w2[e][:].bitcast(U16).rearrange("p (s t c i) -> p s c t i", s=2, t=4, i=8),
+                in_=w2_raw[e].bitcast(U16).rearrange("p (s c i t) -> p s c t i", s=2, t=4, i=8),
+            )
+
+        def sort_w2_scales(e):
+            nc.vector.tensor_copy(
+                out=w2_scale_rows[e][:].rearrange("p (s t c i) -> p s c t i", s=2, t=4, i=16),
+                in_=w2_scale_raw[e // 2][:, e % 2, :].rearrange("p (s c i t) -> p s c t i", s=2, t=4, i=16),
             )
 
         made = {}
@@ -200,7 +206,7 @@ def tile_moe_bdx_glu_sigmoid_kernel(
                 nc.tensor.matmul_mx(
                     out=dh[:, t, :],
                     lhsT=w2[e][:, H * s + 256 * t : H * s + 256 * (t + 1)].bitcast(FP4X4),
-                    lhsT_scale=w2_scale_rows[:, 2 * e + s, P * t : P * (t + 1)],
+                    lhsT_scale=w2_scale_rows[e][:, 512 * s + P * t : 512 * s + P * (t + 1)],
                     rhs=g_codes[:, C * e : C * (e + 1)].bitcast(FP8X4),
                     rhs_scale=g_scales[:, C * e : C * (e + 1)],
                     start=True,
@@ -300,8 +306,8 @@ def tile_moe_bdx_glu_sigmoid_kernel(
                 slope_times_dh(e, 1)
                 product_da3(e, 0)
             product_da3(e, 1)
-            if e == 1:
-                sort_w2(3)
+            if e < 2:
+                sort_w2_scales(e + 2)
             times_a3(e, 1)
             for s in range(2):
                 quantize_da(e, s)
@@ -309,6 +315,8 @@ def tile_moe_bdx_glu_sigmoid_kernel(
         for t in range(3):
             gather_times_gate(t, 0, 2)
             gather_plain(t)
+            if t < 2:
+                sort_w2_scales(t)
         gather_times_gate(3, 0, 1)
         weave(0)
         sort_w2(0)

@@ -275,6 +275,9 @@ def tile_moe_bdx_glu_sigmoid_kernel(
         def scatter_on_scalar(e, kt):
             nc.scalar.activation(windows[kt][:].indirect(offsets[:, 8 * e : 8 * (e + 1)]), dx_sb[:, e, kt, :], COPY)
 
+        def scatter_on_vector(e):
+            nc.vector.tensor_copy(windows[0][:].indirect(offsets[:, 8 * e : 8 * (e + 1)]), dx_sb[:, e, 0, :])
+
         def finish(e):
             dx = psum.tile([P, 2, C], F32, name="dx", bufs=2)
             for kt in range(2):
@@ -282,7 +285,7 @@ def tile_moe_bdx_glu_sigmoid_kernel(
                     for a in range(2):
                         second_pass(dx[:, kt, :], e, kt, s, a)
             nc.scalar.activation(dx_sb[:, e, :, :], dx[:], COPY, scale=-1.0)
-            for kt in range(2):
+            for kt in range(1 if e == 2 else 0, 2):
                 scatter_on_scalar(e, kt)
 
         def finish_last(e):
@@ -291,9 +294,10 @@ def tile_moe_bdx_glu_sigmoid_kernel(
                 for a in range(2):
                     for kt in range(2):
                         second_pass(banks[kt][:], e, kt, s, a)
+            scatter_on_vector(e - 1)
             nc.vector.tensor_scalar(dx_sb[:, e, 0, :], banks[0][:], -1.0, None, MULT)
             nc.scalar.activation(dx_sb[:, e, 1, :], banks[1][:], COPY, scale=-1.0)
-            nc.vector.tensor_copy(windows[0][:].indirect(offsets[:, 8 * e : 8 * (e + 1)]), dx_sb[:, e, 0, :])
+            scatter_on_vector(e)
             scatter_on_scalar(e, 1)
 
         def products(e):

@@ -96,9 +96,9 @@ def tile_moe_bdx_glu_sigmoid_kernel(
             for e in range(e0, e1):
                 w2_raw[e] = raw[:, 2 * H * (e - e0) : 2 * H * (e - e0 + 1)]
 
-        def load_w13_scales(a, r0):
+        def load_w13_scales(a):
             scale_src = (w3_scales, w1_scales)[a].bitcast(I32).rearrange("e s f k -> f (e s) k")
-            for r in (r0, r0 + 1):
+            for r in range(4):
                 nc.sync.dma_start(out=as_words(w13_scale_rows[a])[r:P:32, :, :], in_=scale_src[r:16:4, :, :])
 
         def load_w13(e):
@@ -138,14 +138,13 @@ def tile_moe_bdx_glu_sigmoid_kernel(
         load_saved("a1", 1)
         load_w2_scales(1)
         load_saved("a3", 1)
-        load_w2(2, 4)
+        load_w2(2, 3)
         load_saved("a1", 2)
-        load_w13_scales(0, 0)
-        load_w13_scales(0, 2)
-        load_saved("a1", 3)
-        load_w13_scales(1, 0)
         load_saved("a3", 2)
-        load_w13_scales(1, 2)
+        load_w2(3, 4)
+        load_w13_scales(0)
+        load_saved("a1", 3)
+        load_w13_scales(1)
         load_w13(0)
         load_w13(1)
         load_saved("a3", 3)
@@ -284,8 +283,10 @@ def tile_moe_bdx_glu_sigmoid_kernel(
                 for s in range(2):
                     for a in range(2):
                         second_pass(dx[:, kt, :], e, kt, s, a)
-            nc.scalar.activation(dx_sb[:, e, :, :], dx[:], COPY, scale=-1.0)
-            for kt in range(1 if e == 2 else 0, 2):
+            made["dx", e] = dx
+            first = 1 if e == 1 else 0
+            nc.scalar.activation(dx_sb[:, e, first:, :], dx[:, first:, :], COPY, scale=-1.0)
+            for kt in range(0 if e == 0 else 1, 2):
                 scatter_on_scalar(e, kt)
 
         def finish_last(e):
@@ -294,6 +295,9 @@ def tile_moe_bdx_glu_sigmoid_kernel(
                 for a in range(2):
                     for kt in range(2):
                         second_pass(banks[kt][:], e, kt, s, a)
+            dx_1 = made["da", e, 1].rearrange("p a j t -> p (a j t)")[:, 0 : 2 * C].bitcast(F32)
+            nc.vector.tensor_scalar(dx_1, made["dx", 1][:, 0, :], -1.0, None, MULT)
+            nc.vector.tensor_copy(windows[0][:].indirect(offsets[:, 8:16]), dx_1)
             scatter_on_vector(e - 1)
             nc.vector.tensor_scalar(dx_sb[:, e, 0, :], banks[0][:], -1.0, None, MULT)
             nc.scalar.activation(dx_sb[:, e, 1, :], banks[1][:], COPY, scale=-1.0)

@@ -5,7 +5,6 @@ import concourse.mybir as mybir
 N, T, E, C, H, K = 512, 768, 4, 128, 1024, 256
 SLOTS = E * C
 P = 128
-SORTED_ON_SCALAR = (1, 2, 3)
 
 FLOPS = 2 * SLOTS * H * (N + 2 * K)
 BYTES = 4 * (N * T + 2 * H * SLOTS + P * SLOTS + K * T) + 2 * P * SLOTS // 16 + E * (N * H + 2 * H * K) * 17 // 32
@@ -142,12 +141,12 @@ def tile_moe_bdx_glu_sigmoid_kernel(
         load_saved("a1", 2)
         load_saved("a3", 2)
         load_w2(3, 4)
-        load_w13_scales(0)
         load_saved("a1", 3)
+        load_w13_scales(0)
         load_w13_scales(1)
         load_w13(0)
-        load_w13(1)
         load_saved("a3", 3)
+        load_w13(1)
         load_w13(2)
         load_w13(3)
 
@@ -184,11 +183,12 @@ def tile_moe_bdx_glu_sigmoid_kernel(
                 in_=g_bf[e0 // 2][:, C * (e0 % 2) : C * (e1 - e0 + e0 % 2), :].rearrange("p j t -> p (j t)"),
             )
 
-        def sort_w2(e):
-            move = nc.scalar.copy if e in SORTED_ON_SCALAR else nc.vector.tensor_copy
-            move(
-                out=w2[e][:].bitcast(U16).rearrange("p (s t c i) -> p s c t i", s=2, t=4, i=8),
-                in_=w2_raw[e].bitcast(U16).rearrange("p (s c i t) -> p s c t i", s=2, t=4, i=8),
+        def sort_w2(e, s0=0, s1=2):
+            nc.scalar.copy(
+                out=w2[e][:, H * s0 : H * s1].bitcast(U16).rearrange("p (s t c i) -> p s c t i", s=s1 - s0, t=4, i=8),
+                in_=w2_raw[e][:, H * s0 : H * s1]
+                .bitcast(U16)
+                .rearrange("p (s c i t) -> p s c t i", s=s1 - s0, t=4, i=8),
             )
 
         def sort_w2_scales(e):
@@ -216,19 +216,16 @@ def tile_moe_bdx_glu_sigmoid_kernel(
         def sigmoid(e, s0, s1):
             sig = keep.tile([P, (s1 - s0) * C, 4], F32, name="sig_%d%d" % (e, s0))
             nc.scalar.activation(woven_by_pairs(sig[:]), planes_by_pairs(saved["a1", e, s0, s1]), SIGMOID)
-            made["sig", e, s0, s1] = sig
             for s in range(s0, s1):
                 made["sig", e, s] = sig[:, C * (s - s0) : C * (s - s0 + 1), :]
 
-        def square(e, s0, s1):
-            sq = keep.tile([P, (s1 - s0) * 512], F32, name="sq_%d%d" % (e, s0), align_bytes=64)
+        def square(e, s):
+            sq = keep.tile([P, 512], F32, name="sq_%d%d" % (e, s), align_bytes=64)
             nc.scalar.activation(
-                sq[:], made["sig", e, s0, s1][:].rearrange("p j t -> p (j t)"), SQUARE, bias=one_half[:], scale=-1.0
+                sq[:], made["sig", e, s].rearrange("p j t -> p (j t)"), SQUARE, bias=one_half[:], scale=-1.0
             )
-            for s in range(s0, s1):
-                step = sq[:, 512 * (s - s0) : 512 * (s - s0 + 1)]
-                made["sq", e, s] = step.rearrange("p (j t) -> p j t", t=4)
-                made["da", e, s] = step.bitcast(BF16).rearrange("p (a j t) -> p a j t", a=2, t=4)
+            made["sq", e, s] = sq[:].rearrange("p (j t) -> p j t", t=4)
+            made["da", e, s] = sq[:].bitcast(BF16).rearrange("p (a j t) -> p a j t", a=2, t=4)
 
         def product_da3(e, s):
             nc.vector.scalar_tensor_tensor(
@@ -327,18 +324,19 @@ def tile_moe_bdx_glu_sigmoid_kernel(
                 sort_w2_scales(t)
         gather_times_gate(3, 0, 1)
         weave(0)
-        sort_w2(0)
-        quantize_g(0, 1)
         gather_times_gate(3, 1, 2)
+        quantize_g(0, 1)
         gather_plain(3)
+        sort_w2(0, 0, 1)
         first_product(0, 0)
         sigmoid(0, 0, 1)
-        square(0, 0, 1)
+        square(0, 0)
+        sort_w2(0, 1, 2)
         weave(1)
         quantize_g(1, 2)
         first_product(0, 1)
         sigmoid(0, 1, 2)
-        square(0, 1, 2)
+        square(0, 1)
         weave_times_gate(2)
         weave_times_gate(3)
         quantize_g(2, 4)
@@ -346,12 +344,12 @@ def tile_moe_bdx_glu_sigmoid_kernel(
         for e in range(E):
             products(e)
             if e + 1 < E:
-                if e + 1 in SORTED_ON_SCALAR:
-                    sort_w2(e + 1)
+                sort_w2(e + 1)
                 for s in range(2):
                     first_product(e + 1, s)
                 sigmoid(e + 1, 0, 2)
-                square(e + 1, 0, 2)
+                for s in range(2):
+                    square(e + 1, s)
             if e >= 1:
                 finish(e - 1)
         finish_last(E - 1)

@@ -66,7 +66,7 @@ def tile_moe_bdx_glu_sigmoid_kernel(
         windows = [keep.tile([P, T], F32, name="window%d" % kt) for kt in range(2)]
         zero = keep.tile([P, 1], F32, name="zero")
         one_half = keep.tile([P, 1], F32, name="one_half")
-        dx_sb = keep.tile([P, E, 2, C], F32, name="dx_sb")
+        dx_sb = keep.tile([P, 2, SLOTS], F32, name="dx_sb")
         saved = {}
 
         sources = {"a1": a1, "a3": a3}
@@ -269,10 +269,24 @@ def tile_moe_bdx_glu_sigmoid_kernel(
             )
 
         def scatter_on_scalar(e, kt):
-            nc.scalar.activation(windows[kt][:].indirect(offsets[:, 8 * e : 8 * (e + 1)]), dx_sb[:, e, kt, :], COPY)
+            nc.scalar.activation(
+                windows[kt][:].indirect(offsets[:, 8 * e : 8 * (e + 1)]), dx_sb[:, kt, C * e : C * (e + 1)], COPY
+            )
 
-        def scatter_on_vector(e):
-            nc.vector.tensor_copy(windows[0][:].indirect(offsets[:, 8 * e : 8 * (e + 1)]), dx_sb[:, e, 0, :])
+        def scatter_on_vector(e0, e1):
+            nc.vector.tensor_copy(windows[0][:].indirect(offsets[:, 8 * e0 : 8 * e1]), dx_sb[:, 0, C * e0 : C * e1])
+
+        def copy_out(e, kts, bank):
+            nc.scalar.activation(dx_sb[:, kts, C * e : C * (e + 1)], bank, COPY, scale=-1.0)
+
+        def finish_first():
+            for kt in range(2):
+                bank = psum.tile([P, C], F32, name="dx", bufs=2)
+                for s in range(2):
+                    for a in range(2):
+                        second_pass(bank[:], 0, kt, s, a)
+                copy_out(0, kt, bank[:])
+                scatter_on_scalar(0, kt)
 
         def finish(e):
             dx = psum.tile([P, 2, C], F32, name="dx", bufs=2)
@@ -280,26 +294,20 @@ def tile_moe_bdx_glu_sigmoid_kernel(
                 for s in range(2):
                     for a in range(2):
                         second_pass(dx[:, kt, :], e, kt, s, a)
-            made["dx", e] = dx
-            first = 1 if e == 1 else 0
-            nc.scalar.activation(dx_sb[:, e, first:, :], dx[:, first:, :], COPY, scale=-1.0)
-            for kt in range(0 if e == 0 else 1, 2):
-                scatter_on_scalar(e, kt)
+            copy_out(e, slice(0, 2), dx[:])
+            scatter_on_scalar(e, 1)
 
         def finish_last(e):
             banks = [psum.tile([P, C], F32, name="dx_last", bufs=2) for kt in range(2)]
             for s in range(2):
-                for a in range(2):
-                    for kt in range(2):
+                for kt in (1, 0):
+                    for a in range(2):
                         second_pass(banks[kt][:], e, kt, s, a)
-            dx_1 = made["da", e, 1].rearrange("p a j t -> p (a j t)")[:, 0 : 2 * C].bitcast(F32)
-            nc.vector.tensor_scalar(dx_1, made["dx", 1][:, 0, :], -1.0, None, MULT)
-            nc.vector.tensor_copy(windows[0][:].indirect(offsets[:, 8:16]), dx_1)
-            scatter_on_vector(e - 1)
-            nc.vector.tensor_scalar(dx_sb[:, e, 0, :], banks[0][:], -1.0, None, MULT)
-            nc.scalar.activation(dx_sb[:, e, 1, :], banks[1][:], COPY, scale=-1.0)
-            scatter_on_vector(e)
+            scatter_on_vector(1, e)
+            for kt in (1, 0):
+                copy_out(e, kt, banks[kt][:])
             scatter_on_scalar(e, 1)
+            scatter_on_vector(e, e + 1)
 
         def products(e):
             slope_times_dh(e, 0)
@@ -350,7 +358,9 @@ def tile_moe_bdx_glu_sigmoid_kernel(
                 sigmoid(e + 1, 0, 2)
                 for s in range(2):
                     square(e + 1, s)
-            if e >= 1:
+            if e == 1:
+                finish_first()
+            elif e > 1:
                 finish(e - 1)
         finish_last(E - 1)
         nc.sync.dma_start(out=out[0:P, :], in_=windows[0][:])

from contextlib import ExitStack

import concourse.mybir as mybir

N, T, E, C, H, K = 512, 768, 4, 128, 1024, 256
SLOTS = E * C
P = 128

FLOPS = 2 * SLOTS * H * (N + 2 * K)
BYTES = 4 * (N * T + 2 * H * SLOTS + P * SLOTS + K * T) + 2 * P * SLOTS // 16 + E * (N * H + 2 * H * K) * 17 // 32

F32 = mybir.dt.float32
BF16 = mybir.dt.bfloat16
I32 = mybir.dt.int32
U32 = mybir.dt.uint32
U16 = mybir.dt.uint16
U8 = mybir.dt.uint8
FP8X4 = mybir.dt.float8_e4m3fn_x4
FP4X4 = mybir.dt.float4_e2m1fn_x4
MULT = mybir.AluOpType.mult
SUBTRACT = mybir.AluOpType.subtract
SIGMOID = mybir.ActivationFunctionType.Sigmoid
SQUARE = mybir.ActivationFunctionType.Square
COPY = mybir.ActivationFunctionType.Copy


def planes_by_pairs(ap):
    return ap.rearrange("p t (c i) -> p c t i", i=2)


def woven_by_pairs(ap):
    return ap.rearrange("p (c i) t -> p c t i", i=2)


def as_words(tile):
    return tile[:].rearrange("p r b -> p (r b)").bitcast(I32).rearrange("p (r w) -> p r w", r=tile.shape[1])


def tile_moe_bdx_glu_sigmoid_kernel(
    tc, dyT, a1, a3, w2_words, w2_scales, w1_words, w1_scales, w3_words, w3_scales, gate, offs, out
):
    nc = tc.nc
    with ExitStack() as ctx:
        keep = ctx.enter_context(tc.tile_pool(name="keep", bufs=1))
        psum = ctx.enter_context(tc.psum_pool(name="psum", bufs=4))

        offsets = keep.tile([P, SLOTS // 16], U16, name="offsets")
        dy = [keep.tile([P, T], F32, name="dy%d" % t) for t in range(4)]
        gates = [keep.tile([P, 2 * C], F32, name="gates%d" % half) for half in range(2)]
        g4 = [keep.tile([P, 4, 2 * C], F32, name="g4_%d" % half, align_bytes=64) for half in range(2)]
        g_bf = [keep.tile([P, 2 * C, 4], BF16, name="g_bf%d" % half, align_bytes=64) for half in range(2)]
        g_codes = keep.tile([P, SLOTS], U32, name="g_codes", align_bytes=64)
        g_scales = keep.tile([P, SLOTS], U8, name="g_scales", align_bytes=64)
        w2_raw = {}
        w2 = [keep.tile([P, 2 * H], U8, name="w2_%d" % e, align_bytes=64) for e in range(E)]
        w2_scale_raw = [keep.tile([P, 2, H], U8, name="w2_scale_raw%d" % half) for half in range(2)]
        w2_scale_rows = [keep.tile([P, H], U8, name="w2_scale_rows%d" % e, align_bytes=64) for e in range(E)]
        w13 = {
            (a, e): keep.tile([P, 2, 2 * K], U8, name="w13_%d%d" % (a, e), align_bytes=64)
            for a in range(2)
            for e in range(E)
        }
        w13_scale_rows = [
            keep.tile([P, 2 * E, K], U8, name="w13_scale_rows%d" % a, align_bytes=64) for a in range(2)
        ]
        windows = [keep.tile([P, T], F32, name="window%d" % kt) for kt in range(2)]
        zero = keep.tile([P, 1], F32, name="zero")
        one_half = keep.tile([P, 1], F32, name="one_half")
        dx_sb = keep.tile([P, 2, SLOTS], F32, name="dx_sb")
        saved = {}

        sources = {"a1": a1, "a3": a3}
        dy_rows = dyT.rearrange("(p t) j -> p t j", t=4)

        def load_dy(t):
            nc.sync.dma_start(out=dy[t][:], in_=dy_rows[:, t, :])

        def load_saved(name, e, s0=0, s1=2):
            tile = keep.tile([P, 4, (s1 - s0) * C], F32, name="%s_%d%d" % (name, e, s0))
            rows = sources[name][512 * s0 : 512 * s1, C * e : C * (e + 1)]
            nc.sync.dma_start(
                out=tile[:].rearrange("p t (s j) -> p t s j", s=s1 - s0),
                in_=rows.rearrange("(s p t) j -> p t s j", p=P, t=4),
            )
            saved[name, e, s0, s1] = tile[:]
            for s in range(s0, s1):
                saved[name, e, s] = tile[:, :, C * (s - s0) : C * (s - s0 + 1)]

        def load_w2(e0, e1):
            raw = keep.tile([P, (e1 - e0) * 2 * H], U8, name="w2_raw%d" % e0)
            nc.sync.dma_start(
                out=raw[:].bitcast(I32).rearrange("p (e i) -> p e i", e=e1 - e0),
                in_=w2_words.bitcast(I32)[e0:e1].rearrange("e o p i -> p (e o) i"),
            )
            for e in range(e0, e1):
                w2_raw[e] = raw[:, 2 * H * (e - e0) : 2 * H * (e - e0 + 1)]

        def load_w13_scales(a):
            scale_src = (w3_scales, w1_scales)[a].bitcast(I32).rearrange("e s f k -> f (e s) k")
            for r in range(4):
                nc.sync.dma_start(out=as_words(w13_scale_rows[a])[r:P:32, :, :], in_=scale_src[r:16:4, :, :])

        def load_w13(e):
            for a, words in ((0, w3_words), (1, w1_words)):
                nc.sync.dma_start(out=as_words(w13[a, e]), in_=words.bitcast(I32)[e].rearrange("s p k -> p s k"))

        def load_gate(half):
            nc.sync.dma_start(out=gates[half][:], in_=gate[0:P, 2 * C * half : 2 * C * (half + 1)])

        def load_w2_scales(half):
            scale_src = w2_scales.bitcast(I32).rearrange("e s f i -> f (e s) i")
            for r in range(4):
                nc.sync.dma_start(
                    out=as_words(w2_scale_raw[half])[r:P:32, :, :],
                    in_=scale_src[r:16:4, 2 * half : 2 * half + 2, :],
                )

        for half in range(2):
            nc.gpsimd.memset(w2_scale_raw[half][:].rearrange("p e i -> p (e i)").bitcast(I32), 0)
        load_dy(0)
        load_w2_scales(0)
        nc.sync.dma_start(offsets[:], offs)
        load_gate(0)
        nc.vector.memset(zero[:], 0.0)
        nc.scalar.activation(one_half[:], zero[:], SIGMOID)
        for kt in range(2):
            nc.gpsimd.memset(windows[kt][:], 0.0)
        load_dy(1)
        load_dy(2)
        load_dy(3)
        load_w2(0, 1)
        load_saved("a1", 0, 0, 1)
        load_gate(1)
        load_saved("a1", 0, 1, 2)
        load_saved("a3", 0)
        load_w2(1, 2)
        load_saved("a1", 1)
        load_w2_scales(1)
        load_saved("a3", 1)
        load_w2(2, 3)
        load_saved("a1", 2)
        load_saved("a3", 2)
        load_w2(3, 4)
        load_saved("a1", 3)
        load_w13_scales(0)
        load_w13_scales(1)
        load_w13(0)
        load_saved("a3", 3)
        load_w13(1)
        load_w13(2)
        load_w13(3)

        def gather_times_gate(t, e0, e1):
            j0, j1 = C * e0, C * e1
            nc.vector.tensor_tensor(
                g4[0][:, t, j0:j1], dy[t][:].indirect(offsets[:, j0 // 16 : j1 // 16]), gates[0][:, j0:j1], MULT
            )

        def gather_plain(t):
            nc.scalar.activation(g4[1][:, t, :], dy[t][:].indirect(offsets[:, 16:32]), COPY)

        def weave(e):
            nc.vector.tensor_copy(
                out=woven_by_pairs(g_bf[0][:, C * e : C * (e + 1), :]),
                in_=planes_by_pairs(g4[0][:, :, C * e : C * (e + 1)]),
            )

        def weave_times_gate(e):
            cols = slice(C * (e - 2), C * (e - 1))
            gate_by_pairs = gates[1][:, cols].rearrange("p (c i) -> p c i", i=2).unsqueeze(2)
            nc.vector.tensor_tensor(
                woven_by_pairs(g_bf[1][:, cols, :]),
                planes_by_pairs(g4[1][:, :, cols]),
                gate_by_pairs.to_broadcast([P, C // 2, 4, 2]),
                MULT,
            )

        def quantize_g(e0, e1):
            cols = slice(C * e0, C * e1)
            nc.vector.quantize_mx(
                out=g_codes[:, cols].bitcast(FP8X4),
                scales=g_scales[:, cols],
                in_=g_bf[e0 // 2][:, C * (e0 % 2) : C * (e1 - e0 + e0 % 2), :].rearrange("p j t -> p (j t)"),
            )

        def sort_w2(e, s0=0, s1=2):
            nc.scalar.copy(
                out=w2[e][:, H * s0 : H * s1].bitcast(U16).rearrange("p (s t c i) -> p s c t i", s=s1 - s0, t=4, i=8),
                in_=w2_raw[e][:, H * s0 : H * s1]
                .bitcast(U16)
                .rearrange("p (s c i t) -> p s c t i", s=s1 - s0, t=4, i=8),
            )

        def sort_w2_scales(e):
            nc.vector.tensor_copy(
                out=w2_scale_rows[e][:].rearrange("p (s t c i) -> p s c t i", s=2, t=4, i=16),
                in_=w2_scale_raw[e // 2][:, e % 2, :].rearrange("p (s c i t) -> p s c t i", s=2, t=4, i=16),
            )

        made = {}

        def first_product(e, s):
            dh = psum.tile([P, 4, C], F32, name="dh")
            for t in range(4):
                nc.tensor.matmul_mx(
                    out=dh[:, t, :],
                    lhsT=w2[e][:, H * s + 256 * t : H * s + 256 * (t + 1)].bitcast(FP4X4),
                    lhsT_scale=w2_scale_rows[e][:, 512 * s + P * t : 512 * s + P * (t + 1)],
                    rhs=g_codes[:, C * e : C * (e + 1)].bitcast(FP8X4),
                    rhs_scale=g_scales[:, C * e : C * (e + 1)],
                    start=True,
                    stop=True,
                )
            made["dh", e, s] = dh[:].rearrange("p t j -> p j t")

        def sigmoid(e, s0, s1):
            sig = keep.tile([P, (s1 - s0) * C, 4], F32, name="sig_%d%d" % (e, s0))
            nc.scalar.activation(woven_by_pairs(sig[:]), planes_by_pairs(saved["a1", e, s0, s1]), SIGMOID)
            for s in range(s0, s1):
                made["sig", e, s] = sig[:, C * (s - s0) : C * (s - s0 + 1), :]

        def square(e, s):
            sq = keep.tile([P, 512], F32, name="sq_%d%d" % (e, s), align_bytes=64)
            nc.scalar.activation(
                sq[:], made["sig", e, s].rearrange("p j t -> p (j t)"), SQUARE, bias=one_half[:], scale=-1.0
            )
            made["sq", e, s] = sq[:].rearrange("p (j t) -> p j t", t=4)
            made["da", e, s] = sq[:].bitcast(BF16).rearrange("p (a j t) -> p a j t", a=2, t=4)

        def product_da3(e, s):
            nc.vector.scalar_tensor_tensor(
                made["da", e, s][:, 0, :, :], made["dh", e, s], -1.0, made["sig", e, s], MULT, MULT
            )

        def slope_times_dh(e, s):
            y = keep.tile([P, C, 4], F32, name="y_%d%d" % (e, s))
            nc.vector.scalar_tensor_tensor(y[:], made["sq", e, s], 0.25, made["dh", e, s], SUBTRACT, MULT)
            made["y", e, s] = y

        def times_a3(e, s, engine=nc.vector):
            engine.tensor_tensor(
                woven_by_pairs(made["da", e, s][:, 1, :, :]),
                woven_by_pairs(made["y", e, s][:]),
                planes_by_pairs(saved["a3", e, s]),
                MULT,
            )

        def quantize_da(e, s):
            codes = keep.tile([P, 2 * C], U32, name="da_codes_%d%d" % (e, s), align_bytes=64)
            scales = keep.tile([P, 2 * C], U8, name="da_scales_%d%d" % (e, s), align_bytes=64)
            made["da_mx", e, s] = (codes, scales)
            nc.vector.quantize_mx(
                out=codes[:].bitcast(FP8X4),
                scales=scales[:],
                in_=made["da", e, s].rearrange("p a j t -> p (a j t)"),
            )

        def second_pass(dx, e, kt, s, a):
            codes, scales = made["da_mx", e, s]
            cols = slice(C * a, C * (a + 1))
            nc.tensor.matmul_mx(
                out=dx,
                lhsT=w13[a, e][:, s, 256 * kt : 256 * (kt + 1)].bitcast(FP4X4),
                lhsT_scale=w13_scale_rows[a][:, 2 * e + s, P * kt : P * (kt + 1)],
                rhs=codes[:, cols].bitcast(FP8X4),
                rhs_scale=scales[:, cols],
                start=s == 0 and a == 0,
                stop=s == 1 and a == 1,
            )

        def scatter_on_scalar(e, kt):
            nc.scalar.activation(
                windows[kt][:].indirect(offsets[:, 8 * e : 8 * (e + 1)]), dx_sb[:, kt, C * e : C * (e + 1)], COPY
            )

        def scatter_on_vector(e0, e1):
            nc.vector.tensor_copy(windows[0][:].indirect(offsets[:, 8 * e0 : 8 * e1]), dx_sb[:, 0, C * e0 : C * e1])

        def copy_out(e, kts, bank):
            nc.scalar.activation(dx_sb[:, kts, C * e : C * (e + 1)], bank, COPY, scale=-1.0)

        def finish_first():
            for kt in range(2):
                bank = psum.tile([P, C], F32, name="dx", bufs=2)
                for s in range(2):
                    for a in range(2):
                        second_pass(bank[:], 0, kt, s, a)
                copy_out(0, kt, bank[:])
                scatter_on_scalar(0, kt)

        def finish(e):
            dx = psum.tile([P, 2, C], F32, name="dx", bufs=2)
            for kt in range(2):
                for s in range(2):
                    for a in range(2):
                        second_pass(dx[:, kt, :], e, kt, s, a)
            copy_out(e, slice(0, 2), dx[:])
            scatter_on_scalar(e, 1)

        def finish_last(e):
            banks = [psum.tile([P, C], F32, name="dx_last", bufs=2) for kt in range(2)]
            for s in range(2):
                for kt in (1, 0):
                    for a in range(2):
                        second_pass(banks[kt][:], e, kt, s, a)
            scatter_on_vector(1, e)
            for kt in (1, 0):
                copy_out(e, kt, banks[kt][:])
            scatter_on_scalar(e, 1)
            scatter_on_vector(e, e + 1)

        def products(e):
            slope_times_dh(e, 0)
            times_a3(e, 0, nc.gpsimd)
            if e == 0:
                product_da3(e, 0)
                slope_times_dh(e, 1)
            else:
                slope_times_dh(e, 1)
                product_da3(e, 0)
            product_da3(e, 1)
            if e < 2:
                sort_w2_scales(e + 2)
            times_a3(e, 1)
            for s in range(2):
                quantize_da(e, s)

        for t in range(3):
            gather_times_gate(t, 0, 2)
            gather_plain(t)
            if t < 2:
                sort_w2_scales(t)
        gather_times_gate(3, 0, 1)
        weave(0)
        gather_times_gate(3, 1, 2)
        quantize_g(0, 1)
        gather_plain(3)
        sort_w2(0, 0, 1)
        first_product(0, 0)
        sigmoid(0, 0, 1)
        square(0, 0)
        sort_w2(0, 1, 2)
        weave(1)
        quantize_g(1, 2)
        first_product(0, 1)
        sigmoid(0, 1, 2)
        square(0, 1)
        weave_times_gate(2)
        weave_times_gate(3)
        quantize_g(2, 4)

        for e in range(E):
            products(e)
            if e + 1 < E:
                sort_w2(e + 1)
                for s in range(2):
                    first_product(e + 1, s)
                sigmoid(e + 1, 0, 2)
                for s in range(2):
                    square(e + 1, s)
            if e == 1:
                finish_first()
            elif e > 1:
                finish(e - 1)
        finish_last(E - 1)
        nc.sync.dma_start(out=out[0:P, :], in_=windows[0][:])
        nc.scalar.dma_start(out=out[P : 2 * P, :], in_=windows[1][:])
